import numpy as np, ml_dtypes
CORES = [8,136,40,168]
N = 4
import mx_ref
BF = ml_dtypes.bfloat16
def cols(t, e):
    v = np.concatenate([t.reshape(128, -1, 4), np.zeros((128, 1, 4), BF)], axis=1)
    return np.ascontiguousarray(v[:, e]).reshape(128, -1)
def f(rng, *shape):
    return mx_ref.flush((rng.standard_normal(shape, dtype=np.float32) * np.exp2(rng.integers(-2, 3, shape[:-1] + (1,)))).astype(BF))
def wide(rng, *shape, cols=0):
    v = rng.standard_normal(shape, dtype=np.float32) * np.exp2(rng.integers(-12, 13, shape)).astype(np.float32)
    if cols: v *= np.repeat(np.exp2(rng.integers(-cols, cols + 1, shape[:-2] + (1, shape[-1] // 4))) * (rng.random(shape[:-2] + (1, shape[-1] // 4)) > 0.0625), 4, axis=-1).astype(np.float32)
    return mx_ref.flush(v.astype(BF))
T, K, O = 512, 128, 2
def setup_inputs(rng):
    u = np.zeros((128, 512), BF); u[:, :4] = f(rng, 128, 4)
    return {"x": f(rng, N, 128, 4 * T), "u": np.stack([u] * N), "w": f(rng, N, 128, 512 * O)}
def signs(d):
    return np.where(d["u"][0][:, :4].astype(np.float32) < 0, -1, 1).astype(np.float32)
def blocks(rng, n):
    return np.repeat(rng.permutation(16) < n, 8)
def plant(rng, d, n):
    for s in range(N):
        v = d["x"][s].astype(np.float32).reshape(128, T, 4)
        k = rng.permutation(T)[:n[s]]
        v[:, k] = np.abs(v[:, k]) * signs(d)[:, None] * np.float32(8)
        d["x"][s] = v.reshape(128, -1).astype(BF)
    return d
def setup_inputs_one(rng):
    d = setup_inputs(rng); return plant(rng, d, np.where(np.arange(N) == rng.integers(0, N), K, 0))
def setup_inputs_zeros(rng):
    d = setup_inputs(rng); m = blocks(rng, 2)
    d["u"][:, ~m] = 0
    k = rng.permutation(N * T); g = np.full(N * T, -1, np.float32)
    g[k[:K // 3]] = 1; g[k[K // 3:2 * (K // 3)]] = 0
    v = np.abs(d["x"][:, m].astype(np.float32)).reshape(N, -1, T, 4)
    d["x"][:, m] = (v * signs(d)[m][:, None] * g.reshape(N, 1, T, 1)).reshape(N, -1, 4 * T).astype(BF)
    return d
def setup_inputs_few(rng):
    d = setup_inputs(rng); p = rng.permutation(N); g = p[N - N // 2:]
    d["x"][g] = (-np.abs(d["x"][g].astype(np.float32)) * np.tile(signs(d), (1, T))).astype(BF)
    n = np.zeros(N, int); n[p[:2]] = [K * 3 // 5, K - K * 3 // 5]
    return plant(rng, d, n)
def setup_inputs_ties(rng):
    d = setup_inputs(rng); b = f(rng, 128, 4 * 40); m = blocks(rng, 4)
    d["u"][:, m] = 0
    d["x"] = np.stack([cols(b, rng.permutation(np.arange(T) % 40)) for r in range(N)])
    d["x"][:, m] = f(rng, N, 32, 4 * T); return d
def setup_inputs_spread(rng):
    d = setup_inputs(rng); d["x"] = wide(rng, N, 128, 4 * T, cols=8); return d
def check_inputs(d):
    b = []
    u = d["u"].astype(np.float32)
    if (u != u[:1]).any(): b.append("u_same")
    if (u[:, :, 4:] != 0).any(): b.append("u_zero")
    return b
def reference(x, u, w):
    s = np.stack([mx_ref.matmul(mx_ref.quantize(u[r]), mx_ref.quantize(x[r]))[0] for r in range(N)]).reshape(-1) + np.float32(0.0)
    best = np.lexsort((np.arange(N * T), -s))[:K]
    V = mx_ref.quantize(cols(np.concatenate(list(x), axis=1), best))
    y = np.zeros((N, 128, O * K), np.float32)
    for r in range(N):
        for o in range(O): y[r][:, K * o:K * o + K] = mx_ref.matmul(mx_ref.quantize(np.ascontiguousarray(w[r][:, 512 * o:512 * o + 512])), V)
    who = np.stack([best // T, best % T]).astype(np.float32)
    return {"y": y, "id": np.stack([who] * N)}

@@ -1,0 +1,424 @@
+from concourse.bass import DstId, RemoteDMATransfer
+from concourse.mybir import dt, AluOpType, AxisListType, ActivationFunctionType
+
+OP = AluOpType
+COPY = ActivationFunctionType.Copy
+IDENT = ActivationFunctionType.Identity
+SQUARE = ActivationFunctionType.Square
+K = 128
+BIG = 1e29
+LIFT = 256.0
+GID = 4096
+
+SCRATCH = {
+    "ur": ("sbuf", [128, 512], "bfloat16"), "zoff": ("sbuf", [128, 8], "uint16"),
+    "uq0": ("sbuf", [128, 128], "float8_e4m3fn_x4"), "us0": ("sbuf", [128, 128], "uint8"),
+    "uq": ("sbuf", [128, 128], "float8_e4m3fn_x4"), "us": ("sbuf", [128, 128], "uint8"),
+    "xb": ("sbuf", [128, 2048], "bfloat16"),
+    "xq": ("sbuf", [128, 512], "float8_e4m3fn_x4"), "xs": ("sbuf", [128, 512], "uint8"),
+    "wb": ("sbuf", [128, 1024], "bfloat16"),
+    "wq": ("sbuf", [128, 256], "float8_e4m3fn_x4"), "ws": ("sbuf", [128, 256], "uint8"),
+    "c1": ("sbuf", [128, 256], "float8_e4m3fn_x4"), "s1": ("sbuf", [128, 256], "uint8"),
+    "c2": ("sbuf", [128, 256], "float8_e4m3fn_x4"), "s2": ("sbuf", [128, 256], "uint8"),
+    "yw0": ("sbuf", [128, 256], "float32"), "yw1": ("sbuf", [128, 256], "float32"),
+    "yb0": ("sbuf", [128, 128], "float32"), "yb1": ("sbuf", [128, 128], "float32"),
+    "psf": ("psum", [128, 2048], "float32"),
+    "psp": ("psum", [128, 2048], "float32"),
+    "ip": ("sbuf", [128, 4], "int32"), "pt": ("sbuf", [128, 4], "float32"),
+    "it": ("sbuf", [128, 128], "int32"), "ita": ("sbuf", [128, 128], "int32"),
+    "nb0": ("sbuf", [128, 128], "float32"), "nb": ("sbuf", [128, 128], "float32"),
+    "ch0": ("sbuf", [128, 128], "float32"), "ch1": ("sbuf", [128, 128], "float32"), "ch": ("sbuf", [128, 128], "float32"),
+    "i3": ("sbuf", [128, 64], "float32"), "vals1": ("sbuf", [128, 64], "float32"),
+    "i5": ("sbuf", [128, 16], "int32"), "eoff": ("sbuf", [128, 16], "uint16"),
+    "i6": ("sbuf", [128, 8], "float32"), "gm": ("sbuf", [128, 8], "float32"), "hs": ("sbuf", [128, 128], "float32"),
+    "i7": ("sbuf", [128, 32], "float32"), "hm": ("sbuf", [128, 32], "float32"),
+    "pca": ("sbuf", [128, 3], "int32"), "pcf": ("sbuf", [128, 3], "float32"), "pcq": ("sbuf", [128, 2], "float32"),
+    "pct": ("sbuf", [128, 2], "float32"),
+    "sf": ("sbuf", [128, 512], "float32"), "sm": ("sbuf", [128, 512], "float32"),
+    "cma": ("sbuf", [128, 648], "float32"), "cmb": ("sbuf", [128, 648], "float32"),
+    "cmc": ("sbuf", [128, 648], "float32"), "cmd": ("sbuf", [128, 648], "float32"),
+    "junk": ("sbuf", [128, 4096], "bfloat16"),
+    "pl1": ("sbuf", [128, 4], "float32"),
+    "msg": ("sbuf", [128, 32], "float32"),
+    "at": ("sbuf", [128, 128], "float32"), "o1f": ("sbuf", [128, 8], "float32"), "o1g": ("sbuf", [128, 8], "float32"),
+    "am": ("sbuf", [128, 128], "float32"),
+    "bc": ("sbuf", [128, 128], "float32"), "bs": ("sbuf", [128, 128], "float32"),
+    "off2": ("sbuf", [128, 8], "uint16"),
+    "yx": ("sbuf", [128, 256], "float32"), "fs": ("sbuf", [128, 256], "float32"),
+    "ps": ("sbuf", [128, 2], "float32"), "sel": ("sbuf", [128, 2], "float32"), "nsel": ("sbuf", [128, 2], "float32"),
+    "vd": ("sbuf", [128, 2], "float32"), "cp": ("sbuf", [128, 2], "float32"),
+    "ba": ("sbuf", [128, 520], "float32"), "bb": ("sbuf", [128, 520], "float32"),
+    "pl2": ("sbuf", [128, 2], "float32"),
+    "zx": ("sbuf", [128, 64], "float32"), "zt": ("sbuf", [128, 64], "float32"),
+    "vals2": ("sbuf", [128, 32], "float32"),
+    "idn": ("sbuf", [32, 16], "int32"), "idi": ("sbuf", [32, 32], "int32"), "idf": ("sbuf", [32, 32], "float32"),
+}
+for _n in ("1", "2"):
+    SCRATCH["pu" + _n] = ("sbuf", [128, 4], "uint16")
+    SCRATCH["win" + _n] = ("sbuf", [128, 512], "float32")
+    SCRATCH["sc" + _n] = ("sbuf", [128, 128], "float32")
+    SCRATCH["qa" + _n] = ("sbuf", [64, 8], "float32")
+    for _b in ("ti", "to", "tw", "tb"):
+        SCRATCH[_b + _n] = ("sbuf", [32, 32], "float32")
+    SCRATCH["lst" + _n] = ("sbuf", [128, 8], "uint16")
+
+SEMAPHORES = ["v", "s", "t", "gc", "du", "dx0", "dx1", "dx2", "dx3", "dw", "dy0", "dy1", "did",
+              "h1c", "h1s", "h2c", "h2s", "hm", "sent"]
+
+
+def rank_program(g, core, T, topo):
+    rank = T.rank_of(core)
+    if rank is None:
+        return
+    v, s, t, y = g.vector, g.scalar, g.tensor, g.sync
+    queue = {"g": g, "v": v, "s": s, "t": t, "y": y}
+    count, waited = {}, {}
+    odd, P, Q = rank % 2, rank // 2, (rank // 2) ^ 1
+    own, arr = slice(K * P, K * P + K), slice(K * Q, K * Q + K)
+
+    def done(ins, sem, n=1):
+        ins.then_inc(T.sem[sem], n)
+        count[sem] = count.get(sem, 0) + n
+        return (sem, count[sem])
+
+    def wait(q, *tokens):
+        best = {}
+        for sem, n in tokens:
+            best[sem] = max(best.get(sem, 0), n)
+        for sem, n in best.items():
+            if waited.get((q, sem), 0) < n:
+                waited[(q, sem)] = n
+                queue[q].wait_ge(T.sem[sem], n)
+
+    def V(ins): return done(ins, "v")
+    def S(ins): return done(ins, "s")
+    def X(ins): return done(ins, "t")
+
+    du = done(s.dma_start(T.ur[:, 0:8], T.u[:, 0:8]), "du", 16)
+    dx = [done(y.dma_start(T.xb[:, 512 * d:512 * d + 512], T.x[:, 512 * d:512 * d + 512]), "dx%d" % d, 16) for d in range(4)]
+    dw = done(y.dma_start(T.wb[:, 0:1024], T.w[:, 0:1024]), "dw", 16)
+
+    def iota(buf, pattern, base, cm, flt=False):
+        if flt:
+            return done(g.iota(buf, pattern, base, cm, allow_small_or_imprecise_dtypes=True), "gc")
+        return done(g.iota(buf, pattern, base, cm), "gc")
+    k_it = iota(T.it[:, 0:128], [[1, 128]], 128, -1)
+    k_ip = iota(T.ip[:, 0:4], [[0, 4]], 0, 1)
+    k_i3 = iota(T.i3[:, 0:64], [[128, 4], [1, 16]], 0, 0, True)
+    k_i6 = iota(T.i6[:, 0:8], [[16, 8]], 0, 0, True)
+    k_pt = iota(T.pt[:, 0:4], [[0, 4]], 0, 1, True)
+    k_i5 = iota(T.i5[:, 0:16], [[8, 2], [1, 4], [0, 2]], 0, 0)
+    k_i7 = iota(T.i7[:, 0:32], [[16, 2], [0, 16]], 0, 0, True)
+
+    k_ur = V(v.memset(T.ur[:, 8:512], 0.0))
+    k_zo = V(v.memset(T.zoff[:, 0:8], 0))
+    V(v.memset(T.win1[:, 0:512], 0.0))
+    wait("v", k_it)
+    k = V(v.tensor_scalar(T.ita[:, 0:128], T.it[:, 0:128], 15, None, OP.bitwise_and))
+    wait("v", k)
+    k_d = V(v.tensor_scalar(T.ch0[:, 0:128], T.ita[:, 0:128], 2.0, None, OP.min))
+
+    wait("v", du, k_ur)
+    k_u0 = V(v.quantize_mx(T.uq0[:, 0:128], T.us0[:, 0:128], T.ur[:, 0:512]))
+    wait("v", k_u0, k_zo)
+    k_uc = V(v.tensor_copy(T.uq[:, 0:128].bitcast(dt.uint32), T.uq0[:, 0:128].bitcast(dt.uint32).indirect(T.zoff[:, 0:8])))
+    wait("s", k_u0)
+    k_us = S(s.activation(T.us[:, 0:128], T.us0[:, 0:128].indirect(T.zoff[:, 0:8]), COPY))
+    k = S(s.activation(T.ch1[:, 0:128], T.ch0[:, 0:128], SQUARE, bias=-1.25))
+    wait("s", k)
+    k_ch = S(s.activation(T.ch[:, 0:128], T.ch1[:, 0:128], IDENT, bias=1.125 * LIFT, scale=-2 * LIFT))
+
+    kq = [None] * 4
+
+    def quant(d):
+        e = slice(128 * d, 128 * d + 128)
+        wait("v", dx[d])
+        kq[d] = V(v.quantize_mx(T.xq[:, e], T.xs[:, e], T.xb[:, 512 * d:512 * d + 512]))
+    quant(0)
+    wait("v", k_ip)
+    V(v.tensor_scalar(T.pca[:, 0:1], T.ip[:, 0:1], 112, None, OP.bitwise_and))
+    V(v.tensor_scalar(T.pca[:, 1:2], T.ip[:, 0:1], 15, None, OP.bitwise_and))
+    b = V(v.tensor_scalar(T.pca[:, 2:3], T.ip[:, 0:1], 16, None, OP.bitwise_and))
+    quant(1)
+    wait("v", b)
+    b = V(v.tensor_copy(T.pcf[:, 0:3], T.pca[:, 0:3]))
+    wait("v", b, k_i3)
+    V(v.tensor_scalar(T.pcq[:, 0:1], T.pcf[:, 1:2], 15.0, -8 * LIFT, OP.is_lt, OP.mult))
+    V(v.tensor_scalar(T.vals1[:, 0:64], T.i3[:, 0:64], T.pcf[:, 0:1], 0.5, OP.add, OP.mult))
+    quant(2)
+
+    kp, kh, kf, km = [None] * 4, [None] * 2, [None] * 4, [None] * 4
+
+    def down(c):
+        e = slice(128 * c, 128 * c + 128)
+        wait("t", k_u0, kq[c])
+        kp[c] = X(t.matmul_mx(T.psp[:, 512 * c:512 * c + 128], T.xq[:, e], T.xs[:, e], T.uq0[:, 0:128], T.us0[:, 0:128], True, True))
+
+    def half(h):
+        e = slice(256 * h, 256 * h + 256)
+        wait("t", k_uc, k_us, kq[2 * h + 1])
+        kh[h] = X(t.matmul_mx(T.psf[:, 512 * h:512 * h + 256], T.uq[:, 0:128], T.us[:, 0:128], T.xq[:, e], T.xs[:, e], True, True))
+
+    def block(c):
+        e = slice(128 * c, 128 * c + 128)
+        o = 512 * (2 + c % 2)
+        wait("t", k_uc, k_us, kq[c])
+        if c > 1:
+            wait("t", kf[c - 2])
+        k = X(t.matmul_mx(T.psf[:, o:o + 128], T.uq[:, 0:128], T.us[:, 0:128], T.xq[:, e], T.xs[:, e], True, True))
+        wait("s", k)
+        kf[c] = S(s.activation(T.sf[:, e], T.psf[:, o:o + 128], COPY))
+        wait("g", kf[c])
+        km[c] = done(g.affine_select(T.sm[:, e], T.sf[:, e], [[-1, 128]], OP.is_gt, BIG, 0, 1), "gc")
+
+    cm = [T.cma, T.cmb, T.cmc, T.cmd]
+    jk = [0]
+
+    def total(buf, lo, hi, out, *tokens):
+        wait("s", *tokens)
+        n = hi - lo
+        r = S(s.activation(T.junk[:, jk[0]:jk[0] + n], buf[:, lo:hi], COPY, accum_out=out))
+        jk[0] = jk[0] + n if jk[0] + n + 700 <= 4096 else 0
+        return r
+
+    def cmp(out, src, col, op, weight=None):
+        if weight is None:
+            return V(v.tensor_scalar(out, src, col, None, op))
+        return V(v.tensor_scalar(out, src, col, weight, op, OP.mult))
+    sp = [T.psp[:, 512 * c:512 * c + 1] for c in range(4)]
+    h0, h1, sm = T.psf[:, 0:256], T.psf[:, 512:768], T.sm
+    down(0)
+    block(0)
+    half(0)
+    down(1)
+    block(1)
+    down(2)
+    wait("v", kp[0], kh[0])
+    cmp(cm[0][:, 0:256], h0, sp[0], OP.is_gt)
+    quant(3)
+    half(1)
+    wait("v", kp[1])
+    cmp(cm[1][:, 0:128], T.psf[:, 0:128], sp[1], OP.is_ge)
+    k = cmp(cm[1][:, 128:256], T.psf[:, 128:256], sp[1], OP.is_gt)
+    e1 = total(cm[1], 0, 256, cm[1][:, 256:257], k)
+    wait("v", km[0])
+    k = cmp(cm[0][:, 256:384], sm[:, 0:128], sp[0], OP.is_equal)
+    e0 = total(cm[0], 0, 384, cm[0][:, 384:385], k)
+    block(2)
+    down(3)
+    wait("v", kp[2])
+    cmp(cm[2][:, 0:256], h0, sp[2], OP.is_ge)
+    wait("v", kh[1])
+    k = cmp(cm[2][:, 256:512], h1, sp[2], OP.is_gt)
+    e2 = total(cm[2], 0, 512, cm[2][:, 512:513], k)
+    k = cmp(cm[0][:, 385:641], h1, sp[0], OP.is_gt)
+    block(3)
+    total(cm[0], 384, 641, T.pl1[:, 0:1], k, e0)
+    cmp(cm[1][:, 257:513], h1, sp[1], OP.is_gt)
+    wait("v", km[1])
+    k = cmp(cm[1][:, 513:641], sm[:, 128:256], sp[1], OP.is_equal)
+    pl = total(cm[1], 256, 641, T.pl1[:, 1:2], k, e1)
+    wait("v", kp[3])
+    k = cmp(cm[3][:, 0:256], h0, sp[3], OP.is_ge)
+    e3 = total(cm[3], 0, 256, cm[3][:, 640:641], k)
+    cmp(cm[3][:, 256:384], T.psf[:, 512:640], sp[3], OP.is_ge)
+    cmp(cm[3][:, 384:512], T.psf[:, 640:768], sp[3], OP.is_gt)
+    wait("v", km[2])
+    a = cmp(cm[2][:, 513:641], sm[:, 256:384], sp[2], OP.is_equal)
+    wait("v", km[3])
+    b = cmp(cm[3][:, 512:640], sm[:, 384:512], sp[3], OP.is_equal)
+    V(v.memset(T.ti1[:, 0:32], 0.0))
+    wait("v", a, e2)
+    V(v.tensor_reduce(T.pl1[:, 2:3], cm[2][:, 512:641], AxisListType.X, OP.add))
+    wait("v", b, e3)
+    a = V(v.tensor_reduce(T.pl1[:, 3:4], cm[3][:, 256:641], AxisListType.X, OP.add))
+    wait("v", a, pl)
+    if odd:
+        k_pu = V(v.tensor_scalar(T.pu1[:, 0:4], T.pl1[:, 0:4], -1.0, 511.0, OP.mult, OP.add))
+    else:
+        k_pu = V(v.tensor_copy(T.pu1[:, 0:4], T.pl1[:, 0:4]))
+
+    def invert(n, ready, cols, width, vals, lo, scale, fill):
+        W = lambda b: T[b + n]
+        wait("v", k_ch, *ready)
+        a = V(v.tensor_copy(W("win")[:, 0:width].indirect(W("pu")[:, 0:cols]), vals[:, 0:16 * cols]))
+        wait("v", a)
+        a = V(v.tensor_tensor_scan(W("sc")[:, 0:128], T.ch[:, 0:128], W("win")[:, lo:lo + 128], 0.0, OP.add, OP.max))
+        wait("v", a)
+        a = V(v.tensor_tensor(W("qa")[0:64, 0:8], W("sc")[0:64, 15:128:16], W("sc")[64:128, 15:128:16], OP.add))
+        wait("v", a)
+        a = V(v.tensor_tensor(W("ti")[0:32, 0:8], W("qa")[0:32, 0:8], W("qa")[32:64, 0:8], OP.add))
+        wait("v", a)
+        a = V(v.transpose(W("to")[0:32, 0:32], W("ti")[0:32, 0:32]))
+        wait("v", a)
+        V(v.tensor_tensor(W("tw")[0:32, 0:16], W("to")[0:32, 0:16], W("to")[0:32, 16:32], OP.add))
+        a = V(v.tensor_tensor(W("tw")[0:32, 16:32], W("to")[0:32, 0:16], W("to")[0:32, 16:32], OP.add))
+        wait("v", a)
+        a = V(v.transpose(W("tb")[0:32, 0:32], W("tw")[0:32, 0:32]))
+        fill()
+        wait("v", a)
+        for h in range(4):
+            a = V(v.tensor_scalar(W("lst")[32 * h:32 * h + 32, 0:8], W("tb")[0:32, 0:8], T.pcq[0:32, 0:1], scale, OP.add, OP.mult))
+        return a
+
+    def pick(dc, ds, sc, ss, off, ready_c, ready_s):
+        wait("v", *ready_c)
+        a = V(v.tensor_copy(dc.bitcast(dt.uint32), sc.bitcast(dt.uint32).indirect(off[:, 0:8])))
+        wait("s", *ready_s)
+        b = S(s.activation(ds, ss.indirect(off[:, 0:8]), COPY))
+        return a, b
+
+    def send(out_c, in_c, out_s, in_s, a, b, dst, sem_c, sem_s):
+        rid, pid = topo.addr(dst, core)
+        m = topo.mask(core, dst)
+        n = len(topo.engines(core, dst))
+        for o, i, k, sem in ((out_c.bitcast(dt.uint8), in_c.bitcast(dt.uint8), a, sem_c), (out_s, in_s, b, sem_s)):
+            wait("g", k)
+            g.remote_dma(o, i, T.sem[sem], T.sem["sent"], pid, rid, m)
+            count["sent"] = count.get("sent", 0) + n
+        return (sem_c, n), (sem_s, n)
+
+    def number_constants():
+        V(v.tensor_scalar(T.gm[:, 0:8], T.i6[:, 0:8], T.pcf[:, 0:1], None, OP.is_equal))
+        V(v.tensor_scalar(T.pct[:, 0:1], T.pt[:, 0:1], 128.0 * P + 512.0 * rank / GID, None, OP.add))
+    wait("v", k_i6, k_pt)
+    k_l1 = invert("1", (k_pu,), 4, 512, T.vals1, 384 if odd else 0, 2.0, number_constants)
+    a1, b1 = pick(T.c1[:, 0:K], T.s1[:, 0:K], T.xq[:, 0:512], T.xs[:, 0:512], T.lst1, (k_l1,), (k_l1,))
+    mate = T.cores[rank ^ 1]
+    in1c, in1s = send(T.c1[:, K:2 * K], T.c1[:, 0:K], T.s1[:, K:2 * K], T.s1[:, 0:K], a1, b1, mate, "h1c", "h1s")
+
+    m0 = 8 * rank
+    wait("t", a1, b1)
+    kaf = X(t.matmul_mx(T.psf[:, 0:128], T.uq[:, 0:128], T.us[:, 0:128], T.c1[:, 0:128], T.s1[:, 0:128], True, True))
+    kap = X(t.matmul_mx(T.psp[:, 0:128], T.c1[:, 0:128], T.s1[:, 0:128], T.uq0[:, 0:128], T.us0[:, 0:128], True, True))
+    a = V(v.tensor_scalar(T.o1f[:, 0:8], T.lst1[:, 0:8], 1.0 / GID, T.pct[:, 0:1], OP.mult, OP.add))
+    wait("v", a)
+    a = V(v.tensor_tensor(T.o1g[:, 0:8], T.o1f[:, 0:8], T.gm[:, 0:8], OP.mult))
+    wait("s", kap)
+    k_m4 = S(s.activation(T.msg[:, m0 + 4:m0 + 5], T.psp[:, 0:1], COPY))
+    wait("v", a, kaf)
+    a2 = V(v.transpose(T.at[:, 0:128], T.psf[:, 0:128]))
+    V(v.tensor_reduce(T.msg[:, m0 + 5:m0 + 6], T.o1g[:, 0:8], AxisListType.X, OP.add))
+    wait("v", a2)
+    k_msg = V(v.tensor_copy(T.msg[:, m0:m0 + 4], T.at[:, 0:128:32]))
+    wait("g", k_msg, k_m4)
+    ids, m = [], topo.mask(core, mate)
+    for other in (rank ^ 2, rank ^ 3, rank ^ 1):
+        dst = T.cores[other]
+        rid, pid = topo.addr(dst, core)
+        ids.append(DstId(rid=rid, pnc=pid))
+        m &= topo.mask(core, dst)
+    n = bin(m).count("1")
+    view = T.msg[:, m0:m0 + 6]
+    g.remote_dma_fused([RemoteDMATransfer(dst_ids=ids, dma_engine_mask=m, remote_sem=T.sem["hm"], srcs=[view], dsts=[view] * 3)],
+                       local_sem=T.sem["sent"])
+    in_msg = ("hm", 3 * n)
+    count["sent"] += n
+
+    a = V(v.tensor_scalar(T.nb0[:, 0:128], T.ita[:, 0:128], 0.0, 2 * BIG, OP.is_equal, OP.mult))
+    b = V(v.memset(T.hs[:, 0:128], 0.0))
+    k = V(v.tensor_scalar(T.pcq[:, 1:2], T.pcf[:, 1:2], 128.0, None, OP.add))
+    wait("v", a)
+    a = V(v.tensor_scalar(T.nb[:, 0:128], T.nb0[:, 0:128], -BIG, None, OP.add))
+    wait("v", b, k)
+    k_hs = V(v.tensor_scalar(T.hs[:, 0:128:16], T.i6[:, 0:8], T.pcq[:, 1:2], 1.0 / 128, OP.add, OP.mult))
+    wait("v", a)
+    k_am = V(v.tensor_tensor(T.am[:, 0:128], T.nb[:, 0:128], T.psf[:, 0:128], OP.min))
+    wait("v", dw)
+    k_w = V(v.quantize_mx(T.wq[:, 0:256], T.ws[:, 0:256], T.wb[:, 0:1024]))
+    wait("v", k_i5, k_i7)
+    V(v.tensor_copy(T.eoff[:, 0:16], T.i5[:, 0:16]))
+    V(v.tensor_scalar(T.hm[:, 0:32], T.i7[:, 0:32], T.pcf[:, 2:3], None, OP.is_equal))
+    k_co = V(v.tensor_scalar(T.pct[:, 1:2], T.pt[:, 0:1], -2.0, 127.0, OP.mult, OP.add))
+    V(v.memset(T.win2[:, 0:384], 0.0))
+    V(v.memset(T.ti2[:, 0:32], 0.0))
+
+    word = lambda rk, w: T.msg[:, 8 * rk + w:8 * rk + w + 1]
+    E, O = T.msg[:, 4:32:16], T.msg[:, 12:32:16]
+    ps, sel, nsel = [[T[b][:, j:j + 1] for j in range(2)] for b in ("ps", "sel", "nsel")]
+    fr = (T.psf[:, 512:640], T.psf[:, 0:128]) if odd else (T.psf[:, 0:128], T.psf[:, 512:640])
+    wait("s", in_msg, k_co)
+    ky = S(s.activation(T.yx[:, 0:256], T.msg[:, 16 * Q:16 * Q + 16].indirect(T.eoff[:, 0:16]), COPY))
+    wait("t", in1c, in1s)
+    kb = X(t.matmul_mx(T.psf[:, 512:640], T.uq[:, 0:128], T.us[:, 0:128], T.c1[:, 128:256], T.s1[:, 128:256], True, True))
+    wait("v", kb, k_am)
+    a = V(v.tensor_tensor(T.bc[:, 0:128], T.am[:, 0:128], T.psf[:, 512:640], OP.is_gt if odd else OP.is_ge))
+    wait("v", in_msg, k_m4)
+    V(v.tensor_tensor(T.ps[:, 0:2], E, O, OP.max))
+    V(v.tensor_tensor(T.sel[:, 0:2], O, E, OP.is_gt))
+    wait("v", a, k_hs)
+    a = V(v.tensor_tensor_scan(T.bs[:, 0:128], T.hs[:, 0:128], T.bc[:, 0:128], 0.0, OP.max, OP.subtract))
+    V(v.tensor_tensor(T.nsel[:, 0:2], E, O, OP.is_ge))
+    k_vd = V(v.tensor_tensor(T.vd[:, 0:2], T.msg[:, 13:32:16], T.msg[:, 5:32:16], OP.subtract))
+    wait("v", a)
+    k_o2 = V(v.tensor_scalar(T.off2[:, 0:8], T.bs[:, 15:128:16], 128.0, None, OP.mult))
+    wait("v", k_vd)
+    cmp(T.ba[:, 0:128], fr[1], ps[P], OP.is_gt, nsel[P])
+    a2, b2 = pick(T.c2[:, own], T.s2[:, own], T.c1[:, 0:256], T.s1[:, 0:256], T.off2, (k_o2, in1c), (k_o2, in1s))
+    in2c, in2s = send(T.c2[:, own], T.c2[:, own], T.s2[:, own], T.s2[:, own], a2, b2, T.cores[rank ^ 2], "h2c", "h2s")
+
+    def products(side, bank, *ready):
+        wait("t", k_w, *ready)
+        return [X(t.matmul_mx(bank[:, 512 * (o + 2):512 * (o + 2) + 128], T.wq[:, 128 * o:128 * o + 128], T.ws[:, 128 * o:128 * o + 128],
+                              T.c2[:, side], T.s2[:, side], True, True)) for o in range(2)]
+    ko = products(own, T.psf, a2, b2)
+    kr = products(arr, T.psp, in2c, in2s)
+
+    wait("s", k_vd)
+    for j, buf in ((P, T.ba), (Q, T.bb)):
+        kc = S(s.activation(buf[:, 256:257], sel[j], IDENT, bias=T.pt[:, 0:1], scale=T.pct[:, 1:2]))
+    a = cmp(T.ba[:, 128:256], fr[0], ps[P], OP.is_ge, sel[P])
+    ka = total(T.ba, 0, 257, T.ba[:, 257:258], a, kc)
+    for j in range(2):
+        kcp = S(s.activation(T.cp[:, j:j + 1], T.vd[:, j:j + 1], IDENT, bias=word(2 * j, 5), scale=sel[j]))
+    wait("v", ky)
+    kt = V(v.transpose(T.fs[:, 0:256], T.yx[:, 0:256]))
+    for f in range(2):
+        k = cmp(T.bb[:, 128 * f:128 * f + 128], fr[f], ps[Q], OP.is_ge if P < Q else OP.is_gt)
+    wait("s", kcp)
+    for j in range(2):
+        kz = S(s.activation(T.zx[:, 32 * j:32 * j + 32], T.hm[:, 0:32], COPY, scale=T.cp[:, j:j + 1]))
+    kb = total(T.bb, 0, 257, T.bb[:, 257:258], k)
+    wait("v", kt)
+    k = cmp(T.ba[:, 258:514], T.fs[:, 0:256], ps[P], OP.is_ge if Q < P else OP.is_gt)
+    ka = total(T.ba, 257, 514, T.pl2[:, P:P + 1], k, ka)
+    k = cmp(T.bb[:, 258:386], T.fs[:, 128:256], ps[Q], OP.is_gt, nsel[Q])
+    kb = total(T.bb, 257, 386, T.bb[:, 514:515], k, kb)
+    k = cmp(T.bb[:, 386:514], T.fs[:, 0:128], ps[Q], OP.is_ge, sel[Q])
+    wait("v", kz)
+    a = V(v.transpose(T.zt[:, 0:64], T.zx[:, 0:64]))
+    wait("v", a)
+    for j in range(2):
+        V(v.tensor_tensor(T.vals2[:, 16 * j:16 * j + 16], T.zt[:, 32 * j:32 * j + 16], T.zt[:, 32 * j + 16:32 * j + 32], OP.add))
+    wait("v", k, kb)
+    a = V(v.tensor_reduce(T.pl2[:, Q:Q + 1], T.bb[:, 386:515], AxisListType.X, OP.add))
+    wait("v", a, ka)
+    kv = V(v.tensor_copy(T.pu2[:, 0:2], T.pl2[:, 0:2]))
+
+    yw = (T.yw0, T.yw1)
+    for side, bank, kk in ((own, T.psf, ko), (arr, T.psp, kr)):
+        for o in range(2):
+            wait("s", kk[o])
+            kyw = S(s.activation(yw[o][:, side], bank[:, 512 * (o + 2):512 * (o + 2) + 128], COPY))
+
+    def numbers():
+        V(v.tensor_scalar(T.idn[0:32, 0:16], T.tw2[0:32, 0:16], float(GID), None, OP.mult))
+    k_l2 = invert("2", (kv,), 2, 384, T.vals2, 0, 1.0, numbers)
+
+    wait("v", k_l2, kyw)
+    ky0 = V(v.tensor_copy(T.yb0[:, 0:128], T.yw0[:, 0:256].indirect(T.lst2[:, 0:8])))
+    wait("s", k_l2, kyw)
+    ky1 = S(s.activation(T.yb1[:, 0:128], T.yw1[:, 0:256].indirect(T.lst2[:, 0:8]), COPY))
+    wait("s", ky1)
+    d1 = done(s.dma_start(T.y[:, 128:256], T.yb1[:, 0:128]), "dy1", 16)
+    wait("y", ky0)
+    d0 = done(y.dma_start(T.y[:, 0:128], T.yb0[:, 0:128]), "dy0", 16)
+    V(v.tensor_scalar(T.idi[0:32, 0:16], T.idn[0:32, 0:16], 9, 3, OP.arith_shift_right, OP.bitwise_and))
+    a = V(v.tensor_scalar(T.idi[0:32, 16:32], T.idn[0:32, 0:16], 511, None, OP.bitwise_and))
+    wait("v", a)
+    kid = V(v.tensor_copy(T.idf[0:32, 0:32], T.idi[0:32, 0:32]))
+    wait("y", kid)
+    for row in range(2):
+        d2 = done(y.dma_start(T["id"][row:row + 1, 0:128], T.idf[0:8, 16 * row:16 * row + 16]), "did", 16)
+    wait("g", ("sent", count["sent"]), in1c, in1s, in2c, in2s, in_msg, du, *dx, dw,
+         ("gc", count["gc"]), ("v", count["v"]), ("s", count["s"]), ("t", count["t"]), d0, d1, d2)

@@ -1,18 +1,18 @@
 from concourse.bass import DstId, RemoteDMATransfer
-from concourse.mybir import dt, AluOpType, AxisListType, ActivationFunctionType
+from concourse.mybir import dt, AluOpType, ActivationFunctionType
 
 OP = AluOpType
-COPY = ActivationFunctionType.Copy
-IDENT = ActivationFunctionType.Identity
-SQUARE = ActivationFunctionType.Square
+ACT = ActivationFunctionType
+COPY, IDENT = ACT.Copy, ACT.Identity
 K = 128
 BIG = 1e29
-LIFT = 256.0
-GID = 4096
+STEP = 1.25 * 2.0 ** -24
+TINY = 2.0 ** -122
+SLOT = 24
 
 SCRATCH = {
-    "ur": ("sbuf", [128, 512], "bfloat16"), "zoff": ("sbuf", [128, 8], "uint16"),
-    "uq0": ("sbuf", [128, 128], "float8_e4m3fn_x4"), "us0": ("sbuf", [128, 128], "uint8"),
+    "ur": ("sbuf", [128, 520], "bfloat16"), "zoff": ("sbuf", [128, 8], "uint16"),
+    "uq0": ("sbuf", [128, 130], "float8_e4m3fn_x4"), "us0": ("sbuf", [128, 130], "uint8"),
     "uq": ("sbuf", [128, 128], "float8_e4m3fn_x4"), "us": ("sbuf", [128, 128], "uint8"),
     "xb": ("sbuf", [128, 2048], "bfloat16"),
     "xq": ("sbuf", [128, 512], "float8_e4m3fn_x4"), "xs": ("sbuf", [128, 512], "uint8"),
@@ -21,49 +21,43 @@ SCRATCH = {
     "c1": ("sbuf", [128, 256], "float8_e4m3fn_x4"), "s1": ("sbuf", [128, 256], "uint8"),
     "c2": ("sbuf", [128, 256], "float8_e4m3fn_x4"), "s2": ("sbuf", [128, 256], "uint8"),
     "yw0": ("sbuf", [128, 256], "float32"), "yw1": ("sbuf", [128, 256], "float32"),
-    "yb0": ("sbuf", [128, 128], "float32"), "yb1": ("sbuf", [128, 128], "float32"),
+    "yb": ("sbuf", [128, 256], "float32"),
     "psf": ("psum", [128, 2048], "float32"),
     "psp": ("psum", [128, 2048], "float32"),
-    "ip": ("sbuf", [128, 4], "int32"), "pt": ("sbuf", [128, 4], "float32"),
-    "it": ("sbuf", [128, 128], "int32"), "ita": ("sbuf", [128, 128], "int32"),
+    "ip": ("sbuf", [128, 2], "int32"), "pt": ("sbuf", [128, 2], "float32"),
+    "it": ("sbuf", [128, 128], "int32"), "ita": ("sbuf", [128, 128], "int32"), "tri": ("sbuf", [128, 128], "float32"),
     "nb0": ("sbuf", [128, 128], "float32"), "nb": ("sbuf", [128, 128], "float32"),
-    "ch0": ("sbuf", [128, 128], "float32"), "ch1": ("sbuf", [128, 128], "float32"), "ch": ("sbuf", [128, 128], "float32"),
-    "i3": ("sbuf", [128, 64], "float32"), "vals1": ("sbuf", [128, 64], "float32"),
+    "i3": ("sbuf", [128, 64], "float32"), "vals1": ("sbuf", [128, 64], "bfloat16"),
+    "i4": ("sbuf", [128, 32], "float32"), "vals2": ("sbuf", [128, 32], "bfloat16"),
     "i5": ("sbuf", [128, 16], "int32"), "eoff": ("sbuf", [128, 16], "uint16"),
-    "i6": ("sbuf", [128, 8], "float32"), "gm": ("sbuf", [128, 8], "float32"), "hs": ("sbuf", [128, 128], "float32"),
-    "i7": ("sbuf", [128, 32], "float32"), "hm": ("sbuf", [128, 32], "float32"),
-    "pca": ("sbuf", [128, 3], "int32"), "pcf": ("sbuf", [128, 3], "float32"), "pcq": ("sbuf", [128, 2], "float32"),
+    "i6": ("sbuf", [128, 8], "float32"), "hs": ("sbuf", [128, 128], "float32"),
+    "gr": ("sbuf", [128, 32], "float32"), "gt": ("sbuf", [128, 32], "float32"), "goff": ("sbuf", [128, 2], "uint16"),
+    "pca": ("sbuf", [128, 2], "int32"), "pcf": ("sbuf", [128, 2], "float32"), "pcq": ("sbuf", [128, 2], "float32"),
     "pct": ("sbuf", [128, 2], "float32"),
-    "sf": ("sbuf", [128, 512], "float32"), "sm": ("sbuf", [128, 512], "float32"),
-    "cma": ("sbuf", [128, 648], "float32"), "cmb": ("sbuf", [128, 648], "float32"),
-    "cmc": ("sbuf", [128, 648], "float32"), "cmd": ("sbuf", [128, 648], "float32"),
-    "junk": ("sbuf", [128, 4096], "bfloat16"),
-    "pl1": ("sbuf", [128, 4], "float32"),
-    "msg": ("sbuf", [128, 32], "float32"),
-    "at": ("sbuf", [128, 128], "float32"), "o1f": ("sbuf", [128, 8], "float32"), "o1g": ("sbuf", [128, 8], "float32"),
+    "sp": ("sbuf", [128, 4], "float32"), "dl": ("sbuf", [128, 4], "float32"), "thr": ("sbuf", [128, 512], "float32"),
+    "cm": ("sbuf", [128, 1536], "bfloat16"), "cs": ("sbuf", [128, 768], "bfloat16"),
+    "sg": ("sbuf", [128, 512], "bfloat16"), "junk": ("sbuf", [128, 512], "bfloat16"), "ls": ("sbuf", [128, 4], "float32"),
+    "msg": ("sbuf", [128, 4 * SLOT], "float32"), "at": ("sbuf", [128, 128], "float32"),
     "am": ("sbuf", [128, 128], "float32"),
     "bc": ("sbuf", [128, 128], "float32"), "bs": ("sbuf", [128, 128], "float32"),
     "off2": ("sbuf", [128, 8], "uint16"),
     "yx": ("sbuf", [128, 256], "float32"), "fs": ("sbuf", [128, 256], "float32"),
     "ps": ("sbuf", [128, 2], "float32"), "sel": ("sbuf", [128, 2], "float32"), "nsel": ("sbuf", [128, 2], "float32"),
-    "vd": ("sbuf", [128, 2], "float32"), "cp": ("sbuf", [128, 2], "float32"),
-    "ba": ("sbuf", [128, 520], "float32"), "bb": ("sbuf", [128, 520], "float32"),
-    "pl2": ("sbuf", [128, 2], "float32"),
-    "zx": ("sbuf", [128, 64], "float32"), "zt": ("sbuf", [128, 64], "float32"),
-    "vals2": ("sbuf", [128, 32], "float32"),
-    "idn": ("sbuf", [32, 16], "int32"), "idi": ("sbuf", [32, 32], "int32"), "idf": ("sbuf", [32, 32], "float32"),
+    "vd": ("sbuf", [128, 2], "float32"), "kc": ("sbuf", [128, 2], "float32"),
+    "ba": ("sbuf", [128, 512], "bfloat16"), "bb": ("sbuf", [128, 512], "bfloat16"), "bt": ("sbuf", [128, 512], "bfloat16"),
+    "cp": ("sbuf", [128, 64], "float32"), "idr": ("sbuf", [128, 256], "float32"), "idb": ("sbuf", [128, 128], "float32"),
 }
 for _n in ("1", "2"):
     SCRATCH["pu" + _n] = ("sbuf", [128, 4], "uint16")
-    SCRATCH["win" + _n] = ("sbuf", [128, 512], "float32")
-    SCRATCH["sc" + _n] = ("sbuf", [128, 128], "float32")
-    SCRATCH["qa" + _n] = ("sbuf", [64, 8], "float32")
-    for _b in ("ti", "to", "tw", "tb"):
-        SCRATCH[_b + _n] = ("sbuf", [32, 32], "float32")
-    SCRATCH["lst" + _n] = ("sbuf", [128, 8], "uint16")
+    SCRATCH["win" + _n] = ("sbuf", [128, 528], "bfloat16")
+    SCRATCH["tz" + _n] = ("sbuf", [128, 288], "bfloat16")
+    SCRATCH["qa" + _n] = ("sbuf", [128, 16], "float32")
+    SCRATCH["qb" + _n] = ("sbuf", [64, 16], "float32")
+    SCRATCH["qc" + _n] = ("sbuf", [128, 16], "float32")
+    SCRATCH["lst" + _n] = ("sbuf", [128, 16], "uint16")
 
-SEMAPHORES = ["v", "s", "t", "gc", "du", "dx0", "dx1", "dx2", "dx3", "dw", "dy0", "dy1", "did",
-              "h1c", "h1s", "h2c", "h2s", "hm", "sent"]
+SEMAPHORES = ["v", "s", "t", "gc", "du", "dx0", "dx1", "dx2", "dx3", "dw", "dy", "did",
+              "h1c", "h1s", "h2c", "h2s", "hm", "hp", "sent"]
 
 
 def rank_program(g, core, T, topo):
@@ -94,267 +88,264 @@ def rank_program(g, core, T, topo):
     def S(ins): return done(ins, "s")
     def X(ins): return done(ins, "t")
 
-    du = done(s.dma_start(T.ur[:, 0:8], T.u[:, 0:8]), "du", 16)
-    dx = [done(y.dma_start(T.xb[:, 512 * d:512 * d + 512], T.x[:, 512 * d:512 * d + 512]), "dx%d" % d, 16) for d in range(4)]
+    B = [0, 1, 2, 3] if odd else [3, 2, 1, 0]
+    du = done(s.dma_start(T.ur[:, 8:16], T.u[:, 0:8]), "du", 16)
+    dx = {d: done(y.dma_start(T.xb[:, 512 * d:512 * d + 512], T.x[:, 512 * d:512 * d + 512]), "dx%d" % d, 16) for d in B}
     dw = done(y.dma_start(T.wb[:, 0:1024], T.w[:, 0:1024]), "dw", 16)
 
-    def iota(buf, pattern, base, cm, flt=False):
+    def iota(buf, pattern, base, cm, flt=True):
         if flt:
             return done(g.iota(buf, pattern, base, cm, allow_small_or_imprecise_dtypes=True), "gc")
         return done(g.iota(buf, pattern, base, cm), "gc")
-    k_it = iota(T.it[:, 0:128], [[1, 128]], 128, -1)
-    k_ip = iota(T.ip[:, 0:4], [[0, 4]], 0, 1)
-    k_i3 = iota(T.i3[:, 0:64], [[128, 4], [1, 16]], 0, 0, True)
-    k_i6 = iota(T.i6[:, 0:8], [[16, 8]], 0, 0, True)
-    k_pt = iota(T.pt[:, 0:4], [[0, 4]], 0, 1, True)
-    k_i5 = iota(T.i5[:, 0:16], [[8, 2], [1, 4], [0, 2]], 0, 0)
-    k_i7 = iota(T.i7[:, 0:32], [[16, 2], [0, 16]], 0, 0, True)
+    k_it = iota(T.it[:, 0:128], [[1, 128]], 128, -1, False)
+    k_ip = iota(T.ip[:, 0:2], [[0, 2]], 0, 1, False)
+    k_i3 = iota(T.i3[:, 0:64], [[128, 4], [1, 16]], -256, 0)
+    wait("g", iota(T.gr[:, 0:32], [[0, 32]], 0, 1))
+    iota(T.gr[:, 2:10], [[32, 4], [160, 2]], 0, 0)
+    k_gr = iota(T.gr[:, 18:26], [[32, 4], [-128, 2]], 128, 0)
+    k_i6 = iota(T.i6[:, 0:8], [[16, 8]], 0, 0)
+    k_pt = iota(T.pt[:, 0:2], [[-128, 2]], 0, 1)
+    k_i5 = iota(T.i5[:, 0:16], [[SLOT, 2], [1, 4], [0, 2]], 0, 0, False)
+    k_i4 = iota(T.i4[:, 0:32], [[1, 2], [2, 16]], -128, 0)
 
-    k_ur = V(v.memset(T.ur[:, 8:512], 0.0))
-    k_zo = V(v.memset(T.zoff[:, 0:8], 0))
-    V(v.memset(T.win1[:, 0:512], 0.0))
+    V(v.memset(T.ur[:, 0:8], 0.0))
+    k_ur = V(v.memset(T.ur[:, 16:520], 0.0))
+    k_zo = V(v.memset(T.zoff[:, 0:8], 2))
+    lo1 = 384 if odd else 16
+    V(v.memset(T.win1[:, lo1 - 16:lo1 + 144], 0.0))
     wait("v", k_it)
-    k = V(v.tensor_scalar(T.ita[:, 0:128], T.it[:, 0:128], 15, None, OP.bitwise_and))
+    if odd:
+        k_tri = V(v.tensor_scalar(T.tri[:, 0:128], T.it[:, 0:128], 128.0, None, OP.is_gt))
+    else:
+        k_tri = V(v.tensor_scalar(T.tri[:, 0:128], T.it[:, 0:128], 128.0, -1.0, OP.is_lt, OP.mult))
+    wait("v", k_ip)
+    V(v.tensor_scalar(T.pca[:, 0:1], T.ip[:, 0:1], 112, None, OP.bitwise_and))
+    k = V(v.tensor_scalar(T.pca[:, 1:2], T.ip[:, 0:1], 15, None, OP.bitwise_and))
     wait("v", k)
-    k_d = V(v.tensor_scalar(T.ch0[:, 0:128], T.ita[:, 0:128], 2.0, None, OP.min))
+    k_pc = V(v.tensor_copy(T.pcf[:, 0:2], T.pca[:, 0:2]))
 
     wait("v", du, k_ur)
-    k_u0 = V(v.quantize_mx(T.uq0[:, 0:128], T.us0[:, 0:128], T.ur[:, 0:512]))
+    k_u0 = V(v.quantize_mx(T.uq0[:, 0:130], T.us0[:, 0:130], T.ur[:, 0:520]))
+    wait("v", k_i3, k_pc)
+    V(v.tensor_scalar(T.vals1[:, 0:64], T.i3[:, 0:64], T.pcf[:, 0:1], None, OP.add))
     wait("v", k_u0, k_zo)
-    k_uc = V(v.tensor_copy(T.uq[:, 0:128].bitcast(dt.uint32), T.uq0[:, 0:128].bitcast(dt.uint32).indirect(T.zoff[:, 0:8])))
+    k_uc = V(v.tensor_copy(T.uq[:, 0:128].bitcast(dt.uint32), T.uq0[:, 0:130].bitcast(dt.uint32).indirect(T.zoff[:, 0:8])))
     wait("s", k_u0)
-    k_us = S(s.activation(T.us[:, 0:128], T.us0[:, 0:128].indirect(T.zoff[:, 0:8]), COPY))
-    k = S(s.activation(T.ch1[:, 0:128], T.ch0[:, 0:128], SQUARE, bias=-1.25))
-    wait("s", k)
-    k_ch = S(s.activation(T.ch[:, 0:128], T.ch1[:, 0:128], IDENT, bias=1.125 * LIFT, scale=-2 * LIFT))
+    k_us = S(s.activation(T.us[:, 0:128], T.us0[:, 0:130].indirect(T.zoff[:, 0:8]), COPY))
+    wait("v", k_gr)
+    k_gt = V(v.transpose(T.gt[:, 0:32], T.gr[:, 0:32]))
 
-    kq = [None] * 4
+    kq = {}
 
     def quant(d):
         e = slice(128 * d, 128 * d + 128)
         wait("v", dx[d])
         kq[d] = V(v.quantize_mx(T.xq[:, e], T.xs[:, e], T.xb[:, 512 * d:512 * d + 512]))
-    quant(0)
-    wait("v", k_ip)
-    V(v.tensor_scalar(T.pca[:, 0:1], T.ip[:, 0:1], 112, None, OP.bitwise_and))
-    V(v.tensor_scalar(T.pca[:, 1:2], T.ip[:, 0:1], 15, None, OP.bitwise_and))
-    b = V(v.tensor_scalar(T.pca[:, 2:3], T.ip[:, 0:1], 16, None, OP.bitwise_and))
-    quant(1)
-    wait("v", b)
-    b = V(v.tensor_copy(T.pcf[:, 0:3], T.pca[:, 0:3]))
-    wait("v", b, k_i3)
-    V(v.tensor_scalar(T.pcq[:, 0:1], T.pcf[:, 1:2], 15.0, -8 * LIFT, OP.is_lt, OP.mult))
-    V(v.tensor_scalar(T.vals1[:, 0:64], T.i3[:, 0:64], T.pcf[:, 0:1], 0.5, OP.add, OP.mult))
-    quant(2)
 
-    kp, kh, kf, km = [None] * 4, [None] * 2, [None] * 4, [None] * 4
-
-    def down(c):
-        e = slice(128 * c, 128 * c + 128)
+    def down(c, bank, at=0, start=True, stop=True):
+        e, m = slice(128 * c, 128 * c + 128), slice(2 - at, 130 - at)
         wait("t", k_u0, kq[c])
-        kp[c] = X(t.matmul_mx(T.psp[:, 512 * c:512 * c + 128], T.xq[:, e], T.xs[:, e], T.uq0[:, 0:128], T.us0[:, 0:128], True, True))
+        return X(t.matmul_mx(T.psp[:, 512 * bank:512 * bank + 128], T.xq[:, e], T.xs[:, e], T.uq0[:, m], T.us0[:, m], start, stop))
 
-    def half(h):
+    def along(h, bank):
         e = slice(256 * h, 256 * h + 256)
-        wait("t", k_uc, k_us, kq[2 * h + 1])
-        kh[h] = X(t.matmul_mx(T.psf[:, 512 * h:512 * h + 256], T.uq[:, 0:128], T.us[:, 0:128], T.xq[:, e], T.xs[:, e], True, True))
+        wait("t", k_uc, k_us, kq[2 * h], kq[2 * h + 1])
+        return X(t.matmul_mx(T.psf[:, 512 * bank:512 * bank + 256], T.uq[:, 0:128], T.us[:, 0:128], T.xq[:, e], T.xs[:, e], True, True))
 
-    def block(c):
-        e = slice(128 * c, 128 * c + 128)
-        o = 512 * (2 + c % 2)
-        wait("t", k_uc, k_us, kq[c])
-        if c > 1:
-            wait("t", kf[c - 2])
-        k = X(t.matmul_mx(T.psf[:, o:o + 128], T.uq[:, 0:128], T.us[:, 0:128], T.xq[:, e], T.xs[:, e], True, True))
+    def scores(c, n, src, k):
         wait("s", k)
-        kf[c] = S(s.activation(T.sf[:, e], T.psf[:, o:o + 128], COPY))
-        wait("g", kf[c])
-        km[c] = done(g.affine_select(T.sm[:, e], T.sf[:, e], [[-1, 128]], OP.is_gt, BIG, 0, 1), "gc")
+        a = S(s.activation(T.sp[:, c:c + n], src, COPY))
+        b = S(s.activation(T.dl[:, c:c + n], src, ACT.Abs, bias=TINY, scale=STEP))
+        return a, b
 
-    cm = [T.cma, T.cmb, T.cmc, T.cmd]
-    jk = [0]
+    def bound(c, k):
+        wait("s", k, k_tri)
+        return S(s.activation(T.thr[:, 128 * c:128 * c + 128], T.tri[:, 0:128], IDENT, bias=T.sp[:, c:c + 1], scale=T.dl[:, c:c + 1]))
 
-    def total(buf, lo, hi, out, *tokens):
-        wait("s", *tokens)
-        n = hi - lo
-        r = S(s.activation(T.junk[:, jk[0]:jk[0] + n], buf[:, lo:hi], COPY, accum_out=out))
-        jk[0] = jk[0] + n if jk[0] + n + 700 <= 4096 else 0
-        return r
+    def row(d, n=1):
+        o = 512 * (d // 2) + 128 * (d % 2)
+        return T.psf[:, o:o + 128 * n]
+    strict, loose = (OP.is_lt, OP.is_le) if odd else (OP.is_gt, OP.is_ge)
 
     def cmp(out, src, col, op, weight=None):
         if weight is None:
             return V(v.tensor_scalar(out, src, col, None, op))
         return V(v.tensor_scalar(out, src, col, weight, op, OP.mult))
-    sp = [T.psp[:, 512 * c:512 * c + 1] for c in range(4)]
-    h0, h1, sm = T.psf[:, 0:256], T.psf[:, 512:768], T.sm
-    down(0)
-    block(0)
-    half(0)
-    down(1)
-    block(1)
-    down(2)
-    wait("v", kp[0], kh[0])
-    cmp(cm[0][:, 0:256], h0, sp[0], OP.is_gt)
-    quant(3)
-    half(1)
-    wait("v", kp[1])
-    cmp(cm[1][:, 0:128], T.psf[:, 0:128], sp[1], OP.is_ge)
-    k = cmp(cm[1][:, 128:256], T.psf[:, 128:256], sp[1], OP.is_gt)
-    e1 = total(cm[1], 0, 256, cm[1][:, 256:257], k)
-    wait("v", km[0])
-    k = cmp(cm[0][:, 256:384], sm[:, 0:128], sp[0], OP.is_equal)
-    e0 = total(cm[0], 0, 384, cm[0][:, 384:385], k)
-    block(2)
-    down(3)
-    wait("v", kp[2])
-    cmp(cm[2][:, 0:256], h0, sp[2], OP.is_ge)
-    wait("v", kh[1])
-    k = cmp(cm[2][:, 256:512], h1, sp[2], OP.is_gt)
-    e2 = total(cm[2], 0, 512, cm[2][:, 512:513], k)
-    k = cmp(cm[0][:, 385:641], h1, sp[0], OP.is_gt)
-    block(3)
-    total(cm[0], 384, 641, T.pl1[:, 0:1], k, e0)
-    cmp(cm[1][:, 257:513], h1, sp[1], OP.is_gt)
-    wait("v", km[1])
-    k = cmp(cm[1][:, 513:641], sm[:, 128:256], sp[1], OP.is_equal)
-    pl = total(cm[1], 256, 641, T.pl1[:, 1:2], k, e1)
-    wait("v", kp[3])
-    k = cmp(cm[3][:, 0:256], h0, sp[3], OP.is_ge)
-    e3 = total(cm[3], 0, 256, cm[3][:, 640:641], k)
-    cmp(cm[3][:, 256:384], T.psf[:, 512:640], sp[3], OP.is_ge)
-    cmp(cm[3][:, 384:512], T.psf[:, 640:768], sp[3], OP.is_gt)
-    wait("v", km[2])
-    a = cmp(cm[2][:, 513:641], sm[:, 256:384], sp[2], OP.is_equal)
-    wait("v", km[3])
-    b = cmp(cm[3][:, 512:640], sm[:, 384:512], sp[3], OP.is_equal)
-    V(v.memset(T.ti1[:, 0:32], 0.0))
-    wait("v", a, e2)
-    V(v.tensor_reduce(T.pl1[:, 2:3], cm[2][:, 512:641], AxisListType.X, OP.add))
-    wait("v", b, e3)
-    a = V(v.tensor_reduce(T.pl1[:, 3:4], cm[3][:, 256:641], AxisListType.X, OP.add))
-    wait("v", a, pl)
-    if odd:
-        k_pu = V(v.tensor_scalar(T.pu1[:, 0:4], T.pl1[:, 0:4], -1.0, 511.0, OP.mult, OP.add))
-    else:
-        k_pu = V(v.tensor_copy(T.pu1[:, 0:4], T.pl1[:, 0:4]))
 
-    def invert(n, ready, cols, width, vals, lo, scale, fill):
+    def add_up(out, buf, o, n, first):
+        return V(v.tensor_tensor_scan(out, buf[:, o:o + n], buf[:, o + n:o + 2 * n], first, OP.add, OP.add))
+
+    h0, h1 = B[0] // 2, B[2] // 2
+    sp = [T.sp[:, c:c + 1] for c in range(4)]
+    cm, c01 = T.cm, 2 * h0
+    kt, kl = {}, {}
+
+    def signs(c, i):
+        wait("s", kh0s)
+        return S(s.activation(T.sg[:, 256 * i:256 * i + 256], T.psf[:, 1024:1280], ACT.Sign, bias=sp[c], scale=-1.0))
+
+    def sum_signs(c, i, k):
+        wait("s", k)
+        kl[c] = S(s.activation(T.junk[:, 256 * i:256 * i + 256], T.sg[:, 256 * i:256 * i + 256], ACT.Relu, scale=1.0 if odd else -1.0,
+                               accum_out=T.ls[:, c:c + 1]))
+
+    def own_block(c, o):
+        wait("v", kt[c])
+        return V(v.tensor_tensor(cm[:, o:o + 128], row(c), T.thr[:, 128 * c:128 * c + 128], strict))
+
+    quant(B[0])
+    wait("v", k_gt)
+    k_go = V(v.tensor_scalar(T.goff[:, 0:2], T.gt[:, 0:2], 1.0 / 32, None, OP.mult))
+    quant(B[1])
+    down(B[0], 0, 2 * (B[0] % 2), True, False)
+    k = down(B[1], 0, 2 * (B[1] % 2), False, True)
+    ka, kd = scores(c01, 2, T.psp[:, 0:4:2], k)
+    kh0 = along(h0, h0)
+    kh0s = along(h0, 2)
+    for c in B[0:2]:
+        kt[c] = bound(c, kd)
+    quant(B[2])
+    k = down(B[2], 1)
+    ka2, kd = scores(B[2], 1, T.psp[:, 512:513], k)
+    kt[B[2]] = bound(B[2], kd)
+    k2 = signs(B[2], 0)
+    wait("v", ka, kh0)
+    cmp(cm[:, 0:128], row(B[1]), sp[B[0]], loose)
+    cmp(cm[:, 512:640], row(B[0]), sp[B[1]], strict)
+    quant(B[3])
+    kh1 = along(h1, h1)
+    k = down(B[3], 2)
+    ka3, kd = scores(B[3], 1, T.psp[:, 1024:1025], k)
+    sum_signs(B[2], 0, k2)
+    kt[B[3]] = bound(B[3], kd)
+    sum_signs(B[3], 1, signs(B[3], 1))
+    own_block(B[0], 128)
+    own_block(B[1], 640)
+    wait("v", kh1)
+    a = cmp(cm[:, 256:512], row(2 * h1, 2), sp[B[0]], loose)
+    b = cmp(cm[:, 768:1024], row(2 * h1, 2), sp[B[1]], loose)
+    wait("v", a, ka2)
+    add_up(T.cs[:, 256 * (B[0] % 2):256 * (B[0] % 2) + 256], cm, 0, 256, -256.0)
+    cmp(cm[:, 1024:1152], row(B[3]), sp[B[2]], loose)
+    wait("v", b)
+    b = add_up(T.cs[:, 256 * (B[1] % 2):256 * (B[1] % 2) + 256], cm, 512, 256, -256.0)
+    a = own_block(B[2], 1152)
+    wait("v", ka3)
+    cmp(cm[:, 1280:1408], row(B[2]), sp[B[3]], strict)
+    c = own_block(B[3], 1408)
+    wait("v", a, b)
+    a = add_up(T.cs[:, 512:640], cm, 1024, 128, 0.0)
+    shift = 0.0 if odd else 16.0
+    V(v.tensor_scalar(T.pu1[:, c01:c01 + 2], T.cs[:, 255:512:256], 256.0 + shift, None, OP.add))
+    wait("v", c)
+    c = add_up(T.cs[:, 640:768], cm, 1280, 128, 0.0)
+    wait("v", a, kl[B[2]])
+    V(v.tensor_scalar(T.pu1[:, B[2]:B[2] + 1], T.cs[:, 639:640], T.ls[:, B[2]:B[2] + 1], shift, OP.add, OP.add))
+    wait("v", c, kl[B[3]])
+    k_pu = V(v.tensor_scalar(T.pu1[:, B[3]:B[3] + 1], T.cs[:, 767:768], T.ls[:, B[3]:B[3] + 1], shift, OP.add, OP.add))
+
+    def invert(n, ready, cols, vals, lo, lift):
         W = lambda b: T[b + n]
-        wait("v", k_ch, *ready)
-        a = V(v.tensor_copy(W("win")[:, 0:width].indirect(W("pu")[:, 0:cols]), vals[:, 0:16 * cols]))
+        wait("v", *ready)
+        a = V(v.tensor_copy(W("win")[:, 0:528].indirect(W("pu")[:, 0:cols]), vals[:, 0:16 * cols]))
         wait("v", a)
-        a = V(v.tensor_tensor_scan(W("sc")[:, 0:128], T.ch[:, 0:128], W("win")[:, lo:lo + 128], 0.0, OP.add, OP.max))
+        V(v.transpose(W("tz")[:, 0:128], W("win")[:, lo:lo + 128]))
+        a = V(v.transpose(W("tz")[:, 128:288], W("win")[:, lo - 16:lo + 144]))
         wait("v", a)
-        a = V(v.tensor_tensor(W("qa")[0:64, 0:8], W("sc")[0:64, 15:128:16], W("sc")[64:128, 15:128:16], OP.add))
+        a = V(v.tensor_tensor(W("qa")[:, 0:9], W("tz")[:, 0:288:32], W("tz")[:, 16:288:32], OP.add))
         wait("v", a)
-        a = V(v.tensor_tensor(W("ti")[0:32, 0:8], W("qa")[0:32, 0:8], W("qa")[32:64, 0:8], OP.add))
-        wait("v", a)
-        a = V(v.transpose(W("to")[0:32, 0:32], W("ti")[0:32, 0:32]))
-        wait("v", a)
-        V(v.tensor_tensor(W("tw")[0:32, 0:16], W("to")[0:32, 0:16], W("to")[0:32, 16:32], OP.add))
-        a = V(v.tensor_tensor(W("tw")[0:32, 16:32], W("to")[0:32, 0:16], W("to")[0:32, 16:32], OP.add))
-        wait("v", a)
-        a = V(v.transpose(W("tb")[0:32, 0:32], W("tw")[0:32, 0:32]))
-        fill()
+        a = V(v.tensor_tensor(W("qb")[0:64, 0:9], W("qa")[0:64, 0:9], W("qa")[64:128, 0:9], OP.add))
         wait("v", a)
         for h in range(4):
-            a = V(v.tensor_scalar(W("lst")[32 * h:32 * h + 32, 0:8], W("tb")[0:32, 0:8], T.pcq[0:32, 0:1], scale, OP.add, OP.mult))
-        return a
+            a = V(v.tensor_tensor(W("qc")[32 * h:32 * h + 32, 0:9], W("qb")[0:32, 0:9], W("qb")[32:64, 0:9], OP.add))
+        wait("v", a, k_go)
+        return a, V(v.tensor_scalar(W("lst")[:, 0:16], W("qc")[:, 0:9].indirect(T.goff[:, 0:1]), lift, None, OP.add))
 
     def pick(dc, ds, sc, ss, off, ready_c, ready_s):
         wait("v", *ready_c)
-        a = V(v.tensor_copy(dc.bitcast(dt.uint32), sc.bitcast(dt.uint32).indirect(off[:, 0:8])))
+        a = V(v.tensor_copy(dc.bitcast(dt.uint32), sc.bitcast(dt.uint32).indirect(off)))
         wait("s", *ready_s)
-        b = S(s.activation(ds, ss.indirect(off[:, 0:8]), COPY))
+        b = S(s.activation(ds, ss.indirect(off), COPY))
         return a, b
 
-    def send(out_c, in_c, out_s, in_s, a, b, dst, sem_c, sem_s):
+    def remote(o, i, dst, sem):
         rid, pid = topo.addr(dst, core)
-        m = topo.mask(core, dst)
         n = len(topo.engines(core, dst))
-        for o, i, k, sem in ((out_c.bitcast(dt.uint8), in_c.bitcast(dt.uint8), a, sem_c), (out_s, in_s, b, sem_s)):
-            wait("g", k)
-            g.remote_dma(o, i, T.sem[sem], T.sem["sent"], pid, rid, m)
-            count["sent"] = count.get("sent", 0) + n
-        return (sem_c, n), (sem_s, n)
+        g.remote_dma(o, i, T.sem[sem], T.sem["sent"], pid, rid, topo.mask(core, dst))
+        count["sent"] = count.get("sent", 0) + n
+        return (sem, n)
 
-    def number_constants():
-        V(v.tensor_scalar(T.gm[:, 0:8], T.i6[:, 0:8], T.pcf[:, 0:1], None, OP.is_equal))
-        V(v.tensor_scalar(T.pct[:, 0:1], T.pt[:, 0:1], 128.0 * P + 512.0 * rank / GID, None, OP.add))
-    wait("v", k_i6, k_pt)
-    k_l1 = invert("1", (k_pu,), 4, 512, T.vals1, 384 if odd else 0, 2.0, number_constants)
-    a1, b1 = pick(T.c1[:, 0:K], T.s1[:, 0:K], T.xq[:, 0:512], T.xs[:, 0:512], T.lst1, (k_l1,), (k_l1,))
+    def send(out_c, in_c, out_s, in_s, a, b, dst, sem_c, sem_s):
+        wait("g", a)
+        kc = remote(out_c.bitcast(dt.uint8), in_c.bitcast(dt.uint8), dst, sem_c)
+        wait("g", b)
+        return kc, remote(out_s, in_s, dst, sem_s)
+
+    m0 = SLOT * rank
+    k_q1, k_l1 = invert("1", (k_pu,), 4, T.vals1, lo1, 256.0)
+    wait("s", k_q1, k_go)
+    S(s.activation(T.msg[:, m0 + 5:m0 + 21], T.qc1[:, 0:9].indirect(T.goff[:, 0:1]), IDENT, bias=256.0))
+    a1, b1 = pick(T.c1[:, 0:K], T.s1[:, 0:K], T.xq[:, 0:512], T.xs[:, 0:512], T.lst1[:, 2:10], (k_l1,), (k_l1,))
     mate = T.cores[rank ^ 1]
     in1c, in1s = send(T.c1[:, K:2 * K], T.c1[:, 0:K], T.s1[:, K:2 * K], T.s1[:, 0:K], a1, b1, mate, "h1c", "h1s")
 
-    m0 = 8 * rank
     wait("t", a1, b1)
     kaf = X(t.matmul_mx(T.psf[:, 0:128], T.uq[:, 0:128], T.us[:, 0:128], T.c1[:, 0:128], T.s1[:, 0:128], True, True))
-    kap = X(t.matmul_mx(T.psp[:, 0:128], T.c1[:, 0:128], T.s1[:, 0:128], T.uq0[:, 0:128], T.us0[:, 0:128], True, True))
-    a = V(v.tensor_scalar(T.o1f[:, 0:8], T.lst1[:, 0:8], 1.0 / GID, T.pct[:, 0:1], OP.mult, OP.add))
-    wait("v", a)
-    a = V(v.tensor_tensor(T.o1g[:, 0:8], T.o1f[:, 0:8], T.gm[:, 0:8], OP.mult))
+    kap = X(t.matmul_mx(T.psp[:, 0:128], T.c1[:, 0:128], T.s1[:, 0:128], T.uq0[:, 2:130], T.us0[:, 2:130], True, True))
+    V(v.tensor_scalar(T.ita[:, 0:128], T.it[:, 0:128], 15, None, OP.bitwise_and))
     wait("s", kap)
     k_m4 = S(s.activation(T.msg[:, m0 + 4:m0 + 5], T.psp[:, 0:1], COPY))
-    wait("v", a, kaf)
+    wait("v", kaf)
     a2 = V(v.transpose(T.at[:, 0:128], T.psf[:, 0:128]))
-    V(v.tensor_reduce(T.msg[:, m0 + 5:m0 + 6], T.o1g[:, 0:8], AxisListType.X, OP.add))
     wait("v", a2)
     k_msg = V(v.tensor_copy(T.msg[:, m0:m0 + 4], T.at[:, 0:128:32]))
     wait("g", k_msg, k_m4)
     ids, m = [], topo.mask(core, mate)
-    for other in (rank ^ 2, rank ^ 3, rank ^ 1):
+    for other in (rank ^ 2, rank ^ 3):
         dst = T.cores[other]
         rid, pid = topo.addr(dst, core)
         ids.append(DstId(rid=rid, pnc=pid))
         m &= topo.mask(core, dst)
     n = bin(m).count("1")
     view = T.msg[:, m0:m0 + 6]
-    g.remote_dma_fused([RemoteDMATransfer(dst_ids=ids, dma_engine_mask=m, remote_sem=T.sem["hm"], srcs=[view], dsts=[view] * 3)],
+    g.remote_dma_fused([RemoteDMATransfer(dst_ids=ids, dma_engine_mask=m, remote_sem=T.sem["hm"], srcs=[view], dsts=[view] * 2)],
                        local_sem=T.sem["sent"])
-    in_msg = ("hm", 3 * n)
+    in_msg = ("hm", 2 * n)
     count["sent"] += n
+    view = T.msg[:, m0 + 4:m0 + 6]
+    in_mate = remote(view, view, mate, "hp")
 
     a = V(v.tensor_scalar(T.nb0[:, 0:128], T.ita[:, 0:128], 0.0, 2 * BIG, OP.is_equal, OP.mult))
     b = V(v.memset(T.hs[:, 0:128], 0.0))
     k = V(v.tensor_scalar(T.pcq[:, 1:2], T.pcf[:, 1:2], 128.0, None, OP.add))
     wait("v", a)
     a = V(v.tensor_scalar(T.nb[:, 0:128], T.nb0[:, 0:128], -BIG, None, OP.add))
-    wait("v", b, k)
+    wait("v", b, k, k_i6)
     k_hs = V(v.tensor_scalar(T.hs[:, 0:128:16], T.i6[:, 0:8], T.pcq[:, 1:2], 1.0 / 128, OP.add, OP.mult))
     wait("v", a)
     k_am = V(v.tensor_tensor(T.am[:, 0:128], T.nb[:, 0:128], T.psf[:, 0:128], OP.min))
     wait("v", dw)
     k_w = V(v.quantize_mx(T.wq[:, 0:256], T.ws[:, 0:256], T.wb[:, 0:1024]))
-    wait("v", k_i5, k_i7)
+    wait("v", k_i5, k_i4, k_pt)
     V(v.tensor_copy(T.eoff[:, 0:16], T.i5[:, 0:16]))
-    V(v.tensor_scalar(T.hm[:, 0:32], T.i7[:, 0:32], T.pcf[:, 2:3], None, OP.is_equal))
-    k_co = V(v.tensor_scalar(T.pct[:, 1:2], T.pt[:, 0:1], -2.0, 127.0, OP.mult, OP.add))
-    V(v.memset(T.win2[:, 0:384], 0.0))
-    V(v.memset(T.ti2[:, 0:32], 0.0))
+    k = V(v.tensor_scalar(T.pcq[:, 0:1], T.pcf[:, 0:1], 2.0, None, OP.mult))
+    V(v.tensor_scalar(T.pct[:, 0:1], T.pt[:, 0:1], -2.0, 127.0, OP.mult, OP.add))
+    V(v.memset(T.win2[:, 0:160], 0.0))
+    V(v.memset(T.cp[:, 0:64], 0.0))
+    V(v.memset(T.idr[:, 64:256], 0.0))
+    wait("v", k)
+    k_co = V(v.tensor_scalar(T.vals2[:, 0:32], T.i4[:, 0:32], T.pcq[:, 0:1], None, OP.add))
 
-    word = lambda rk, w: T.msg[:, 8 * rk + w:8 * rk + w + 1]
-    E, O = T.msg[:, 4:32:16], T.msg[:, 12:32:16]
-    ps, sel, nsel = [[T[b][:, j:j + 1] for j in range(2)] for b in ("ps", "sel", "nsel")]
     fr = (T.psf[:, 512:640], T.psf[:, 0:128]) if odd else (T.psf[:, 0:128], T.psf[:, 512:640])
-    wait("s", in_msg, k_co)
-    ky = S(s.activation(T.yx[:, 0:256], T.msg[:, 16 * Q:16 * Q + 16].indirect(T.eoff[:, 0:16]), COPY))
     wait("t", in1c, in1s)
     kb = X(t.matmul_mx(T.psf[:, 512:640], T.uq[:, 0:128], T.us[:, 0:128], T.c1[:, 128:256], T.s1[:, 128:256], True, True))
     wait("v", kb, k_am)
     a = V(v.tensor_tensor(T.bc[:, 0:128], T.am[:, 0:128], T.psf[:, 512:640], OP.is_gt if odd else OP.is_ge))
-    wait("v", in_msg, k_m4)
-    V(v.tensor_tensor(T.ps[:, 0:2], E, O, OP.max))
-    V(v.tensor_tensor(T.sel[:, 0:2], O, E, OP.is_gt))
     wait("v", a, k_hs)
     a = V(v.tensor_tensor_scan(T.bs[:, 0:128], T.hs[:, 0:128], T.bc[:, 0:128], 0.0, OP.max, OP.subtract))
-    V(v.tensor_tensor(T.nsel[:, 0:2], E, O, OP.is_ge))
-    k_vd = V(v.tensor_tensor(T.vd[:, 0:2], T.msg[:, 13:32:16], T.msg[:, 5:32:16], OP.subtract))
     wait("v", a)
     k_o2 = V(v.tensor_scalar(T.off2[:, 0:8], T.bs[:, 15:128:16], 128.0, None, OP.mult))
-    wait("v", k_vd)
-    cmp(T.ba[:, 0:128], fr[1], ps[P], OP.is_gt, nsel[P])
-    a2, b2 = pick(T.c2[:, own], T.s2[:, own], T.c1[:, 0:256], T.s1[:, 0:256], T.off2, (k_o2, in1c), (k_o2, in1s))
+    a2, b2 = pick(T.c2[:, own], T.s2[:, own], T.c1[:, 0:256], T.s1[:, 0:256], T.off2[:, 0:8], (k_o2, in1c), (k_o2, in1s))
     in2c, in2s = send(T.c2[:, own], T.c2[:, own], T.s2[:, own], T.s2[:, own], a2, b2, T.cores[rank ^ 2], "h2c", "h2s")
 
     def products(side, bank, *ready):
@@ -364,61 +355,67 @@ def rank_program(g, core, T, topo):
     ko = products(own, T.psf, a2, b2)
     kr = products(arr, T.psp, in2c, in2s)
 
-    wait("s", k_vd)
-    for j, buf in ((P, T.ba), (Q, T.bb)):
-        kc = S(s.activation(buf[:, 256:257], sel[j], IDENT, bias=T.pt[:, 0:1], scale=T.pct[:, 1:2]))
-    a = cmp(T.ba[:, 128:256], fr[0], ps[P], OP.is_ge, sel[P])
-    ka = total(T.ba, 0, 257, T.ba[:, 257:258], a, kc)
+    word = lambda rk, w: T.msg[:, SLOT * rk + w:SLOT * rk + w + 1]
+    E, O = T.msg[:, 4:4 * SLOT:2 * SLOT], T.msg[:, SLOT + 4:4 * SLOT:2 * SLOT]
+    ps, sel, nsel = [[T[b][:, j:j + 1] for j in range(2)] for b in ("ps", "sel", "nsel")]
+    wait("s", in_msg, k_co)
+    ky = S(s.activation(T.yx[:, 0:256], T.msg[:, 2 * SLOT * Q:2 * SLOT * (Q + 1)].indirect(T.eoff[:, 0:16]), COPY))
+    wait("v", in_msg, in_mate, k_m4)
+    a = V(v.tensor_tensor(T.ps[:, 0:2], E, O, OP.max))
+    k_sel = V(v.tensor_tensor(T.sel[:, 0:2], O, E, OP.is_gt))
+    b = V(v.tensor_tensor(T.nsel[:, 0:2], E, O, OP.is_ge))
+    k_vd = V(v.tensor_tensor(T.vd[:, 0:2], T.msg[:, SLOT + 5:4 * SLOT:2 * SLOT], T.msg[:, 5:4 * SLOT:2 * SLOT], OP.subtract))
+    wait("s", k_sel)
     for j in range(2):
-        kcp = S(s.activation(T.cp[:, j:j + 1], T.vd[:, j:j + 1], IDENT, bias=word(2 * j, 5), scale=sel[j]))
+        kc = S(s.activation(T.kc[:, j:j + 1], sel[j], IDENT, bias=T.pt[:, 1:2], scale=T.pct[:, 0:1]))
+    wait("s", k_vd)
+    for j in range(2):
+        S(s.activation(T.cp[:, 32 * j:32 * j + 1], sel[j], IDENT, bias=2.0 * j))
+        kcp = S(s.activation(T.cp[:, 32 * j + 1:32 * j + 2], T.vd[:, j:j + 1], IDENT, bias=word(2 * j, 5), scale=sel[j]))
+    wait("v", a)
+    for f in range(2):
+        cmp(T.bb[:, 128 * f:128 * f + 128], fr[f], ps[Q], OP.is_ge if P < Q else OP.is_gt)
+    wait("v", b)
+    cmp(T.ba[:, 0:128], fr[1], ps[P], OP.is_gt, nsel[P])
+    cmp(T.ba[:, 128:256], fr[0], ps[P], OP.is_ge, sel[P])
     wait("v", ky)
     kt = V(v.transpose(T.fs[:, 0:256], T.yx[:, 0:256]))
-    for f in range(2):
-        k = cmp(T.bb[:, 128 * f:128 * f + 128], fr[f], ps[Q], OP.is_ge if P < Q else OP.is_gt)
-    wait("s", kcp)
+    wait("v", kcp)
     for j in range(2):
-        kz = S(s.activation(T.zx[:, 32 * j:32 * j + 32], T.hm[:, 0:32], COPY, scale=T.cp[:, j:j + 1]))
-    kb = total(T.bb, 0, 257, T.bb[:, 257:258], k)
+        kz = V(v.transpose(T.idr[:, j:64:2], T.cp[:, 32 * j:32 * j + 32]))
     wait("v", kt)
-    k = cmp(T.ba[:, 258:514], T.fs[:, 0:256], ps[P], OP.is_ge if Q < P else OP.is_gt)
-    ka = total(T.ba, 257, 514, T.pl2[:, P:P + 1], k, ka)
-    k = cmp(T.bb[:, 258:386], T.fs[:, 128:256], ps[Q], OP.is_gt, nsel[Q])
-    kb = total(T.bb, 257, 386, T.bb[:, 514:515], k, kb)
-    k = cmp(T.bb[:, 386:514], T.fs[:, 0:128], ps[Q], OP.is_ge, sel[Q])
-    wait("v", kz)
-    a = V(v.transpose(T.zt[:, 0:64], T.zx[:, 0:64]))
+    a = cmp(T.ba[:, 256:512], T.fs[:, 0:256], ps[P], OP.is_ge if Q < P else OP.is_gt)
+    cmp(T.bb[:, 256:384], T.fs[:, 128:256], ps[Q], OP.is_gt, nsel[Q])
+    b = cmp(T.bb[:, 384:512], T.fs[:, 0:128], ps[Q], OP.is_ge, sel[Q])
+    wait("v", a, kc)
+    add_up(T.bt[:, 256 * P:256 * P + 256], T.ba, 0, 256, T.kc[:, P:P + 1])
+    wait("v", b)
+    a = add_up(T.bt[:, 256 * Q:256 * Q + 256], T.bb, 0, 256, T.kc[:, Q:Q + 1])
     wait("v", a)
-    for j in range(2):
-        V(v.tensor_tensor(T.vals2[:, 16 * j:16 * j + 16], T.zt[:, 32 * j:32 * j + 16], T.zt[:, 32 * j + 16:32 * j + 32], OP.add))
-    wait("v", k, kb)
-    a = V(v.tensor_reduce(T.pl2[:, Q:Q + 1], T.bb[:, 386:515], AxisListType.X, OP.add))
-    wait("v", a, ka)
-    kv = V(v.tensor_copy(T.pu2[:, 0:2], T.pl2[:, 0:2]))
+    kv = V(v.tensor_scalar(T.pu2[:, 0:2], T.bt[:, 255:512:256], 144.0, None, OP.add))
 
     yw = (T.yw0, T.yw1)
-    for side, bank, kk in ((own, T.psf, ko), (arr, T.psp, kr)):
-        for o in range(2):
-            wait("s", kk[o])
-            kyw = S(s.activation(yw[o][:, side], bank[:, 512 * (o + 2):512 * (o + 2) + 128], COPY))
+    for o in range(2):
+        wait("s", ko[o])
+        S(s.activation(yw[o][:, P:256:2], T.psf[:, 512 * (o + 2):512 * (o + 2) + 128], COPY))
+    wait("s", kz)
+    for a in range(1, 4):
+        S(s.activation(T.idr[0:2, 64 * a:64 * a + 64], T.idr[32 * a:32 * a + 2, 0:64], COPY))
+    for o in range(2):
+        wait("s", kr[o])
+        kyw = S(s.activation(yw[o][:, Q:256:2], T.psp[:, 512 * (o + 2):512 * (o + 2) + 128], COPY))
 
-    def numbers():
-        V(v.tensor_scalar(T.idn[0:32, 0:16], T.tw2[0:32, 0:16], float(GID), None, OP.mult))
-    k_l2 = invert("2", (kv,), 2, 384, T.vals2, 0, 1.0, numbers)
+    k_q2, k_l2 = invert("2", (kv,), 2, T.vals2, 16, 128.0)
 
+    off = T.lst2[:, 2:10]
     wait("v", k_l2, kyw)
-    ky0 = V(v.tensor_copy(T.yb0[:, 0:128], T.yw0[:, 0:256].indirect(T.lst2[:, 0:8])))
+    ky0 = V(v.tensor_copy(T.yb[:, 0:128], T.yw0[:, 0:256].indirect(off)))
+    ki = V(v.tensor_copy(T.idb[:, 0:128], T.idr[:, 0:256].indirect(off)))
     wait("s", k_l2, kyw)
-    ky1 = S(s.activation(T.yb1[:, 0:128], T.yw1[:, 0:256].indirect(T.lst2[:, 0:8]), COPY))
-    wait("s", ky1)
-    d1 = done(s.dma_start(T.y[:, 128:256], T.yb1[:, 0:128]), "dy1", 16)
-    wait("y", ky0)
-    d0 = done(y.dma_start(T.y[:, 0:128], T.yb0[:, 0:128]), "dy0", 16)
-    V(v.tensor_scalar(T.idi[0:32, 0:16], T.idn[0:32, 0:16], 9, 3, OP.arith_shift_right, OP.bitwise_and))
-    a = V(v.tensor_scalar(T.idi[0:32, 16:32], T.idn[0:32, 0:16], 511, None, OP.bitwise_and))
-    wait("v", a)
-    kid = V(v.tensor_copy(T.idf[0:32, 0:32], T.idi[0:32, 0:32]))
-    wait("y", kid)
-    for row in range(2):
-        d2 = done(y.dma_start(T["id"][row:row + 1, 0:128], T.idf[0:8, 16 * row:16 * row + 16]), "did", 16)
-    wait("g", ("sent", count["sent"]), in1c, in1s, in2c, in2s, in_msg, du, *dx, dw,
-         ("gc", count["gc"]), ("v", count["v"]), ("s", count["s"]), ("t", count["t"]), d0, d1, d2)
+    ky1 = S(s.activation(T.yb[:, 128:256], T.yw1[:, 0:256].indirect(off), COPY))
+    wait("y", ky0, ky1)
+    d0 = done(y.dma_start(T.y[:, 0:256], T.yb[:, 0:256]), "dy", 16)
+    wait("s", ki)
+    d2 = done(s.dma_start(T["id"][0:2, 0:128], T.idb[0:2, 0:128]), "did", 16)
+    wait("g", ("sent", count["sent"]), in1c, in1s, in2c, in2s, in_msg, in_mate, du, *dx.values(), dw,
+         ("gc", count["gc"]), ("v", count["v"]), ("s", count["s"]), ("t", count["t"]), d0, d2)

@@ -24,27 +24,29 @@ SCRATCH = {
     "yb": ("sbuf", [128, 256], "float32"),
     "psf": ("psum", [128, 2048], "float32"),
     "psp": ("psum", [128, 2048], "float32"),
-    "ip": ("sbuf", [128, 2], "int32"), "pt": ("sbuf", [128, 2], "float32"),
+    "ip": ("sbuf", [128, 2], "int32"), "pt": ("sbuf", [128, 4], "float32"),
     "it": ("sbuf", [128, 128], "int32"), "ita": ("sbuf", [128, 128], "int32"), "tri": ("sbuf", [128, 128], "float32"),
-    "nb0": ("sbuf", [128, 128], "float32"), "nb": ("sbuf", [128, 128], "float32"),
+    "nb": ("sbuf", [128, 128], "float32"),
     "i3": ("sbuf", [128, 64], "float32"), "vals1": ("sbuf", [128, 64], "bfloat16"),
     "i4": ("sbuf", [128, 32], "float32"), "vals2": ("sbuf", [128, 32], "bfloat16"),
     "i5": ("sbuf", [128, 16], "int32"), "eoff": ("sbuf", [128, 16], "uint16"),
-    "i6": ("sbuf", [128, 8], "float32"), "hs": ("sbuf", [128, 128], "float32"),
+    "i6": ("sbuf", [128, 8], "float32"), "hs": ("sbuf", [128, 128], "bfloat16"),
     "gr": ("sbuf", [128, 32], "float32"), "gt": ("sbuf", [128, 32], "float32"), "goff": ("sbuf", [128, 2], "uint16"),
     "pca": ("sbuf", [128, 2], "int32"), "pcf": ("sbuf", [128, 2], "float32"), "pcq": ("sbuf", [128, 2], "float32"),
-    "pct": ("sbuf", [128, 2], "float32"),
     "sp": ("sbuf", [128, 4], "float32"), "dl": ("sbuf", [128, 4], "float32"), "thr": ("sbuf", [128, 512], "float32"),
     "cm": ("sbuf", [128, 1536], "bfloat16"), "cs": ("sbuf", [128, 768], "bfloat16"),
-    "sg": ("sbuf", [128, 512], "bfloat16"), "junk": ("sbuf", [128, 512], "bfloat16"), "ls": ("sbuf", [128, 4], "float32"),
+    "sg": ("sbuf", [128, 640], "bfloat16"), "junk": ("sbuf", [128, 640], "bfloat16"), "ls": ("sbuf", [128, 4], "float32"),
     "msg": ("sbuf", [128, 4 * SLOT], "float32"), "at": ("sbuf", [128, 128], "float32"),
+    "pum": ("sbuf", [128, 8], "uint16"), "winm": ("sbuf", [128, 528], "bfloat16"), "tzm": ("sbuf", [128, 128], "bfloat16"),
+    "qam": ("sbuf", [128, 4], "float32"), "qbm": ("sbuf", [64, 4], "float32"),
     "am": ("sbuf", [128, 128], "float32"),
-    "bc": ("sbuf", [128, 128], "float32"), "bs": ("sbuf", [128, 128], "float32"),
+    "bc": ("sbuf", [128, 128], "bfloat16"), "bs": ("sbuf", [128, 128], "bfloat16"),
     "off2": ("sbuf", [128, 8], "uint16"),
     "yx": ("sbuf", [128, 256], "float32"), "fs": ("sbuf", [128, 256], "float32"),
     "ps": ("sbuf", [128, 2], "float32"), "sel": ("sbuf", [128, 2], "float32"), "nsel": ("sbuf", [128, 2], "float32"),
     "vd": ("sbuf", [128, 2], "float32"), "kc": ("sbuf", [128, 2], "float32"),
-    "ba": ("sbuf", [128, 512], "bfloat16"), "bb": ("sbuf", [128, 512], "bfloat16"), "bt": ("sbuf", [128, 512], "bfloat16"),
+    "ba": ("sbuf", [128, 512], "bfloat16"), "bb": ("sbuf", [128, 256], "bfloat16"), "bt": ("sbuf", [128, 384], "bfloat16"),
+    "sq": ("sbuf", [128, 512], "bfloat16"), "lq": ("sbuf", [128, 1], "float32"),
     "cp": ("sbuf", [128, 64], "float32"), "idr": ("sbuf", [128, 256], "float32"), "idb": ("sbuf", [128, 128], "float32"),
 }
 for _n in ("1", "2"):
@@ -91,6 +93,7 @@ def rank_program(g, core, T, topo):
     B = [0, 1, 2, 3] if odd else [3, 2, 1, 0]
     du = done(s.dma_start(T.ur[:, 8:16], T.u[:, 0:8]), "du", 16)
     dx = {d: done(y.dma_start(T.xb[:, 512 * d:512 * d + 512], T.x[:, 512 * d:512 * d + 512]), "dx%d" % d, 16) for d in B}
+    wait("y", dx[B[3]])
     dw = done(y.dma_start(T.wb[:, 0:1024], T.w[:, 0:1024]), "dw", 16)
 
     def iota(buf, pattern, base, cm, flt=True):
@@ -103,39 +106,49 @@ def rank_program(g, core, T, topo):
     wait("g", iota(T.gr[:, 0:32], [[0, 32]], 0, 1))
     iota(T.gr[:, 2:10], [[32, 4], [160, 2]], 0, 0)
     k_gr = iota(T.gr[:, 18:26], [[32, 4], [-128, 2]], 128, 0)
-    k_i6 = iota(T.i6[:, 0:8], [[16, 8]], 0, 0)
-    k_pt = iota(T.pt[:, 0:2], [[-128, 2]], 0, 1)
-    k_i5 = iota(T.i5[:, 0:16], [[SLOT, 2], [1, 4], [0, 2]], 0, 0, False)
     k_i4 = iota(T.i4[:, 0:32], [[1, 2], [2, 16]], -128, 0)
+    iota(T.i6[:, 0:8], [[16, 8]], 0, 0)
+    iota(T.pt[:, 0:1], [[0, 1]], -128, 1)
+    iota(T.pt[:, 1:2], [[0, 1]], 127, -2)
+    iota(T.pt[:, 2:3], [[0, 1]], 0, 256)
+    iota(T.i5[:, 0:16], [[SLOT, 2], [1, 4], [0, 2]], 0, 0, False)
+    lo1, lom = (384, 16) if odd else (16, 384)
+    for buf, a, n in ((T.hs, 0, 128), (T.winm, lom, 128), (T.win2, 0, 160), (T.cp, 0, 64), (T.idr, 64, 192)):
+        k_zero = iota(buf[:, a:a + n], [[0, n]], 0, 0)
 
     V(v.memset(T.ur[:, 0:8], 0.0))
     k_ur = V(v.memset(T.ur[:, 16:520], 0.0))
     k_zo = V(v.memset(T.zoff[:, 0:8], 2))
-    lo1 = 384 if odd else 16
     V(v.memset(T.win1[:, lo1 - 16:lo1 + 144], 0.0))
     wait("v", k_it)
     if odd:
         k_tri = V(v.tensor_scalar(T.tri[:, 0:128], T.it[:, 0:128], 128.0, None, OP.is_gt))
     else:
         k_tri = V(v.tensor_scalar(T.tri[:, 0:128], T.it[:, 0:128], 128.0, -1.0, OP.is_lt, OP.mult))
+    V(v.tensor_scalar(T.ita[:, 0:128], T.it[:, 0:128], 15, None, OP.bitwise_and))
     wait("v", k_ip)
     V(v.tensor_scalar(T.pca[:, 0:1], T.ip[:, 0:1], 112, None, OP.bitwise_and))
     k = V(v.tensor_scalar(T.pca[:, 1:2], T.ip[:, 0:1], 15, None, OP.bitwise_and))
     wait("v", k)
     k_pc = V(v.tensor_copy(T.pcf[:, 0:2], T.pca[:, 0:2]))
+    V(v.tensor_scalar(T.nb[:, 0:128], T.ita[:, 0:128], 0.0, -BIG, OP.not_equal, OP.mult))
 
     wait("v", du, k_ur)
     k_u0 = V(v.quantize_mx(T.uq0[:, 0:130], T.us0[:, 0:130], T.ur[:, 0:520]))
-    wait("v", k_i3, k_pc)
-    V(v.tensor_scalar(T.vals1[:, 0:64], T.i3[:, 0:64], T.pcf[:, 0:1], None, OP.add))
     wait("v", k_u0, k_zo)
     k_uc = V(v.tensor_copy(T.uq[:, 0:128].bitcast(dt.uint32), T.uq0[:, 0:130].bitcast(dt.uint32).indirect(T.zoff[:, 0:8])))
     wait("s", k_u0)
     k_us = S(s.activation(T.us[:, 0:128], T.us0[:, 0:130].indirect(T.zoff[:, 0:8]), COPY))
+    wait("s", k_i3, k_pc)
+    k_v1 = S(s.activation(T.vals1[:, 0:64], T.i3[:, 0:64], IDENT, bias=T.pcf[:, 0:1]))
+    S(s.activation(T.pcq[:, 0:1], T.pcf[:, 1:2], IDENT, bias=128.0))
+    k = S(s.activation(T.pcq[:, 1:2], T.pcf[:, 0:1], COPY, scale=2.0))
+    wait("s", k, k_i4)
+    S(s.activation(T.vals2[:, 0:32], T.i4[:, 0:32], IDENT, bias=T.pcq[:, 1:2]))
     wait("v", k_gr)
     k_gt = V(v.transpose(T.gt[:, 0:32], T.gr[:, 0:32]))
 
-    kq = {}
+    kq, kr, kt, kl = {}, {}, {}, {}
 
     def quant(d):
         e = slice(128 * d, 128 * d + 128)
@@ -147,10 +160,10 @@ def rank_program(g, core, T, topo):
         wait("t", k_u0, kq[c])
         return X(t.matmul_mx(T.psp[:, 512 * bank:512 * bank + 128], T.xq[:, e], T.xs[:, e], T.uq0[:, m], T.us0[:, m], start, stop))
 
-    def along(h, bank):
-        e = slice(256 * h, 256 * h + 256)
-        wait("t", k_uc, k_us, kq[2 * h], kq[2 * h + 1])
-        return X(t.matmul_mx(T.psf[:, 512 * bank:512 * bank + 256], T.uq[:, 0:128], T.us[:, 0:128], T.xq[:, e], T.xs[:, e], True, True))
+    def along(out, d, n):
+        e = slice(128 * d, 128 * (d + n))
+        wait("t", k_uc, k_us, *[kq[c] for c in range(d, d + n)])
+        return X(t.matmul_mx(out, T.uq[:, 0:128], T.us[:, 0:128], T.xq[:, e], T.xs[:, e], True, True))
 
     def scores(c, n, src, k):
         wait("s", k)
@@ -160,94 +173,98 @@ def rank_program(g, core, T, topo):
 
     def bound(c, k):
         wait("s", k, k_tri)
-        return S(s.activation(T.thr[:, 128 * c:128 * c + 128], T.tri[:, 0:128], IDENT, bias=T.sp[:, c:c + 1], scale=T.dl[:, c:c + 1]))
+        kt[c] = S(s.activation(T.thr[:, 128 * c:128 * c + 128], T.tri[:, 0:128], IDENT, bias=T.sp[:, c:c + 1], scale=T.dl[:, c:c + 1]))
 
-    def row(d, n=1):
-        o = 512 * (d // 2) + 128 * (d % 2)
-        return T.psf[:, o:o + 128 * n]
     strict, loose = (OP.is_lt, OP.is_le) if odd else (OP.is_gt, OP.is_ge)
+    row = [T.psf[:, 512 * d:512 * d + 128] for d in range(4)]
+    sp = [T.sp[:, c:c + 1] for c in range(4)]
+    cm = T.cm
 
     def cmp(out, src, col, op, weight=None):
         if weight is None:
             return V(v.tensor_scalar(out, src, col, None, op))
         return V(v.tensor_scalar(out, src, col, weight, op, OP.mult))
 
+    def cell(i, j, o):
+        c, d = B[i], B[j]
+        wait("v", kr[d])
+        if i == j:
+            wait("v", kt[c])
+            return V(v.tensor_tensor(cm[:, o:o + 128], row[d], T.thr[:, 128 * c:128 * c + 128], strict))
+        return cmp(cm[:, o:o + 128], row[d], sp[c], loose if i < j else strict)
+
     def add_up(out, buf, o, n, first):
         return V(v.tensor_tensor_scan(out, buf[:, o:o + n], buf[:, o + n:o + 2 * n], first, OP.add, OP.add))
 
-    h0, h1 = B[0] // 2, B[2] // 2
-    sp = [T.sp[:, c:c + 1] for c in range(4)]
-    cm, c01 = T.cm, 2 * h0
-    kt, kl = {}, {}
+    def signs(i, o):
+        wait("s", krs)
+        return S(s.activation(T.sg[:, o:o + 256], T.psp[:, 1536:1792], ACT.Sign, bias=sp[B[i]], scale=-1.0))
 
-    def signs(c, i):
-        wait("s", kh0s)
-        return S(s.activation(T.sg[:, 256 * i:256 * i + 256], T.psf[:, 1024:1280], ACT.Sign, bias=sp[c], scale=-1.0))
-
-    def sum_signs(c, i, k):
+    def sum_signs(i, o, k):
         wait("s", k)
-        kl[c] = S(s.activation(T.junk[:, 256 * i:256 * i + 256], T.sg[:, 256 * i:256 * i + 256], ACT.Relu, scale=1.0 if odd else -1.0,
-                               accum_out=T.ls[:, c:c + 1]))
+        kl[i] = S(s.activation(T.junk[:, o:o + 256], T.sg[:, o:o + 256], ACT.Relu, scale=1.0 if odd else -1.0,
+                               accum_out=T.ls[:, i:i + 1]))
 
-    def own_block(c, o):
-        wait("v", kt[c])
-        return V(v.tensor_tensor(cm[:, o:o + 128], row(c), T.thr[:, 128 * c:128 * c + 128], strict))
-
+    c01 = min(B[0:2])
     quant(B[0])
+    down(B[0], 0, 2 * (B[0] % 2), True, False)
+    kr[B[0]] = along(row[B[0]], B[0], 1)
     wait("v", k_gt)
     k_go = V(v.tensor_scalar(T.goff[:, 0:2], T.gt[:, 0:2], 1.0 / 32, None, OP.mult))
     quant(B[1])
-    down(B[0], 0, 2 * (B[0] % 2), True, False)
     k = down(B[1], 0, 2 * (B[1] % 2), False, True)
+    kr[B[1]] = along(row[B[1]], B[1], 1)
+    krs = along(T.psp[:, 1536:1792], c01, 2)
     ka, kd = scores(c01, 2, T.psp[:, 0:4:2], k)
-    kh0 = along(h0, h0)
-    kh0s = along(h0, 2)
     for c in B[0:2]:
-        kt[c] = bound(c, kd)
+        bound(c, kd)
     quant(B[2])
     k = down(B[2], 1)
+    kr[B[2]] = along(row[B[2]], B[2], 1)
     ka2, kd = scores(B[2], 1, T.psp[:, 512:513], k)
-    kt[B[2]] = bound(B[2], kd)
-    k2 = signs(B[2], 0)
-    wait("v", ka, kh0)
-    cmp(cm[:, 0:128], row(B[1]), sp[B[0]], loose)
-    cmp(cm[:, 512:640], row(B[0]), sp[B[1]], strict)
+    bound(B[2], kd)
+    k2 = signs(2, 0)
+    wait("v", ka)
+    cell(1, 0, 512)
+    cell(0, 1, 0)
+    cell(0, 0, 128)
     quant(B[3])
-    kh1 = along(h1, h1)
     k = down(B[3], 2)
+    kr[B[3]] = along(row[B[3]], B[3], 1)
     ka3, kd = scores(B[3], 1, T.psp[:, 1024:1025], k)
-    sum_signs(B[2], 0, k2)
-    kt[B[3]] = bound(B[3], kd)
-    sum_signs(B[3], 1, signs(B[3], 1))
-    own_block(B[0], 128)
-    own_block(B[1], 640)
-    wait("v", kh1)
-    a = cmp(cm[:, 256:512], row(2 * h1, 2), sp[B[0]], loose)
-    b = cmp(cm[:, 768:1024], row(2 * h1, 2), sp[B[1]], loose)
-    wait("v", a, ka2)
+    sum_signs(2, 0, k2)
+    bound(B[3], kd)
+    sum_signs(3, 256, signs(3, 256))
+    cell(1, 1, 640)
+    cell(0, 2, 256)
+    cell(1, 2, 768)
+    cell(2, 2, 1024)
+    a = cell(0, 3, 384)
+    b = cell(1, 3, 896)
+    c = cell(2, 3, 1152)
+    wait("v", a, ka3)
     add_up(T.cs[:, 256 * (B[0] % 2):256 * (B[0] % 2) + 256], cm, 0, 256, -256.0)
-    cmp(cm[:, 1024:1152], row(B[3]), sp[B[2]], loose)
+    cell(3, 2, 1408)
+    d = cell(3, 3, 1280)
     wait("v", b)
     b = add_up(T.cs[:, 256 * (B[1] % 2):256 * (B[1] % 2) + 256], cm, 512, 256, -256.0)
-    a = own_block(B[2], 1152)
-    wait("v", ka3)
-    cmp(cm[:, 1280:1408], row(B[2]), sp[B[3]], strict)
-    c = own_block(B[3], 1408)
-    wait("v", a, b)
-    a = add_up(T.cs[:, 512:640], cm, 1024, 128, 0.0)
+    wait("v", d)
+    c = add_up(T.cs[:, 512:640], cm, 1024, 128, 0.0)
+    d = add_up(T.cs[:, 640:768], cm, 1280, 128, 0.0)
     shift = 0.0 if odd else 16.0
+    wait("v", b)
     V(v.tensor_scalar(T.pu1[:, c01:c01 + 2], T.cs[:, 255:512:256], 256.0 + shift, None, OP.add))
-    wait("v", c)
-    c = add_up(T.cs[:, 640:768], cm, 1280, 128, 0.0)
-    wait("v", a, kl[B[2]])
-    V(v.tensor_scalar(T.pu1[:, B[2]:B[2] + 1], T.cs[:, 639:640], T.ls[:, B[2]:B[2] + 1], shift, OP.add, OP.add))
-    wait("v", c, kl[B[3]])
-    k_pu = V(v.tensor_scalar(T.pu1[:, B[3]:B[3] + 1], T.cs[:, 767:768], T.ls[:, B[3]:B[3] + 1], shift, OP.add, OP.add))
+    wait("v", c, kl[2])
+    V(v.tensor_scalar(T.pu1[:, B[2]:B[2] + 1], T.cs[:, 639:640], T.ls[:, 2:3], shift, OP.add, OP.add))
+    wait("v", d, kl[3])
+    k_pu = V(v.tensor_scalar(T.pu1[:, B[3]:B[3] + 1], T.cs[:, 767:768], T.ls[:, 3:4], shift, OP.add, OP.add))
 
-    def invert(n, ready, cols, vals, lo, lift):
+    def invert(n, ready, cols, vals, lo, lift, fill=None):
         W = lambda b: T[b + n]
         wait("v", *ready)
         a = V(v.tensor_copy(W("win")[:, 0:528].indirect(W("pu")[:, 0:cols]), vals[:, 0:16 * cols]))
+        if fill:
+            fill()
         wait("v", a)
         V(v.transpose(W("tz")[:, 0:128], W("win")[:, lo:lo + 128]))
         a = V(v.transpose(W("tz")[:, 128:288], W("win")[:, lo - 16:lo + 144]))
@@ -281,18 +298,19 @@ def rank_program(g, core, T, topo):
         wait("g", b)
         return kc, remote(out_s, in_s, dst, sem_s)
 
-    m0 = SLOT * rank
-    k_q1, k_l1 = invert("1", (k_pu,), 4, T.vals1, lo1, 256.0)
-    wait("s", k_q1, k_go)
-    S(s.activation(T.msg[:, m0 + 5:m0 + 21], T.qc1[:, 0:9].indirect(T.goff[:, 0:1]), IDENT, bias=256.0))
-    a1, b1 = pick(T.c1[:, 0:K], T.s1[:, 0:K], T.xq[:, 0:512], T.xs[:, 0:512], T.lst1[:, 2:10], (k_l1,), (k_l1,))
+    m0, m1 = SLOT * rank, SLOT * (rank ^ 1)
     mate = T.cores[rank ^ 1]
+    wait("g", k_pu)
+    in_places = remote(T.pum[:, 0:4], T.pu1[:, 0:4], mate, "hp")
+    k_q1, k_l1 = invert("1", (k_pu, k_v1), 4, T.vals1, lo1, 256.0)
+    wait("s", k_q1, k_go)
+    S(s.activation(T.msg[:, m0 + 5:m0 + 21], T.qc1[:, 0:9].indirect(T.goff[:, 0:1]), COPY))
+    a1, b1 = pick(T.c1[:, 0:K], T.s1[:, 0:K], T.xq[:, 0:512], T.xs[:, 0:512], T.lst1[:, 2:10], (k_l1,), (k_l1,))
     in1c, in1s = send(T.c1[:, K:2 * K], T.c1[:, 0:K], T.s1[:, K:2 * K], T.s1[:, 0:K], a1, b1, mate, "h1c", "h1s")
 
     wait("t", a1, b1)
     kaf = X(t.matmul_mx(T.psf[:, 0:128], T.uq[:, 0:128], T.us[:, 0:128], T.c1[:, 0:128], T.s1[:, 0:128], True, True))
     kap = X(t.matmul_mx(T.psp[:, 0:128], T.c1[:, 0:128], T.s1[:, 0:128], T.uq0[:, 2:130], T.us0[:, 2:130], True, True))
-    V(v.tensor_scalar(T.ita[:, 0:128], T.it[:, 0:128], 15, None, OP.bitwise_and))
     wait("s", kap)
     k_m4 = S(s.activation(T.msg[:, m0 + 4:m0 + 5], T.psp[:, 0:1], COPY))
     wait("v", kaf)
@@ -312,33 +330,34 @@ def rank_program(g, core, T, topo):
                        local_sem=T.sem["sent"])
     in_msg = ("hm", 2 * n)
     count["sent"] += n
-    view = T.msg[:, m0 + 4:m0 + 6]
-    in_mate = remote(view, view, mate, "hp")
 
-    a = V(v.tensor_scalar(T.nb0[:, 0:128], T.ita[:, 0:128], 0.0, 2 * BIG, OP.is_equal, OP.mult))
-    b = V(v.memset(T.hs[:, 0:128], 0.0))
-    k = V(v.tensor_scalar(T.pcq[:, 1:2], T.pcf[:, 1:2], 128.0, None, OP.add))
-    wait("v", a)
-    a = V(v.tensor_scalar(T.nb[:, 0:128], T.nb0[:, 0:128], -BIG, None, OP.add))
-    wait("v", b, k, k_i6)
-    k_hs = V(v.tensor_scalar(T.hs[:, 0:128:16], T.i6[:, 0:8], T.pcq[:, 1:2], 1.0 / 128, OP.add, OP.mult))
-    wait("v", a)
-    k_am = V(v.tensor_tensor(T.am[:, 0:128], T.nb[:, 0:128], T.psf[:, 0:128], OP.min))
+    wait("v", k_zero)
+    k_am = V(v.tensor_tensor(T.am[:, 0:128], T.nb[:, 0:128], T.psf[:, 0:128], OP.add))
+    k_co = V(v.tensor_copy(T.eoff[:, 0:16], T.i5[:, 0:16]))
     wait("v", dw)
     k_w = V(v.quantize_mx(T.wq[:, 0:256], T.ws[:, 0:256], T.wb[:, 0:1024]))
-    wait("v", k_i5, k_i4, k_pt)
-    V(v.tensor_copy(T.eoff[:, 0:16], T.i5[:, 0:16]))
-    k = V(v.tensor_scalar(T.pcq[:, 0:1], T.pcf[:, 0:1], 2.0, None, OP.mult))
-    V(v.tensor_scalar(T.pct[:, 0:1], T.pt[:, 0:1], -2.0, 127.0, OP.mult, OP.add))
-    V(v.memset(T.win2[:, 0:160], 0.0))
-    V(v.memset(T.cp[:, 0:64], 0.0))
-    V(v.memset(T.idr[:, 64:256], 0.0))
-    wait("v", k)
-    k_co = V(v.tensor_scalar(T.vals2[:, 0:32], T.i4[:, 0:32], T.pcq[:, 0:1], None, OP.add))
+    wait("v", in_places)
+    a = V(v.tensor_copy(T.winm[:, 0:528].indirect(T.pum[:, 0:4]), T.vals1[:, 0:64]))
+    wait("v", a)
+    a = V(v.transpose(T.tzm[:, 0:128], T.winm[:, lom:lom + 128]))
+    k_hs = V(v.tensor_scalar(T.hs[:, 0:128:16], T.i6[:, 0:8], T.pcq[:, 0:1], 1.0 / 128, OP.add, OP.mult))
+    wait("v", a)
+    a = V(v.tensor_tensor(T.qam[:, 0:4], T.tzm[:, 0:128:32], T.tzm[:, 16:128:32], OP.add))
+    wait("v", a)
+    a = V(v.tensor_tensor(T.qbm[0:64, 0:4], T.qam[0:64, 0:4], T.qam[64:128, 0:4], OP.add))
+    wait("v", a)
+    for h in range(4):
+        k_im = V(v.tensor_tensor(T.msg[32 * h:32 * h + 32, m1 + 5:m1 + 6], T.qbm[0:32, h:h + 1], T.qbm[32:64, h:h + 1], OP.add))
 
     fr = (T.psf[:, 512:640], T.psf[:, 0:128]) if odd else (T.psf[:, 0:128], T.psf[:, 512:640])
     wait("t", in1c, in1s)
     kb = X(t.matmul_mx(T.psf[:, 512:640], T.uq[:, 0:128], T.us[:, 0:128], T.c1[:, 128:256], T.s1[:, 128:256], True, True))
+    kbp = X(t.matmul_mx(T.psp[:, 512:640], T.c1[:, 128:256], T.s1[:, 128:256], T.uq0[:, 2:130], T.us0[:, 2:130], True, True))
+    kbs = X(t.matmul_mx(T.psp[:, 1024:1280], T.uq[:, 0:128], T.us[:, 0:128], T.c1[:, 0:256], T.s1[:, 0:256], True, True))
+    wait("s", kbp)
+    k_m4 = S(s.activation(T.msg[:, m1 + 4:m1 + 5], T.psp[:, 512:513], COPY))
+    wait("s", in_msg, k_co)
+    ky = S(s.activation(T.yx[:, 0:256], T.msg[:, 2 * SLOT * Q:2 * SLOT * (Q + 1)].indirect(T.eoff[:, 0:16]), COPY))
     wait("v", kb, k_am)
     a = V(v.tensor_tensor(T.bc[:, 0:128], T.am[:, 0:128], T.psf[:, 512:640], OP.is_gt if odd else OP.is_ge))
     wait("v", a, k_hs)
@@ -353,69 +372,76 @@ def rank_program(g, core, T, topo):
         return [X(t.matmul_mx(bank[:, 512 * (o + 2):512 * (o + 2) + 128], T.wq[:, 128 * o:128 * o + 128], T.ws[:, 128 * o:128 * o + 128],
                               T.c2[:, side], T.s2[:, side], True, True)) for o in range(2)]
     ko = products(own, T.psf, a2, b2)
-    kr = products(arr, T.psp, in2c, in2s)
 
     word = lambda rk, w: T.msg[:, SLOT * rk + w:SLOT * rk + w + 1]
     E, O = T.msg[:, 4:4 * SLOT:2 * SLOT], T.msg[:, SLOT + 4:4 * SLOT:2 * SLOT]
     ps, sel, nsel = [[T[b][:, j:j + 1] for j in range(2)] for b in ("ps", "sel", "nsel")]
-    wait("s", in_msg, k_co)
-    ky = S(s.activation(T.yx[:, 0:256], T.msg[:, 2 * SLOT * Q:2 * SLOT * (Q + 1)].indirect(T.eoff[:, 0:16]), COPY))
-    wait("v", in_msg, in_mate, k_m4)
+    wait("v", in_msg, k_m4)
     a = V(v.tensor_tensor(T.ps[:, 0:2], E, O, OP.max))
     k_sel = V(v.tensor_tensor(T.sel[:, 0:2], O, E, OP.is_gt))
     b = V(v.tensor_tensor(T.nsel[:, 0:2], E, O, OP.is_ge))
-    k_vd = V(v.tensor_tensor(T.vd[:, 0:2], T.msg[:, SLOT + 5:4 * SLOT:2 * SLOT], T.msg[:, 5:4 * SLOT:2 * SLOT], OP.subtract))
+    wait("s", a, kbs)
+    ks = S(s.activation(T.sq[:, 0:256], T.psp[:, 1024:1280], ACT.Sign, bias=ps[Q], scale=-1.0))
     wait("s", k_sel)
     for j in range(2):
-        kc = S(s.activation(T.kc[:, j:j + 1], sel[j], IDENT, bias=T.pt[:, 1:2], scale=T.pct[:, 0:1]))
-    wait("s", k_vd)
+        kc = S(s.activation(T.kc[:, j:j + 1], sel[j], IDENT, bias=T.pt[:, 0:1], scale=T.pt[:, 1:2]))
+    wait("s", ks)
+    kq2 = S(s.activation(T.sq[:, 256:512], T.sq[:, 0:256], ACT.Relu, scale=1.0 if P < Q else -1.0, accum_out=T.lq[:, 0:1]))
+    wait("t", ks)
+    kr = products(arr, T.psp, in2c, in2s)
+    wait("s", k_im)
+    for j in range(2):
+        k = S(s.activation(T.vd[:, j:j + 1], word(2 * j, 5), IDENT, bias=word(2 * j + 1, 5), scale=-1.0))
+    wait("s", k)
     for j in range(2):
         S(s.activation(T.cp[:, 32 * j:32 * j + 1], sel[j], IDENT, bias=2.0 * j))
         kcp = S(s.activation(T.cp[:, 32 * j + 1:32 * j + 2], T.vd[:, j:j + 1], IDENT, bias=word(2 * j, 5), scale=sel[j]))
-    wait("v", a)
-    for f in range(2):
-        cmp(T.bb[:, 128 * f:128 * f + 128], fr[f], ps[Q], OP.is_ge if P < Q else OP.is_gt)
+    wait("v", ky)
+    kf = V(v.transpose(T.fs[:, 0:256], T.yx[:, 0:256]))
     wait("v", b)
     cmp(T.ba[:, 0:128], fr[1], ps[P], OP.is_gt, nsel[P])
     cmp(T.ba[:, 128:256], fr[0], ps[P], OP.is_ge, sel[P])
-    wait("v", ky)
-    kt = V(v.transpose(T.fs[:, 0:256], T.yx[:, 0:256]))
-    wait("v", kcp)
-    for j in range(2):
-        kz = V(v.transpose(T.idr[:, j:64:2], T.cp[:, 32 * j:32 * j + 32]))
-    wait("v", kt)
+    wait("v", kf)
     a = cmp(T.ba[:, 256:512], T.fs[:, 0:256], ps[P], OP.is_ge if Q < P else OP.is_gt)
-    cmp(T.bb[:, 256:384], T.fs[:, 128:256], ps[Q], OP.is_gt, nsel[Q])
-    b = cmp(T.bb[:, 384:512], T.fs[:, 0:128], ps[Q], OP.is_ge, sel[Q])
+    cmp(T.bb[:, 0:128], T.fs[:, 128:256], ps[Q], OP.is_gt, nsel[Q])
+    b = cmp(T.bb[:, 128:256], T.fs[:, 0:128], ps[Q], OP.is_ge, sel[Q])
     wait("v", a, kc)
-    add_up(T.bt[:, 256 * P:256 * P + 256], T.ba, 0, 256, T.kc[:, P:P + 1])
+    a = add_up(T.bt[:, 0:256], T.ba, 0, 256, T.kc[:, P:P + 1])
     wait("v", b)
-    a = add_up(T.bt[:, 256 * Q:256 * Q + 256], T.bb, 0, 256, T.kc[:, Q:Q + 1])
+    b = add_up(T.bt[:, 256:384], T.bb, 0, 128, T.kc[:, Q:Q + 1])
     wait("v", a)
-    kv = V(v.tensor_scalar(T.pu2[:, 0:2], T.bt[:, 255:512:256], 144.0, None, OP.add))
+    V(v.tensor_scalar(T.pu2[:, P:P + 1], T.bt[:, 255:256], 144.0, None, OP.add))
+    wait("v", b, kq2)
+    kv = V(v.tensor_scalar(T.pu2[:, Q:Q + 1], T.bt[:, 383:384], T.lq[:, 0:1], 400.0 if P < Q else 144.0,
+                           OP.subtract if P < Q else OP.add, OP.add))
 
     yw = (T.yw0, T.yw1)
     for o in range(2):
         wait("s", ko[o])
         S(s.activation(yw[o][:, P:256:2], T.psf[:, 512 * (o + 2):512 * (o + 2) + 128], COPY))
-    wait("s", kz)
+    kz = []
+
+    def numbers():
+        wait("v", kcp)
+        for j in range(2):
+            kz.append(V(v.transpose(T.idr[:, j:64:2], T.cp[:, 32 * j:32 * j + 32])))
+    k_q2, k_l2 = invert("2", (kv,), 2, T.vals2, 16, 128.0, numbers)
+    wait("s", *kz)
     for a in range(1, 4):
         S(s.activation(T.idr[0:2, 64 * a:64 * a + 64], T.idr[32 * a:32 * a + 2, 0:64], COPY))
     for o in range(2):
         wait("s", kr[o])
         kyw = S(s.activation(yw[o][:, Q:256:2], T.psp[:, 512 * (o + 2):512 * (o + 2) + 128], COPY))
 
-    k_q2, k_l2 = invert("2", (kv,), 2, T.vals2, 16, 128.0)
-
     off = T.lst2[:, 2:10]
     wait("v", k_l2, kyw)
     ky0 = V(v.tensor_copy(T.yb[:, 0:128], T.yw0[:, 0:256].indirect(off)))
-    ki = V(v.tensor_copy(T.idb[:, 0:128], T.idr[:, 0:256].indirect(off)))
+    ki = V(v.tensor_scalar(T.idb[:, 0:128], T.idr[:, 0:256].indirect(off), T.pt[:, 2:3], None, OP.add))
     wait("s", k_l2, kyw)
     ky1 = S(s.activation(T.yb[:, 128:256], T.yw1[:, 0:256].indirect(off), COPY))
     wait("y", ky0, ky1)
     d0 = done(y.dma_start(T.y[:, 0:256], T.yb[:, 0:256]), "dy", 16)
     wait("s", ki)
     d2 = done(s.dma_start(T["id"][0:2, 0:128], T.idb[0:2, 0:128]), "did", 16)
-    wait("g", ("sent", count["sent"]), in1c, in1s, in2c, in2s, in_msg, in_mate, du, *dx.values(), dw,
+    wait("g", ("sent", count["sent"]), in1c, in1s, in2c, in2s, in_msg, in_places, du, *dx.values(), dw,
          ("gc", count["gc"]), ("v", count["v"]), ("s", count["s"]), ("t", count["t"]), d0, d2)

@@ -24,29 +24,30 @@ SCRATCH = {
     "yb": ("sbuf", [128, 256], "float32"),
     "psf": ("psum", [128, 2048], "float32"),
     "psp": ("psum", [128, 2048], "float32"),
-    "ip": ("sbuf", [128, 2], "int32"), "pt": ("sbuf", [128, 4], "float32"),
+    "ip": ("sbuf", [128, 2], "int32"), "pt": ("sbuf", [128, 8], "float32"),
     "it": ("sbuf", [128, 128], "int32"), "ita": ("sbuf", [128, 128], "int32"), "tri": ("sbuf", [128, 128], "float32"),
     "nb": ("sbuf", [128, 128], "float32"),
     "i3": ("sbuf", [128, 64], "float32"), "vals1": ("sbuf", [128, 64], "bfloat16"),
     "i4": ("sbuf", [128, 32], "float32"), "vals2": ("sbuf", [128, 32], "bfloat16"),
     "i5": ("sbuf", [128, 16], "int32"), "eoff": ("sbuf", [128, 16], "uint16"),
-    "i6": ("sbuf", [128, 8], "float32"), "hs": ("sbuf", [128, 128], "bfloat16"),
+    "i6": ("sbuf", [128, 16], "float32"), "jc": ("sbuf", [128, 16], "float32"), "dg": ("sbuf", [128, 16], "float32"),
+    "seg": ("sbuf", [128, 224], "float32"), "rs": ("sbuf", [128, 128], "float32"),
     "gr": ("sbuf", [128, 32], "float32"), "gt": ("sbuf", [128, 32], "float32"), "goff": ("sbuf", [128, 2], "uint16"),
     "pca": ("sbuf", [128, 2], "int32"), "pcf": ("sbuf", [128, 2], "float32"), "pcq": ("sbuf", [128, 2], "float32"),
     "sp": ("sbuf", [128, 4], "float32"), "dl": ("sbuf", [128, 4], "float32"), "thr": ("sbuf", [128, 512], "float32"),
     "cm": ("sbuf", [128, 1536], "bfloat16"), "cs": ("sbuf", [128, 768], "bfloat16"),
-    "sg": ("sbuf", [128, 640], "bfloat16"), "junk": ("sbuf", [128, 640], "bfloat16"), "ls": ("sbuf", [128, 4], "float32"),
+    "sg": ("sbuf", [128, 512], "bfloat16"), "junk": ("sbuf", [128, 512], "bfloat16"), "ls": ("sbuf", [128, 4], "float32"),
     "msg": ("sbuf", [128, 4 * SLOT], "float32"), "at": ("sbuf", [128, 128], "float32"),
-    "pum": ("sbuf", [128, 8], "uint16"), "winm": ("sbuf", [128, 528], "bfloat16"), "tzm": ("sbuf", [128, 128], "bfloat16"),
-    "qam": ("sbuf", [128, 4], "float32"), "qbm": ("sbuf", [64, 4], "float32"),
-    "am": ("sbuf", [128, 128], "float32"),
-    "bc": ("sbuf", [128, 128], "bfloat16"), "bs": ("sbuf", [128, 128], "bfloat16"),
-    "off2": ("sbuf", [128, 8], "uint16"),
+    "spm": ("sbuf", [128, 4], "float32"), "pum": ("sbuf", [128, 8], "uint16"), "valm": ("sbuf", [128, 64], "float32"),
+    "winm": ("sbuf", [128, 528], "float32"), "tzm": ("sbuf", [128, 288], "float32"), "qam": ("sbuf", [128, 416], "float32"),
+    "qbm": ("sbuf", [64, 16], "float32"), "qcm": ("sbuf", [128, 16], "float32"), "ml": ("sbuf", [128, 16], "float32"),
+    "am": ("sbuf", [128, 128], "float32"), "ow": ("sbuf", [128, 256], "float32"),
+    "bc": ("sbuf", [128, 16], "float32"), "bs": ("sbuf", [128, 16], "float32"), "off2": ("sbuf", [128, 16], "uint16"),
     "yx": ("sbuf", [128, 256], "float32"), "fs": ("sbuf", [128, 256], "float32"),
     "ps": ("sbuf", [128, 2], "float32"), "sel": ("sbuf", [128, 2], "float32"), "nsel": ("sbuf", [128, 2], "float32"),
     "vd": ("sbuf", [128, 2], "float32"), "kc": ("sbuf", [128, 2], "float32"),
-    "ba": ("sbuf", [128, 512], "bfloat16"), "bb": ("sbuf", [128, 256], "bfloat16"), "bt": ("sbuf", [128, 384], "bfloat16"),
-    "sq": ("sbuf", [128, 512], "bfloat16"), "lq": ("sbuf", [128, 1], "float32"),
+    "ba": ("sbuf", [128, 512], "bfloat16"), "bb": ("sbuf", [128, 128], "bfloat16"), "bt": ("sbuf", [128, 256], "bfloat16"),
+    "bu": ("sbuf", [128, 64], "float32"), "sq": ("sbuf", [128, 768], "bfloat16"), "lq": ("sbuf", [128, 2], "float32"),
     "cp": ("sbuf", [128, 64], "float32"), "idr": ("sbuf", [128, 256], "float32"), "idb": ("sbuf", [128, 128], "float32"),
 }
 for _n in ("1", "2"):
@@ -59,7 +60,7 @@ for _n in ("1", "2"):
     SCRATCH["lst" + _n] = ("sbuf", [128, 16], "uint16")
 
 SEMAPHORES = ["v", "s", "t", "gc", "du", "dx0", "dx1", "dx2", "dx3", "dw", "dy", "did",
-              "h1c", "h1s", "h2c", "h2s", "hm", "hp", "sent"]
+              "h1c", "h1s", "h2c", "h2s", "hm", "hr", "hp", "hi", "sent"]
 
 
 def rank_program(g, core, T, topo):
@@ -89,6 +90,7 @@ def rank_program(g, core, T, topo):
     def V(ins): return done(ins, "v")
     def S(ins): return done(ins, "s")
     def X(ins): return done(ins, "t")
+    def G(ins): return done(ins, "gc")
 
     B = [0, 1, 2, 3] if odd else [3, 2, 1, 0]
     du = done(s.dma_start(T.ur[:, 8:16], T.u[:, 0:8]), "du", 16)
@@ -98,23 +100,21 @@ def rank_program(g, core, T, topo):
 
     def iota(buf, pattern, base, cm, flt=True):
         if flt:
-            return done(g.iota(buf, pattern, base, cm, allow_small_or_imprecise_dtypes=True), "gc")
-        return done(g.iota(buf, pattern, base, cm), "gc")
+            return G(g.iota(buf, pattern, base, cm, allow_small_or_imprecise_dtypes=True))
+        return G(g.iota(buf, pattern, base, cm))
     k_it = iota(T.it[:, 0:128], [[1, 128]], 128, -1, False)
     k_ip = iota(T.ip[:, 0:2], [[0, 2]], 0, 1, False)
     k_i3 = iota(T.i3[:, 0:64], [[128, 4], [1, 16]], -256, 0)
+    k_i4 = iota(T.i4[:, 0:32], [[1, 2], [2, 16]], -128, 0)
     wait("g", iota(T.gr[:, 0:32], [[0, 32]], 0, 1))
     iota(T.gr[:, 2:10], [[32, 4], [160, 2]], 0, 0)
     k_gr = iota(T.gr[:, 18:26], [[32, 4], [-128, 2]], 128, 0)
-    k_i4 = iota(T.i4[:, 0:32], [[1, 2], [2, 16]], -128, 0)
-    iota(T.i6[:, 0:8], [[16, 8]], 0, 0)
-    iota(T.pt[:, 0:1], [[0, 1]], -128, 1)
-    iota(T.pt[:, 1:2], [[0, 1]], 127, -2)
-    iota(T.pt[:, 2:3], [[0, 1]], 0, 256)
+    k_i6 = iota(T.i6[:, 0:16], [[16, 16]], -32, 0)
     iota(T.i5[:, 0:16], [[SLOT, 2], [1, 4], [0, 2]], 0, 0, False)
+    for i, (base, step) in enumerate(((-128, 1), (127, -2), (0, 256), (255, -2), (272 if P < Q else 16, 1))):
+        iota(T.pt[:, i:i + 1], [[0, 1]], base, step)
+    k_one = iota(T.seg[:, 0:224], [[0, 224]], 1, 0)
     lo1, lom = (384, 16) if odd else (16, 384)
-    for buf, a, n in ((T.hs, 0, 128), (T.winm, lom, 128), (T.win2, 0, 160), (T.cp, 0, 64), (T.idr, 64, 192)):
-        k_zero = iota(buf[:, a:a + n], [[0, n]], 0, 0)
 
     V(v.memset(T.ur[:, 0:8], 0.0))
     k_ur = V(v.memset(T.ur[:, 16:520], 0.0))
@@ -132,6 +132,7 @@ def rank_program(g, core, T, topo):
     wait("v", k)
     k_pc = V(v.tensor_copy(T.pcf[:, 0:2], T.pca[:, 0:2]))
     V(v.tensor_scalar(T.nb[:, 0:128], T.ita[:, 0:128], 0.0, -BIG, OP.not_equal, OP.mult))
+    V(v.tensor_scalar(T.dg[:, 0:16], T.ita[:, 0:16], 0.0, None, OP.is_equal))
 
     wait("v", du, k_ur)
     k_u0 = V(v.quantize_mx(T.uq0[:, 0:130], T.us0[:, 0:130], T.ur[:, 0:520]))
@@ -141,44 +142,42 @@ def rank_program(g, core, T, topo):
     k_us = S(s.activation(T.us[:, 0:128], T.us0[:, 0:130].indirect(T.zoff[:, 0:8]), COPY))
     wait("s", k_i3, k_pc)
     k_v1 = S(s.activation(T.vals1[:, 0:64], T.i3[:, 0:64], IDENT, bias=T.pcf[:, 0:1]))
-    S(s.activation(T.pcq[:, 0:1], T.pcf[:, 1:2], IDENT, bias=128.0))
-    k = S(s.activation(T.pcq[:, 1:2], T.pcf[:, 0:1], COPY, scale=2.0))
-    wait("s", k, k_i4)
-    S(s.activation(T.vals2[:, 0:32], T.i4[:, 0:32], IDENT, bias=T.pcq[:, 1:2]))
-    wait("v", k_gr)
-    k_gt = V(v.transpose(T.gt[:, 0:32], T.gr[:, 0:32]))
 
-    kq, kr, kt, kl = {}, {}, {}, {}
+    kq, kr, kp, kt, kl = {}, {}, {}, {}, {}
+    strict, loose = (OP.is_lt, OP.is_le) if odd else (OP.is_gt, OP.is_ge)
+    row = [T.psf[:, 512 * d:512 * d + 128] for d in range(4)]
+    sp = [T.sp[:, c:c + 1] for c in range(4)]
+    cm = T.cm
 
-    def quant(d):
-        e = slice(128 * d, 128 * d + 128)
+    def quant(i):
+        d = B[i]
         wait("v", dx[d])
-        kq[d] = V(v.quantize_mx(T.xq[:, e], T.xs[:, e], T.xb[:, 512 * d:512 * d + 512]))
-
-    def down(c, bank, at=0, start=True, stop=True):
-        e, m = slice(128 * c, 128 * c + 128), slice(2 - at, 130 - at)
-        wait("t", k_u0, kq[c])
-        return X(t.matmul_mx(T.psp[:, 512 * bank:512 * bank + 128], T.xq[:, e], T.xs[:, e], T.uq0[:, m], T.us0[:, m], start, stop))
+        kq[d] = V(v.quantize_mx(T.xq[:, 128 * d:128 * d + 128], T.xs[:, 128 * d:128 * d + 128], T.xb[:, 512 * d:512 * d + 512]))
 
     def along(out, d, n):
         e = slice(128 * d, 128 * (d + n))
         wait("t", k_uc, k_us, *[kq[c] for c in range(d, d + n)])
         return X(t.matmul_mx(out, T.uq[:, 0:128], T.us[:, 0:128], T.xq[:, e], T.xs[:, e], True, True))
 
-    def scores(c, n, src, k):
+    def down(i):
+        c, bank = B[i], 512 * (i // 2)
+        e, m = slice(128 * c, 128 * c + 128), slice(2 - 2 * (c % 2), 130 - 2 * (c % 2))
+        wait("t", k_u0, kq[c])
+        return X(t.matmul_mx(T.psp[:, bank:bank + 128], T.xq[:, e], T.xs[:, e], T.uq0[:, m], T.us0[:, m], i % 2 == 0, i % 2 == 1))
+
+    def scores(i, k):
+        c, src = min(B[i:i + 2]), T.psp[:, 256 * i:256 * i + 4:2]
         wait("s", k)
-        a = S(s.activation(T.sp[:, c:c + n], src, COPY))
-        b = S(s.activation(T.dl[:, c:c + n], src, ACT.Abs, bias=TINY, scale=STEP))
-        return a, b
+        kp[i] = kp[i + 1] = S(s.activation(T.sp[:, c:c + 2], src, COPY))
+        return S(s.activation(T.dl[:, c:c + 2], src, ACT.Abs, bias=TINY, scale=STEP))
 
-    def bound(c, k):
+    def bound(i, k):
+        c = B[i]
         wait("s", k, k_tri)
-        kt[c] = S(s.activation(T.thr[:, 128 * c:128 * c + 128], T.tri[:, 0:128], IDENT, bias=T.sp[:, c:c + 1], scale=T.dl[:, c:c + 1]))
+        kt[i] = S(s.activation(T.thr[:, 128 * c:128 * c + 128], T.tri[:, 0:128], IDENT, bias=sp[c], scale=T.dl[:, c:c + 1]))
 
-    strict, loose = (OP.is_lt, OP.is_le) if odd else (OP.is_gt, OP.is_ge)
-    row = [T.psf[:, 512 * d:512 * d + 128] for d in range(4)]
-    sp = [T.sp[:, c:c + 1] for c in range(4)]
-    cm = T.cm
+    def rows(i):
+        kr[i] = along(row[B[i]], B[i], 1)
 
     def cmp(out, src, col, op, weight=None):
         if weight is None:
@@ -187,17 +186,17 @@ def rank_program(g, core, T, topo):
 
     def cell(i, j, o):
         c, d = B[i], B[j]
-        wait("v", kr[d])
         if i == j:
-            wait("v", kt[c])
+            wait("v", kr[j], kt[i])
             return V(v.tensor_tensor(cm[:, o:o + 128], row[d], T.thr[:, 128 * c:128 * c + 128], strict))
+        wait("v", kr[j], kp[i])
         return cmp(cm[:, o:o + 128], row[d], sp[c], loose if i < j else strict)
 
     def add_up(out, buf, o, n, first):
         return V(v.tensor_tensor_scan(out, buf[:, o:o + n], buf[:, o + n:o + 2 * n], first, OP.add, OP.add))
 
     def signs(i, o):
-        wait("s", krs)
+        wait("s", krs, kp[i])
         return S(s.activation(T.sg[:, o:o + 256], T.psp[:, 1536:1792], ACT.Sign, bias=sp[B[i]], scale=-1.0))
 
     def sum_signs(i, o, k):
@@ -206,77 +205,74 @@ def rank_program(g, core, T, topo):
                                accum_out=T.ls[:, i:i + 1]))
 
     c01 = min(B[0:2])
-    quant(B[0])
-    down(B[0], 0, 2 * (B[0] % 2), True, False)
-    kr[B[0]] = along(row[B[0]], B[0], 1)
-    wait("v", k_gt)
-    k_go = V(v.tensor_scalar(T.goff[:, 0:2], T.gt[:, 0:2], 1.0 / 32, None, OP.mult))
-    quant(B[1])
-    k = down(B[1], 0, 2 * (B[1] % 2), False, True)
-    kr[B[1]] = along(row[B[1]], B[1], 1)
+    quant(0)
+    down(0)
+    rows(0)
+    quant(1)
+    k = scores(0, down(1))
+    rows(1)
+    bound(0, k)
+    bound(1, k)
+    quant(2)
+    down(2)
+    rows(2)
+    quant(3)
+    k = scores(2, down(3))
     krs = along(T.psp[:, 1536:1792], c01, 2)
-    ka, kd = scores(c01, 2, T.psp[:, 0:4:2], k)
-    for c in B[0:2]:
-        bound(c, kd)
-    quant(B[2])
-    k = down(B[2], 1)
-    kr[B[2]] = along(row[B[2]], B[2], 1)
-    ka2, kd = scores(B[2], 1, T.psp[:, 512:513], k)
-    bound(B[2], kd)
+    rows(3)
     k2 = signs(2, 0)
-    wait("v", ka)
-    cell(1, 0, 512)
-    cell(0, 1, 0)
-    cell(0, 0, 128)
-    quant(B[3])
-    k = down(B[3], 2)
-    kr[B[3]] = along(row[B[3]], B[3], 1)
-    ka3, kd = scores(B[3], 1, T.psp[:, 1024:1025], k)
+    bound(2, k)
+    k3 = signs(3, 256)
+    bound(3, k)
     sum_signs(2, 0, k2)
-    bound(B[3], kd)
-    sum_signs(3, 256, signs(3, 256))
-    cell(1, 1, 640)
-    cell(0, 2, 256)
-    cell(1, 2, 768)
-    cell(2, 2, 1024)
-    a = cell(0, 3, 384)
-    b = cell(1, 3, 896)
-    c = cell(2, 3, 1152)
-    wait("v", a, ka3)
-    add_up(T.cs[:, 256 * (B[0] % 2):256 * (B[0] % 2) + 256], cm, 0, 256, -256.0)
+    sum_signs(3, 256, k3)
+    for i, j, o in ((1, 0, 512), (0, 1, 0), (0, 2, 256), (0, 0, 128), (1, 2, 768), (1, 1, 640), (0, 3, 384), (1, 3, 896), (2, 3, 1152)):
+        b = cell(i, j, o)
     cell(3, 2, 1408)
-    d = cell(3, 3, 1280)
     wait("v", b)
+    c = cell(2, 2, 1024)
+    add_up(T.cs[:, 256 * (B[0] % 2):256 * (B[0] % 2) + 256], cm, 0, 256, -256.0)
     b = add_up(T.cs[:, 256 * (B[1] % 2):256 * (B[1] % 2) + 256], cm, 512, 256, -256.0)
-    wait("v", d)
+    d = cell(3, 3, 1280)
+    wait("v", c)
     c = add_up(T.cs[:, 512:640], cm, 1024, 128, 0.0)
-    d = add_up(T.cs[:, 640:768], cm, 1280, 128, 0.0)
     shift = 0.0 if odd else 16.0
     wait("v", b)
     V(v.tensor_scalar(T.pu1[:, c01:c01 + 2], T.cs[:, 255:512:256], 256.0 + shift, None, OP.add))
+    wait("v", d)
+    d = add_up(T.cs[:, 640:768], cm, 1280, 128, 0.0)
     wait("v", c, kl[2])
     V(v.tensor_scalar(T.pu1[:, B[2]:B[2] + 1], T.cs[:, 639:640], T.ls[:, 2:3], shift, OP.add, OP.add))
     wait("v", d, kl[3])
     k_pu = V(v.tensor_scalar(T.pu1[:, B[3]:B[3] + 1], T.cs[:, 767:768], T.ls[:, 3:4], shift, OP.add, OP.add))
 
-    def invert(n, ready, cols, vals, lo, lift, fill=None):
+    def over_blocks(out, mid, src, fill):
+        a = V(v.tensor_tensor(mid[0:64, 0:9], src(0, 64), src(64, 128), OP.add))
+        fill(3)
+        wait("v", a)
+        for h in range(4):
+            a = V(v.tensor_tensor(out[32 * h:32 * h + 32, 0:9], mid[0:32, 0:9], mid[32:64, 0:9], OP.add))
+        return a
+
+    def invert(n, ready, cols, vals, lo, lift, fill):
         W = lambda b: T[b + n]
         wait("v", *ready)
         a = V(v.tensor_copy(W("win")[:, 0:528].indirect(W("pu")[:, 0:cols]), vals[:, 0:16 * cols]))
-        if fill:
-            fill()
+        fill(0)
         wait("v", a)
         V(v.transpose(W("tz")[:, 0:128], W("win")[:, lo:lo + 128]))
         a = V(v.transpose(W("tz")[:, 128:288], W("win")[:, lo - 16:lo + 144]))
+        fill(1)
         wait("v", a)
         a = V(v.tensor_tensor(W("qa")[:, 0:9], W("tz")[:, 0:288:32], W("tz")[:, 16:288:32], OP.add))
+        fill(2)
         wait("v", a)
-        a = V(v.tensor_tensor(W("qb")[0:64, 0:9], W("qa")[0:64, 0:9], W("qa")[64:128, 0:9], OP.add))
+        a = over_blocks(W("qc"), W("qb"), lambda p, q: W("qa")[p:q, 0:9], fill)
+        fill(4)
         wait("v", a)
-        for h in range(4):
-            a = V(v.tensor_tensor(W("qc")[32 * h:32 * h + 32, 0:9], W("qb")[0:32, 0:9], W("qb")[32:64, 0:9], OP.add))
-        wait("v", a, k_go)
-        return a, V(v.tensor_scalar(W("lst")[:, 0:16], W("qc")[:, 0:9].indirect(T.goff[:, 0:1]), lift, None, OP.add))
+        b = V(v.tensor_scalar(W("lst")[:, 0:16], W("qc")[:, 0:9].indirect(T.goff[:, 0:1]), lift, None, OP.add))
+        fill(5)
+        return a, b
 
     def pick(dc, ds, sc, ss, off, ready_c, ready_s):
         wait("v", *ready_c)
@@ -298,12 +294,44 @@ def rank_program(g, core, T, topo):
         wait("g", b)
         return kc, remote(out_s, in_s, dst, sem_s)
 
-    m0, m1 = SLOT * rank, SLOT * (rank ^ 1)
+    k_gt = []
+
+    def last_list(i):
+        if i == 0:
+            wait("v", k_gr)
+            k_gt.append(V(v.transpose(T.gt[:, 0:32], T.gr[:, 0:32])))
+        elif i == 1:
+            wait("v", *k_gt)
+            V(v.tensor_scalar(T.goff[:, 0:2], T.gt[:, 0:2], 1.0 / 32, None, OP.mult))
+
+    def w_codes(o):
+        wait("v", dw)
+        return V(v.quantize_mx(T.wq[:, 128 * o:128 * o + 128], T.ws[:, 128 * o:128 * o + 128], T.wb[:, 512 * o:512 * o + 512]))
+
+    m0 = SLOT * rank
+    word = lambda rk, w: T.msg[:, SLOT * rk + w:SLOT * rk + w + 1]
     mate = T.cores[rank ^ 1]
+    wait("g", kp[3])
+    in_raw = remote(T.spm[:, 0:4], T.sp[:, 0:4], mate, "hr")
+    wait("g", k_one)
+    G(g.affine_select(T.seg[:, 0:224], T.seg[:, 0:224], [[0, 7], [1, 32]], OP.is_gt, 0.0, 0, 0))
     wait("g", k_pu)
     in_places = remote(T.pum[:, 0:4], T.pu1[:, 0:4], mate, "hp")
-    k_q1, k_l1 = invert("1", (k_pu, k_v1), 4, T.vals1, lo1, 256.0)
-    wait("s", k_q1, k_go)
+    wait("g", iota(T.rs[:, 0:128], [[0, 128]], 0, 0))
+    k_rs = G(g.affine_select(T.rs[:, 0:128], T.rs[:, 0:128], [[0, 8], [1, 16]], OP.is_gt, -2 * BIG, 0, 0))
+    S(s.activation(T.pcq[:, 0:1], T.pcf[:, 1:2], COPY, scale=1.0 / 128))
+    k = S(s.activation(T.pcq[:, 1:2], T.pcf[:, 0:1], COPY, scale=2.0))
+    for buf, a, n in ((T.winm, lom - 16, 160), (T.ow, 0, 32), (T.ow, 160, 96), (T.win2, 0, 160), (T.cp, 0, 64), (T.idr, 64, 192)):
+        S(s.activation(buf[:, a:a + n], T.thr[:, 128 * c01:128 * c01 + n], COPY, scale=0.0))
+    wait("s", k, k_i6)
+    S(s.activation(T.vals2[:, 0:32], T.i4[:, 0:32], IDENT, bias=T.pcq[:, 1:2]))
+    S(s.activation(T.jc[:, 0:16], T.i6[:, 0:16], IDENT, bias=T.pcq[:, 0:1], scale=1.0 / 128))
+    wait("s", in_raw)
+    for c in range(4):
+        k_vm = S(s.activation(T.valm[:, 16 * c:16 * c + 16], T.dg[:, 0:16], COPY, scale=T.spm[:, c:c + 1]))
+
+    k_q1, k_l1 = invert("1", (k_pu, k_v1), 4, T.vals1, lo1, 256.0, last_list)
+    wait("s", k_q1)
     S(s.activation(T.msg[:, m0 + 5:m0 + 21], T.qc1[:, 0:9].indirect(T.goff[:, 0:1]), COPY))
     a1, b1 = pick(T.c1[:, 0:K], T.s1[:, 0:K], T.xq[:, 0:512], T.xs[:, 0:512], T.lst1[:, 2:10], (k_l1,), (k_l1,))
     in1c, in1s = send(T.c1[:, K:2 * K], T.c1[:, 0:K], T.s1[:, K:2 * K], T.s1[:, 0:K], a1, b1, mate, "h1c", "h1s")
@@ -312,10 +340,15 @@ def rank_program(g, core, T, topo):
     kaf = X(t.matmul_mx(T.psf[:, 0:128], T.uq[:, 0:128], T.us[:, 0:128], T.c1[:, 0:128], T.s1[:, 0:128], True, True))
     kap = X(t.matmul_mx(T.psp[:, 0:128], T.c1[:, 0:128], T.s1[:, 0:128], T.uq0[:, 2:130], T.us0[:, 2:130], True, True))
     wait("s", kap)
-    k_m4 = S(s.activation(T.msg[:, m0 + 4:m0 + 5], T.psp[:, 0:1], COPY))
+    k_m4 = S(s.activation(word(rank, 4), T.psp[:, 0:1], COPY))
+    wait("v", in_places, k_vm, k_one)
+    a = V(v.tensor_copy(T.winm[:, 0:528].indirect(T.pum[:, 0:4]), T.valm[:, 0:64]))
+    k_co = V(v.tensor_copy(T.eoff[:, 0:16], T.i5[:, 0:16]))
     wait("v", kaf)
-    a2 = V(v.transpose(T.at[:, 0:128], T.psf[:, 0:128]))
-    wait("v", a2)
+    b = V(v.transpose(T.at[:, 0:128], T.psf[:, 0:128]))
+    wait("v", a)
+    k_t1 = V(v.transpose(T.tzm[:, 0:128], T.winm[:, lom:lom + 128]))
+    wait("v", b)
     k_msg = V(v.tensor_copy(T.msg[:, m0:m0 + 4], T.at[:, 0:128:32]))
     wait("g", k_msg, k_m4)
     ids, m = [], topo.mask(core, mate)
@@ -330,112 +363,120 @@ def rank_program(g, core, T, topo):
                        local_sem=T.sem["sent"])
     in_msg = ("hm", 2 * n)
     count["sent"] += n
-
-    wait("v", k_zero)
-    k_am = V(v.tensor_tensor(T.am[:, 0:128], T.nb[:, 0:128], T.psf[:, 0:128], OP.add))
-    k_co = V(v.tensor_copy(T.eoff[:, 0:16], T.i5[:, 0:16]))
-    wait("v", dw)
-    k_w = V(v.quantize_mx(T.wq[:, 0:256], T.ws[:, 0:256], T.wb[:, 0:1024]))
-    wait("v", in_places)
-    a = V(v.tensor_copy(T.winm[:, 0:528].indirect(T.pum[:, 0:4]), T.vals1[:, 0:64]))
-    wait("v", a)
-    a = V(v.transpose(T.tzm[:, 0:128], T.winm[:, lom:lom + 128]))
-    k_hs = V(v.tensor_scalar(T.hs[:, 0:128:16], T.i6[:, 0:8], T.pcq[:, 0:1], 1.0 / 128, OP.add, OP.mult))
-    wait("v", a)
-    a = V(v.tensor_tensor(T.qam[:, 0:4], T.tzm[:, 0:128:32], T.tzm[:, 16:128:32], OP.add))
-    wait("v", a)
-    a = V(v.tensor_tensor(T.qbm[0:64, 0:4], T.qam[0:64, 0:4], T.qam[64:128, 0:4], OP.add))
-    wait("v", a)
-    for h in range(4):
-        k_im = V(v.tensor_tensor(T.msg[32 * h:32 * h + 32, m1 + 5:m1 + 6], T.qbm[0:32, h:h + 1], T.qbm[32:64, h:h + 1], OP.add))
+    in_ids = remote(word(rank, 5), word(rank, 5), mate, "hi")
 
     fr = (T.psf[:, 512:640], T.psf[:, 0:128]) if odd else (T.psf[:, 0:128], T.psf[:, 512:640])
+    ps, nsel = [[T[b][:, j:j + 1] for j in range(2)] for b in ("ps", "nsel")]
+    sel = [T.cp[:, 0:1], T.sel[:, 0:1]]
+    a = V(v.transpose(T.tzm[:, 128:288], T.winm[:, lom - 16:lom + 144]))
+    b = V(v.tensor_tensor(T.am[:, 0:128], T.nb[:, 0:128], T.psf[:, 0:128], OP.add))
+    wait("v", a, k_rs)
+    a = V(v.tensor_tensor_scan(T.qam[:, 64:288], T.seg[:, 0:224], T.tzm[:, 64:288], 0.0, OP.mult, OP.add))
+    wait("s", k_t1)
+    for h in range(2):
+        k = S(s.activation(T.qam[:, 288 + 32 * h:320 + 32 * h], T.tzm[:, 32 * h:32 * h + 32], COPY,
+                           accum_out=T.qam[:, 32 * h + 31:32 * h + 32]))
+    wait("v", b)
+    V(v.tensor_tensor_scan(T.ow[:, 32:160], T.rs[:, 0:128], T.am[:, 0:128], 0.0, OP.add, OP.max))
+    wait("v", a, k)
+    a = over_blocks(T.qcm, T.qbm, lambda p, q: T.qam[p:q, 31:288:32], lambda i: None)
+    k_w = [w_codes(0)]
+    wait("s", a)
+    k_ml = S(s.activation(T.ml[:, 0:16], T.qcm[:, 0:9].indirect(T.goff[:, 0:1]), COPY))
+    wait("v", a)
+    a = V(v.tensor_tensor(T.bc[:, 0:16], T.qcm[:, 0:9].indirect(T.goff[:, 0:1]), T.ow[:, 15:256:16], OP.is_ge if odd else OP.is_gt))
+    k_w.append(w_codes(1))
+    wait("v", a)
+    a = V(v.tensor_tensor(T.bs[:, 0:16], T.bc[:, 0:16], T.jc[:, 0:16], OP.add))
+    E, O = (T.ml[:, 0:1], word(rank, 4)) if odd else (word(rank, 4), T.ml[:, 0:1])
+    wait("v", k_ml, k_m4)
+    b = V(v.tensor_tensor(sel[P], O, E, OP.is_gt))
+    V(v.tensor_tensor(nsel[P], E, O, OP.is_ge))
+    wait("v", a)
+    k_o2 = V(v.tensor_scalar(T.off2[:, 0:16], T.bs[:, 0:16], 128.0, None, OP.mult))
+    V(v.tensor_tensor(ps[P], E, O, OP.max))
+    wait("v", b)
+    k_sp = V(v.tensor_scalar(T.kc[:, P:P + 1], sel[P], T.pt[:, 1:2], T.pt[:, 0:1], OP.mult, OP.add))
+
     wait("t", in1c, in1s)
     kb = X(t.matmul_mx(T.psf[:, 512:640], T.uq[:, 0:128], T.us[:, 0:128], T.c1[:, 128:256], T.s1[:, 128:256], True, True))
-    kbp = X(t.matmul_mx(T.psp[:, 512:640], T.c1[:, 128:256], T.s1[:, 128:256], T.uq0[:, 2:130], T.us0[:, 2:130], True, True))
     kbs = X(t.matmul_mx(T.psp[:, 1024:1280], T.uq[:, 0:128], T.us[:, 0:128], T.c1[:, 0:256], T.s1[:, 0:256], True, True))
-    wait("s", kbp)
-    k_m4 = S(s.activation(T.msg[:, m1 + 4:m1 + 5], T.psp[:, 512:513], COPY))
     wait("s", in_msg, k_co)
     ky = S(s.activation(T.yx[:, 0:256], T.msg[:, 2 * SLOT * Q:2 * SLOT * (Q + 1)].indirect(T.eoff[:, 0:16]), COPY))
-    wait("v", kb, k_am)
-    a = V(v.tensor_tensor(T.bc[:, 0:128], T.am[:, 0:128], T.psf[:, 512:640], OP.is_gt if odd else OP.is_ge))
-    wait("v", a, k_hs)
-    a = V(v.tensor_tensor_scan(T.bs[:, 0:128], T.hs[:, 0:128], T.bc[:, 0:128], 0.0, OP.max, OP.subtract))
-    wait("v", a)
-    k_o2 = V(v.tensor_scalar(T.off2[:, 0:8], T.bs[:, 15:128:16], 128.0, None, OP.mult))
-    a2, b2 = pick(T.c2[:, own], T.s2[:, own], T.c1[:, 0:256], T.s1[:, 0:256], T.off2[:, 0:8], (k_o2, in1c), (k_o2, in1s))
+    a2, b2 = pick(T.c2[:, own], T.s2[:, own], T.c1[:, 0:256], T.s1[:, 0:256], T.off2[:, 2:10], (k_o2, in1c), (k_o2, in1s))
     in2c, in2s = send(T.c2[:, own], T.c2[:, own], T.s2[:, own], T.s2[:, own], a2, b2, T.cores[rank ^ 2], "h2c", "h2s")
 
     def products(side, bank, *ready):
-        wait("t", k_w, *ready)
+        wait("t", *k_w, *ready)
         return [X(t.matmul_mx(bank[:, 512 * (o + 2):512 * (o + 2) + 128], T.wq[:, 128 * o:128 * o + 128], T.ws[:, 128 * o:128 * o + 128],
                               T.c2[:, side], T.s2[:, side], True, True)) for o in range(2)]
     ko = products(own, T.psf, a2, b2)
 
-    word = lambda rk, w: T.msg[:, SLOT * rk + w:SLOT * rk + w + 1]
-    E, O = T.msg[:, 4:4 * SLOT:2 * SLOT], T.msg[:, SLOT + 4:4 * SLOT:2 * SLOT]
-    ps, sel, nsel = [[T[b][:, j:j + 1] for j in range(2)] for b in ("ps", "sel", "nsel")]
-    wait("v", in_msg, k_m4)
-    a = V(v.tensor_tensor(T.ps[:, 0:2], E, O, OP.max))
-    k_sel = V(v.tensor_tensor(T.sel[:, 0:2], O, E, OP.is_gt))
-    b = V(v.tensor_tensor(T.nsel[:, 0:2], E, O, OP.is_ge))
-    wait("s", a, kbs)
-    ks = S(s.activation(T.sq[:, 0:256], T.psp[:, 1024:1280], ACT.Sign, bias=ps[Q], scale=-1.0))
-    wait("s", k_sel)
-    for j in range(2):
-        kc = S(s.activation(T.kc[:, j:j + 1], sel[j], IDENT, bias=T.pt[:, 0:1], scale=T.pt[:, 1:2]))
-    wait("s", ks)
-    kq2 = S(s.activation(T.sq[:, 256:512], T.sq[:, 0:256], ACT.Relu, scale=1.0 if P < Q else -1.0, accum_out=T.lq[:, 0:1]))
-    wait("t", ks)
-    kr = products(arr, T.psp, in2c, in2s)
-    wait("s", k_im)
-    for j in range(2):
-        k = S(s.activation(T.vd[:, j:j + 1], word(2 * j, 5), IDENT, bias=word(2 * j + 1, 5), scale=-1.0))
-    wait("s", k)
-    for j in range(2):
-        S(s.activation(T.cp[:, 32 * j:32 * j + 1], sel[j], IDENT, bias=2.0 * j))
-        kcp = S(s.activation(T.cp[:, 32 * j + 1:32 * j + 2], T.vd[:, j:j + 1], IDENT, bias=word(2 * j, 5), scale=sel[j]))
+    E, O = word(2 * Q, 4), word(2 * Q + 1, 4)
+    wait("v", in_msg)
+    a = V(v.tensor_tensor(ps[Q], E, O, OP.max))
+    wait("v", kb, k_sp)
+    cmp(T.ba[:, 0:128], fr[1], ps[P], OP.is_gt, nsel[P])
     wait("v", ky)
     kf = V(v.transpose(T.fs[:, 0:256], T.yx[:, 0:256]))
-    wait("v", b)
-    cmp(T.ba[:, 0:128], fr[1], ps[P], OP.is_gt, nsel[P])
+    k_sq = V(v.tensor_tensor(sel[Q], O, E, OP.is_gt))
+    k_nq = V(v.tensor_tensor(nsel[Q], E, O, OP.is_ge))
     cmp(T.ba[:, 128:256], fr[0], ps[P], OP.is_ge, sel[P])
+    wait("s", a, kbs)
+    ks = S(s.activation(T.sq[:, 0:256], T.psp[:, 1024:1280], ACT.Sign, bias=ps[Q], scale=-1.0))
+    wait("s", kf)
+    k = S(s.activation(T.sq[:, 256:384], T.fs[:, 0:128], ACT.Sign, bias=ps[Q], scale=-1.0))
+    wait("s", ks, k_sq)
+    kc = S(s.activation(T.kc[:, Q:Q + 1], sel[Q], IDENT, bias=T.pt[:, 4:5], scale=T.pt[:, 3:4]))
+    S(s.activation(T.sq[:, 384:640], T.sq[:, 0:256], ACT.Relu, scale=1.0 if P < Q else -1.0, accum_out=T.lq[:, 0:1]))
+    wait("s", k)
+    kq2 = S(s.activation(T.sq[:, 640:768], T.sq[:, 256:384], ACT.Relu, scale=sel[Q], accum_out=T.lq[:, 1:2]))
+    wait("t", ks)
+    kn = products(arr, T.psp, in2c, in2s)
     wait("v", kf)
     a = cmp(T.ba[:, 256:512], T.fs[:, 0:256], ps[P], OP.is_ge if Q < P else OP.is_gt)
-    cmp(T.bb[:, 0:128], T.fs[:, 128:256], ps[Q], OP.is_gt, nsel[Q])
-    b = cmp(T.bb[:, 128:256], T.fs[:, 0:128], ps[Q], OP.is_ge, sel[Q])
+    wait("v", k_nq)
+    b = cmp(T.bb[:, 0:128], T.fs[:, 128:256], ps[Q], OP.is_gt, nsel[Q])
     wait("v", a, kc)
     a = add_up(T.bt[:, 0:256], T.ba, 0, 256, T.kc[:, P:P + 1])
     wait("v", b)
-    b = add_up(T.bt[:, 256:384], T.bb, 0, 128, T.kc[:, Q:Q + 1])
+    b = add_up(T.bu[:, 0:64], T.bb, 0, 64, T.kc[:, Q:Q + 1])
     wait("v", a)
     V(v.tensor_scalar(T.pu2[:, P:P + 1], T.bt[:, 255:256], 144.0, None, OP.add))
     wait("v", b, kq2)
-    kv = V(v.tensor_scalar(T.pu2[:, Q:Q + 1], T.bt[:, 383:384], T.lq[:, 0:1], 400.0 if P < Q else 144.0,
-                           OP.subtract if P < Q else OP.add, OP.add))
+    kv = V(v.tensor_scalar(T.pu2[:, Q:Q + 1], T.bu[:, 63:64], T.lq[:, 1:2], T.lq[:, 0:1], OP.subtract, OP.subtract if P < Q else OP.add))
 
+    wait("s", in_ids)
+    for j in range(2):
+        k = S(s.activation(T.vd[:, j:j + 1], word(2 * j, 5), IDENT, bias=word(2 * j + 1, 5), scale=-1.0))
+    S(s.activation(T.cp[:, 32:33], sel[1], IDENT, bias=2.0))
+    wait("s", k)
+    for j in range(2):
+        kcp = S(s.activation(T.cp[:, 32 * j + 1:32 * j + 2], T.vd[:, j:j + 1], IDENT, bias=word(2 * j, 5), scale=sel[j]))
     yw = (T.yw0, T.yw1)
-    for o in range(2):
-        wait("s", ko[o])
-        S(s.activation(yw[o][:, P:256:2], T.psf[:, 512 * (o + 2):512 * (o + 2) + 128], COPY))
+    wait("s", ko[1])
+    S(s.activation(T.yw1[:, P:256:2], T.psf[:, 1536:1664], COPY))
     kz = []
 
-    def numbers():
-        wait("v", kcp)
-        for j in range(2):
-            kz.append(V(v.transpose(T.idr[:, j:64:2], T.cp[:, 32 * j:32 * j + 32])))
+    def numbers(i):
+        if i == 0:
+            wait("v", ko[0])
+            V(v.tensor_copy(T.yw0[:, P:256:2], T.psf[:, 1024:1152]))
+        elif i < 3:
+            wait("v", kcp)
+            kz.append(V(v.transpose(T.idr[:, i - 1:64:2], T.cp[:, 32 * i - 32:32 * i])))
+        else:
+            wait("v", kz[1])
+            kz.append(V(v.tensor_copy(T.idr[0:2, 64 * i - 128:64 * i - 64], T.idr[32 * i - 64:32 * i - 62, 0:64])))
     k_q2, k_l2 = invert("2", (kv,), 2, T.vals2, 16, 128.0, numbers)
-    wait("s", *kz)
-    for a in range(1, 4):
-        S(s.activation(T.idr[0:2, 64 * a:64 * a + 64], T.idr[32 * a:32 * a + 2, 0:64], COPY))
     for o in range(2):
-        wait("s", kr[o])
+        wait("s", kn[o])
         kyw = S(s.activation(yw[o][:, Q:256:2], T.psp[:, 512 * (o + 2):512 * (o + 2) + 128], COPY))
 
     off = T.lst2[:, 2:10]
     wait("v", k_l2, kyw)
     ky0 = V(v.tensor_copy(T.yb[:, 0:128], T.yw0[:, 0:256].indirect(off)))
+    wait("v", *kz)
     ki = V(v.tensor_scalar(T.idb[:, 0:128], T.idr[:, 0:256].indirect(off), T.pt[:, 2:3], None, OP.add))
     wait("s", k_l2, kyw)
     ky1 = S(s.activation(T.yb[:, 128:256], T.yw1[:, 0:256].indirect(off), COPY))
@@ -443,5 +484,5 @@ def rank_program(g, core, T, topo):
     d0 = done(y.dma_start(T.y[:, 0:256], T.yb[:, 0:256]), "dy", 16)
     wait("s", ki)
     d2 = done(s.dma_start(T["id"][0:2, 0:128], T.idb[0:2, 0:128]), "did", 16)
-    wait("g", ("sent", count["sent"]), in1c, in1s, in2c, in2s, in_msg, in_places, du, *dx.values(), dw,
+    wait("g", ("sent", count["sent"]), in1c, in1s, in2c, in2s, in_msg, in_raw, in_places, in_ids, du, *dx.values(), dw,
          ("gc", count["gc"]), ("v", count["v"]), ("s", count["s"]), ("t", count["t"]), d0, d2)

@@ -8,7 +8,11 @@ K = 128
 BIG = 1e29
 STEP = 1.25 * 2.0 ** -24
 TINY = 2.0 ** -122
-SLOT = 24
+SLOT = 4
+
+OPT = {"q0": True, "three": False, "scal": [(2, 0), (3, 0), (3, 1)],
+       "order": "d0 r0 q1 d1 s0 r1 b0 b1 q2 z0 d2 r2 q3 z1 d3 s2 r3 c10 c01 c02 c00 c12 c11 c21 g20 b2 g30 b3 g31 l2 l3 "
+                "c03 c13 c23 c32 c22 t0 c33 t1 t2 t3 p02 p2 p3"}
 
 SCRATCH = {
     "ur": ("sbuf", [128, 520], "bfloat16"), "zoff": ("sbuf", [128, 8], "uint16"),
@@ -25,42 +29,41 @@ SCRATCH = {
     "psf": ("psum", [128, 2048], "float32"),
     "psp": ("psum", [128, 2048], "float32"),
     "ip": ("sbuf", [128, 2], "int32"), "pt": ("sbuf", [128, 8], "float32"),
-    "it": ("sbuf", [128, 128], "int32"), "ita": ("sbuf", [128, 128], "int32"), "tri": ("sbuf", [128, 128], "float32"),
-    "nb": ("sbuf", [128, 128], "float32"),
+    "it": ("sbuf", [128, 128], "int32"), "ita": ("sbuf", [128, 16], "int32"), "tri": ("sbuf", [128, 128], "float32"),
+    "nb": ("sbuf", [128, 16], "float32"), "dg": ("sbuf", [128, 16], "float32"), "seg": ("sbuf", [128, 128], "float32"),
     "i3": ("sbuf", [128, 64], "float32"), "vals1": ("sbuf", [128, 64], "bfloat16"),
     "i4": ("sbuf", [128, 32], "float32"), "vals2": ("sbuf", [128, 32], "bfloat16"),
-    "i5": ("sbuf", [128, 16], "int32"), "eoff": ("sbuf", [128, 16], "uint16"),
-    "i6": ("sbuf", [128, 16], "float32"), "jc": ("sbuf", [128, 16], "float32"), "dg": ("sbuf", [128, 16], "float32"),
-    "seg": ("sbuf", [128, 224], "float32"), "rs": ("sbuf", [128, 128], "float32"),
-    "gr": ("sbuf", [128, 32], "float32"), "gt": ("sbuf", [128, 32], "float32"), "goff": ("sbuf", [128, 2], "uint16"),
+    "i5": ("sbuf", [128, 16], "int32"), "eoff": ("sbuf", [128, 20], "uint16"),
+    "i6": ("sbuf", [128, 8], "float32"), "jt": ("sbuf", [128, 8], "float32"), "jc": ("sbuf", [128, 8], "float32"),
+    "gr": ("sbuf", [128, 96], "float32"), "gt": ("sbuf", [128, 96], "float32"), "goff": ("sbuf", [128, 2], "uint16"),
     "pca": ("sbuf", [128, 2], "int32"), "pcf": ("sbuf", [128, 2], "float32"), "pcq": ("sbuf", [128, 2], "float32"),
     "sp": ("sbuf", [128, 4], "float32"), "dl": ("sbuf", [128, 4], "float32"), "thr": ("sbuf", [128, 512], "float32"),
-    "cm": ("sbuf", [128, 1536], "bfloat16"), "cs": ("sbuf", [128, 768], "bfloat16"),
+    "cm": ("sbuf", [128, 2048], "bfloat16"), "cs": ("sbuf", [128, 1024], "bfloat16"),
     "sg": ("sbuf", [128, 512], "bfloat16"), "junk": ("sbuf", [128, 512], "bfloat16"), "ls": ("sbuf", [128, 4], "float32"),
-    "msg": ("sbuf", [128, 4 * SLOT], "float32"), "at": ("sbuf", [128, 128], "float32"),
+    "raw": ("sbuf", [128, 512], "float32"), "valo": ("sbuf", [128, 64], "float32"),
+    "wins": ("sbuf", [128, 528], "float32"), "tzs": ("sbuf", [128, 128], "float32"),
+    "msg": ("sbuf", [128, 16], "float32"), "cu": ("sbuf", [128, 4], "uint16"), "cf": ("sbuf", [128, 4], "float32"), "at": ("sbuf", [128, 20], "float32"),
     "spm": ("sbuf", [128, 4], "float32"), "pum": ("sbuf", [128, 8], "uint16"), "valm": ("sbuf", [128, 64], "float32"),
-    "winm": ("sbuf", [128, 528], "float32"), "tzm": ("sbuf", [128, 288], "float32"), "qam": ("sbuf", [128, 416], "float32"),
-    "qbm": ("sbuf", [64, 16], "float32"), "qcm": ("sbuf", [128, 16], "float32"), "ml": ("sbuf", [128, 16], "float32"),
-    "am": ("sbuf", [128, 128], "float32"), "ow": ("sbuf", [128, 256], "float32"),
-    "bc": ("sbuf", [128, 16], "float32"), "bs": ("sbuf", [128, 16], "float32"), "off2": ("sbuf", [128, 16], "uint16"),
-    "yx": ("sbuf", [128, 256], "float32"), "fs": ("sbuf", [128, 256], "float32"),
-    "ps": ("sbuf", [128, 2], "float32"), "sel": ("sbuf", [128, 2], "float32"), "nsel": ("sbuf", [128, 2], "float32"),
-    "vd": ("sbuf", [128, 2], "float32"), "kc": ("sbuf", [128, 2], "float32"),
-    "ba": ("sbuf", [128, 512], "bfloat16"), "bb": ("sbuf", [128, 128], "bfloat16"), "bt": ("sbuf", [128, 256], "bfloat16"),
-    "bu": ("sbuf", [128, 64], "float32"), "sq": ("sbuf", [128, 768], "bfloat16"), "lq": ("sbuf", [128, 2], "float32"),
+    "osr": ("sbuf", [128, 528], "float32"), "cb": ("sbuf", [128, 96], "bfloat16"), "cr": ("sbuf", [64, 96], "bfloat16"),
+    "ct": ("sbuf", [64, 32], "bfloat16"), "cn": ("sbuf", [64, 32], "float32"),
+    "bc": ("sbuf", [128, 8], "float32"), "bs": ("sbuf", [128, 8], "float32"), "off2": ("sbuf", [128, 8], "uint16"),
+    "yx": ("sbuf", [128, 272], "float32"), "fs": ("sbuf", [128, 256], "float32"),
+    "ps": ("sbuf", [128, 2], "float32"), "sel": ("sbuf", [128, 2], "float32"), "vd": ("sbuf", [128, 2], "float32"),
+    "ba": ("sbuf", [128, 768], "bfloat16"), "bu": ("sbuf", [128, 400], "float32"),
+    "sq": ("sbuf", [128, 528], "bfloat16"), "lq": ("sbuf", [128, 2], "float32"),
     "cp": ("sbuf", [128, 64], "float32"), "idr": ("sbuf", [128, 256], "float32"), "idb": ("sbuf", [128, 128], "float32"),
 }
 for _n in ("1", "2"):
     SCRATCH["pu" + _n] = ("sbuf", [128, 4], "uint16")
     SCRATCH["win" + _n] = ("sbuf", [128, 528], "bfloat16")
     SCRATCH["tz" + _n] = ("sbuf", [128, 288], "bfloat16")
-    SCRATCH["qa" + _n] = ("sbuf", [128, 16], "float32")
+    SCRATCH["qa" + _n] = ("sbuf", [128, 416], "float32")
     SCRATCH["qb" + _n] = ("sbuf", [64, 16], "float32")
     SCRATCH["qc" + _n] = ("sbuf", [128, 16], "float32")
     SCRATCH["lst" + _n] = ("sbuf", [128, 16], "uint16")
 
 SEMAPHORES = ["v", "s", "t", "gc", "du", "dx0", "dx1", "dx2", "dx3", "dw", "dy", "did",
-              "h1c", "h1s", "h2c", "h2s", "hm", "hr", "hp", "hi", "sent"]
+              "h1c", "h1s", "h2c", "h2s", "hm", "hr", "hq", "hp", "hi", "sent"]
 
 
 def rank_program(g, core, T, topo):
@@ -106,58 +109,77 @@ def rank_program(g, core, T, topo):
     k_ip = iota(T.ip[:, 0:2], [[0, 2]], 0, 1, False)
     k_i3 = iota(T.i3[:, 0:64], [[128, 4], [1, 16]], -256, 0)
     k_i4 = iota(T.i4[:, 0:32], [[1, 2], [2, 16]], -128, 0)
-    wait("g", iota(T.gr[:, 0:32], [[0, 32]], 0, 1))
+    k_i6 = iota(T.i6[:, 0:8], [[16, 8]], 0, 0)
+    iota(T.seg[:, 0:128], [[0, 128]], 1, 0)
+    k = iota(T.gr[:, 0:32], [[0, 32]], 0, 1)
+    iota(T.gr[:, 32:64], [[0, 8], [64 * SLOT, 2], [32 * SLOT, 2]] if False else [[0, 8], [128, 4]] if OPT["three"] else [[0, 16], [128, 2]], 0, 1)
+    iota(T.gr[:, 64:96], [[0, 16], [32 * 9, 2]], 0, 1)
+    wait("g", k)
     iota(T.gr[:, 2:10], [[32, 4], [160, 2]], 0, 0)
     k_gr = iota(T.gr[:, 18:26], [[32, 4], [-128, 2]], 128, 0)
-    k_i6 = iota(T.i6[:, 0:16], [[16, 16]], -32, 0)
-    iota(T.i5[:, 0:16], [[SLOT, 2], [1, 4], [0, 2]], 0, 0, False)
-    for i, (base, step) in enumerate(((-128, 1), (127, -2), (0, 256), (255, -2), (272 if P < Q else 16, 1))):
-        iota(T.pt[:, i:i + 1], [[0, 1]], base, step)
-    k_one = iota(T.seg[:, 0:224], [[0, 224]], 1, 0)
+    k_seg = iota(T.seg[:, 0:128:32], [[0, 4]], 0, 0)
     lo1, lom = (384, 16) if odd else (16, 384)
 
     V(v.memset(T.ur[:, 0:8], 0.0))
     k_ur = V(v.memset(T.ur[:, 16:520], 0.0))
     k_zo = V(v.memset(T.zoff[:, 0:8], 2))
     V(v.memset(T.win1[:, lo1 - 16:lo1 + 144], 0.0))
+    wait("s", k_ur)
+    for a, b in ((0, lom), (lom + K, 528)):
+        S(s.activation(T.osr[:, a:b], T.ur[:, 16:16 + b - a], IDENT, bias=BIG))
+    S(s.activation(T.wins[:, lo1:lo1 + K], T.ur[:, 16:16 + K], COPY))
     wait("v", k_it)
     if odd:
         k_tri = V(v.tensor_scalar(T.tri[:, 0:128], T.it[:, 0:128], 128.0, None, OP.is_gt))
     else:
         k_tri = V(v.tensor_scalar(T.tri[:, 0:128], T.it[:, 0:128], 128.0, -1.0, OP.is_lt, OP.mult))
-    V(v.tensor_scalar(T.ita[:, 0:128], T.it[:, 0:128], 15, None, OP.bitwise_and))
+    V(v.tensor_scalar(T.ita[:, 0:16], T.it[:, 0:16], 15, None, OP.bitwise_and))
     wait("v", k_ip)
     V(v.tensor_scalar(T.pca[:, 0:1], T.ip[:, 0:1], 112, None, OP.bitwise_and))
     k = V(v.tensor_scalar(T.pca[:, 1:2], T.ip[:, 0:1], 15, None, OP.bitwise_and))
+    V(v.memset(T.win2[:, 0:160], 0.0))
+    V(v.memset(T.cb[:, 64:96], 0.0))
+    V(v.memset(T.cp[:, 0:64], 0.0))
     wait("v", k)
     k_pc = V(v.tensor_copy(T.pcf[:, 0:2], T.pca[:, 0:2]))
-    V(v.tensor_scalar(T.nb[:, 0:128], T.ita[:, 0:128], 0.0, -BIG, OP.not_equal, OP.mult))
-    V(v.tensor_scalar(T.dg[:, 0:16], T.ita[:, 0:16], 0.0, None, OP.is_equal))
+    V(v.tensor_scalar(T.nb[:, 0:16], T.ita[:, 0:16], 0.0, -BIG, OP.not_equal, OP.mult))
+    k_nb = V(v.tensor_scalar(T.dg[:, 0:16], T.ita[:, 0:16], 0.0, None, OP.is_equal))
+    wait("s", k_pc, k_i3)
+    k = S(s.activation(T.pcq[:, 1:2], T.pcf[:, 0:1], COPY, scale=2.0))
+    k_v1 = S(s.activation(T.vals1[:, 0:64], T.i3[:, 0:64], IDENT, bias=T.pcf[:, 0:1]))
 
     wait("v", du, k_ur)
     k_u0 = V(v.quantize_mx(T.uq0[:, 0:130], T.us0[:, 0:130], T.ur[:, 0:520]))
-    wait("v", k_u0, k_zo)
-    k_uc = V(v.tensor_copy(T.uq[:, 0:128].bitcast(dt.uint32), T.uq0[:, 0:130].bitcast(dt.uint32).indirect(T.zoff[:, 0:8])))
-    wait("s", k_u0)
-    k_us = S(s.activation(T.us[:, 0:128], T.us0[:, 0:130].indirect(T.zoff[:, 0:8]), COPY))
-    wait("s", k_i3, k_pc)
-    k_v1 = S(s.activation(T.vals1[:, 0:64], T.i3[:, 0:64], IDENT, bias=T.pcf[:, 0:1]))
-
-    kq, kr, kp, kt, kl = {}, {}, {}, {}, {}
-    strict, loose = (OP.is_lt, OP.is_le) if odd else (OP.is_gt, OP.is_ge)
-    row = [T.psf[:, 512 * d:512 * d + 128] for d in range(4)]
-    sp = [T.sp[:, c:c + 1] for c in range(4)]
-    cm = T.cm
+    kq = {}
 
     def quant(i):
         d = B[i]
         wait("v", dx[d])
         kq[d] = V(v.quantize_mx(T.xq[:, 128 * d:128 * d + 128], T.xs[:, 128 * d:128 * d + 128], T.xb[:, 512 * d:512 * d + 512]))
+    if OPT["q0"]:
+        quant(0)
+    wait("v", k_u0, k_zo)
+    k_uc = V(v.tensor_copy(T.uq[:, 0:128].bitcast(dt.uint32), T.uq0[:, 0:130].bitcast(dt.uint32).indirect(T.zoff[:, 0:8])))
+    if not OPT["q0"]:
+        quant(0)
+    wait("s", k_u0, k_zo)
+    k_us = S(s.activation(T.us[:, 0:128], T.us0[:, 0:130].indirect(T.zoff[:, 0:8]), COPY))
+    wait("s", k, k_i6)
+    k = S(s.activation(T.jt[:, 0:8], T.i6[:, 0:8], IDENT, bias=T.pcf[:, 1:2]))
+    S(s.activation(T.vals2[:, 0:32], T.i4[:, 0:32], IDENT, bias=T.pcq[:, 1:2]))
+    wait("s", k)
+    S(s.activation(T.jc[:, 0:8], T.jt[:, 0:8], COPY, scale=1.0 / 128))
 
-    def along(out, d, n):
-        e = slice(128 * d, 128 * (d + n))
-        wait("t", k_uc, k_us, *[kq[c] for c in range(d, d + n)])
-        return X(t.matmul_mx(out, T.uq[:, 0:128], T.us[:, 0:128], T.xq[:, e], T.xs[:, e], True, True))
+    kr, kp, kt, kl, kc, ks = {}, {}, {}, {}, {}, {}
+    strict, loose = (OP.is_lt, OP.is_le) if odd else (OP.is_gt, OP.is_ge)
+    row = [T.psf[:, 512 * d:512 * d + 128] for d in range(4)]
+    sp = [T.sp[:, c:c + 1] for c in range(4)]
+    cm = T.cm
+
+    def rows(i):
+        e = slice(128 * B[i], 128 * B[i] + 128)
+        wait("t", k_uc, k_us, kq[B[i]])
+        kr[i] = X(t.matmul_mx(row[B[i]], T.uq[:, 0:128], T.us[:, 0:128], T.xq[:, e], T.xs[:, e], True, True))
 
     def down(i):
         c, bank = B[i], 512 * (i // 2)
@@ -176,85 +198,68 @@ def rank_program(g, core, T, topo):
         wait("s", k, k_tri)
         kt[i] = S(s.activation(T.thr[:, 128 * c:128 * c + 128], T.tri[:, 0:128], IDENT, bias=sp[c], scale=T.dl[:, c:c + 1]))
 
-    def rows(i):
-        kr[i] = along(row[B[i]], B[i], 1)
+    def cmp(out, src, col, op):
+        return V(v.tensor_scalar(out, src, col, None, op))
 
-    def cmp(out, src, col, op, weight=None):
-        if weight is None:
-            return V(v.tensor_scalar(out, src, col, None, op))
-        return V(v.tensor_scalar(out, src, col, weight, op, OP.mult))
+    SCAL = OPT["scal"]
+    mine_v = {i: [j for j in range(4) if (i, j) not in SCAL] for i in range(4)}
+    mine_s = {i: [j for j in range(4) if (i, j) in SCAL] for i in range(4)}
 
-    def cell(i, j, o):
-        c, d = B[i], B[j]
+    def cell(i, j):
+        c, d, o = B[i], B[j], 512 * i + 128 * mine_v[i].index(j)
         if i == j:
             wait("v", kr[j], kt[i])
-            return V(v.tensor_tensor(cm[:, o:o + 128], row[d], T.thr[:, 128 * c:128 * c + 128], strict))
-        wait("v", kr[j], kp[i])
-        return cmp(cm[:, o:o + 128], row[d], sp[c], loose if i < j else strict)
+            kc[i, j] = V(v.tensor_tensor(cm[:, o:o + 128], row[d], T.thr[:, 128 * c:128 * c + 128], strict))
+        else:
+            wait("v", kr[j], kp[i])
+            kc[i, j] = cmp(cm[:, o:o + 128], row[d], sp[c], loose if i < j else strict)
 
     def add_up(out, buf, o, n, first):
         return V(v.tensor_tensor_scan(out, buf[:, o:o + n], buf[:, o + n:o + 2 * n], first, OP.add, OP.add))
 
-    def signs(i, o):
-        wait("s", krs, kp[i])
-        return S(s.activation(T.sg[:, o:o + 256], T.psp[:, 1536:1792], ACT.Sign, bias=sp[B[i]], scale=-1.0))
+    def signs(i, j):
+        o = 256 * (i - 2) + 128 * mine_s[i].index(j)
+        wait("s", kp[i], *[kc[h, j] for h in range(4) if j in mine_v[h]])
+        ks[i] = S(s.activation(T.sg[:, o:o + 128], row[B[j]], ACT.Sign, bias=sp[B[i]], scale=-1.0))
 
-    def sum_signs(i, o, k):
-        wait("s", k)
-        kl[i] = S(s.activation(T.junk[:, o:o + 256], T.sg[:, o:o + 256], ACT.Relu, scale=1.0 if odd else -1.0,
-                               accum_out=T.ls[:, i:i + 1]))
+    def sum_signs(i):
+        o, n = 256 * (i - 2), 128 * len(mine_s[i])
+        wait("s", ks[i])
+        kl[i] = S(s.activation(T.junk[:, o:o + n], T.sg[:, o:o + n], ACT.Relu, scale=1.0 if odd else -1.0, accum_out=T.ls[:, i:i + 1]))
 
+    def total(i):
+        n, e = 64 * len(mine_v[i]), 256 * B[i] + 256
+        wait("v", *[kc[i, j] for j in mine_v[i]])
+        kn_[i] = add_up(T.cs[:, e - n:e], cm, 512 * i, n, -256.0)
+
+    def places(i, n=1):
+        c, lift = min(B[i:i + n]), 256.0 if odd else 272.0
+        wait("v", *[kn_[h] for h in range(i, i + n)])
+        src = T.cs[:, 256 * c + 255:256 * (c + n):256]
+        if mine_s[i]:
+            wait("v", kl[i])
+            kn_["pu"] = V(v.tensor_scalar(T.pu1[:, c:c + 1], src, T.ls[:, i:i + 1], lift, OP.add, OP.add))
+        else:
+            kn_["pu"] = V(v.tensor_scalar(T.pu1[:, c:c + n], src, lift, None, OP.add))
+
+    def lists(i):
+        if i == 0:
+            wait("v", k_gr)
+            kn_["gt"] = V(v.transpose(T.gt[:, 0:96], T.gr[:, 0:96]))
+        else:
+            wait("v", kn_["gt"])
+            V(v.tensor_scalar(T.goff[:, 0:2], T.gt[:, 0:2], 1.0 / 32, None, OP.mult))
+            V(v.tensor_scalar(T.eoff[:, 16:20:2], T.gt[:, 32:96:32], 1.0 / 32, None, OP.mult))
+
+    kn_, kd = {}, {}
     c01 = min(B[0:2])
-    quant(0)
-    down(0)
-    rows(0)
-    quant(1)
-    k = scores(0, down(1))
-    rows(1)
-    bound(0, k)
-    bound(1, k)
-    quant(2)
-    down(2)
-    rows(2)
-    quant(3)
-    k = scores(2, down(3))
-    krs = along(T.psp[:, 1536:1792], c01, 2)
-    rows(3)
-    k2 = signs(2, 0)
-    bound(2, k)
-    k3 = signs(3, 256)
-    bound(3, k)
-    sum_signs(2, 0, k2)
-    sum_signs(3, 256, k3)
-    for i, j, o in ((1, 0, 512), (0, 1, 0), (0, 2, 256), (0, 0, 128), (1, 2, 768), (1, 1, 640), (0, 3, 384), (1, 3, 896), (2, 3, 1152)):
-        b = cell(i, j, o)
-    cell(3, 2, 1408)
-    wait("v", b)
-    c = cell(2, 2, 1024)
-    add_up(T.cs[:, 256 * (B[0] % 2):256 * (B[0] % 2) + 256], cm, 0, 256, -256.0)
-    b = add_up(T.cs[:, 256 * (B[1] % 2):256 * (B[1] % 2) + 256], cm, 512, 256, -256.0)
-    d = cell(3, 3, 1280)
-    wait("v", c)
-    c = add_up(T.cs[:, 512:640], cm, 1024, 128, 0.0)
-    shift = 0.0 if odd else 16.0
-    wait("v", b)
-    V(v.tensor_scalar(T.pu1[:, c01:c01 + 2], T.cs[:, 255:512:256], 256.0 + shift, None, OP.add))
-    wait("v", d)
-    d = add_up(T.cs[:, 640:768], cm, 1280, 128, 0.0)
-    wait("v", c, kl[2])
-    V(v.tensor_scalar(T.pu1[:, B[2]:B[2] + 1], T.cs[:, 639:640], T.ls[:, 2:3], shift, OP.add, OP.add))
-    wait("v", d, kl[3])
-    k_pu = V(v.tensor_scalar(T.pu1[:, B[3]:B[3] + 1], T.cs[:, 767:768], T.ls[:, 3:4], shift, OP.add, OP.add))
+    call = {"q": quant, "d": lambda i: kd.update({i: down(i)}), "r": rows, "s": lambda i: kd.update({i: scores(i, kd[i + 1])}),
+            "b": lambda i: bound(i, kd[i & 2]), "c": cell, "g": signs, "l": sum_signs, "t": total, "p": places, "z": lists}
+    for step in OPT["order"].split():
+        call[step[0]](*[int(ch) for ch in step[1:]])
+    k_pu = kn_["pu"]
 
-    def over_blocks(out, mid, src, fill):
-        a = V(v.tensor_tensor(mid[0:64, 0:9], src(0, 64), src(64, 128), OP.add))
-        fill(3)
-        wait("v", a)
-        for h in range(4):
-            a = V(v.tensor_tensor(out[32 * h:32 * h + 32, 0:9], mid[0:32, 0:9], mid[32:64, 0:9], OP.add))
-        return a
-
-    def invert(n, ready, cols, vals, lo, lift, fill):
+    def invert(n, ready, cols, vals, lo, lift, fill, wide=9):
         W = lambda b: T[b + n]
         wait("v", *ready)
         a = V(v.tensor_copy(W("win")[:, 0:528].indirect(W("pu")[:, 0:cols]), vals[:, 0:16 * cols]))
@@ -264,208 +269,256 @@ def rank_program(g, core, T, topo):
         a = V(v.transpose(W("tz")[:, 128:288], W("win")[:, lo - 16:lo + 144]))
         fill(1)
         wait("v", a)
-        a = V(v.tensor_tensor(W("qa")[:, 0:9], W("tz")[:, 0:288:32], W("tz")[:, 16:288:32], OP.add))
-        fill(2)
+        a = V(v.tensor_tensor(W("qa")[:, 31:288:32], W("tz")[:, 0:288:32], W("tz")[:, 16:288:32], OP.add))
+        a = fill(2) or a
         wait("v", a)
-        a = over_blocks(W("qc"), W("qb"), lambda p, q: W("qa")[p:q, 0:9], fill)
+        a = V(v.tensor_tensor(W("qb")[0:64, 0:wide], W("qa")[0:64, 31:32 * wide:32], W("qa")[64:128, 31:32 * wide:32], OP.add))
+        fill(3)
+        wait("v", a)
+        for h in range(4):
+            a = V(v.tensor_tensor(W("qc")[32 * h:32 * h + 32, 0:wide], W("qb")[0:32, 0:wide], W("qb")[32:64, 0:wide], OP.add))
         fill(4)
         wait("v", a)
         b = V(v.tensor_scalar(W("lst")[:, 0:16], W("qc")[:, 0:9].indirect(T.goff[:, 0:1]), lift, None, OP.add))
         fill(5)
         return a, b
 
-    def pick(dc, ds, sc, ss, off, ready_c, ready_s):
-        wait("v", *ready_c)
-        a = V(v.tensor_copy(dc.bitcast(dt.uint32), sc.bitcast(dt.uint32).indirect(off)))
-        wait("s", *ready_s)
-        b = S(s.activation(ds, ss.indirect(off), COPY))
-        return a, b
+    def pick_codes(dc, sc, off, *ready):
+        wait("v", *ready)
+        return V(v.tensor_copy(dc.bitcast(dt.uint32), sc.bitcast(dt.uint32).indirect(off)))
 
-    def remote(o, i, dst, sem):
+    def pick_scales(ds, ss, off, *ready):
+        wait("s", *ready)
+        return S(s.activation(ds, ss.indirect(off), COPY))
+
+    def remote(o, i, dst, sem, *ready):
+        wait("g", *ready)
         rid, pid = topo.addr(dst, core)
         n = len(topo.engines(core, dst))
-        g.remote_dma(o, i, T.sem[sem], T.sem["sent"], pid, rid, topo.mask(core, dst))
+        codes = sem in ("h1c", "h2c")
+        g.remote_dma(o.bitcast(dt.uint8) if codes else o, i.bitcast(dt.uint8) if codes else i, T.sem[sem], T.sem["sent"], pid, rid,
+                     topo.mask(core, dst))
         count["sent"] = count.get("sent", 0) + n
         return (sem, n)
-
-    def send(out_c, in_c, out_s, in_s, a, b, dst, sem_c, sem_s):
-        wait("g", a)
-        kc = remote(out_c.bitcast(dt.uint8), in_c.bitcast(dt.uint8), dst, sem_c)
-        wait("g", b)
-        return kc, remote(out_s, in_s, dst, sem_s)
-
-    k_gt = []
-
-    def last_list(i):
-        if i == 0:
-            wait("v", k_gr)
-            k_gt.append(V(v.transpose(T.gt[:, 0:32], T.gr[:, 0:32])))
-        elif i == 1:
-            wait("v", *k_gt)
-            V(v.tensor_scalar(T.goff[:, 0:2], T.gt[:, 0:2], 1.0 / 32, None, OP.mult))
 
     def w_codes(o):
         wait("v", dw)
         return V(v.quantize_mx(T.wq[:, 128 * o:128 * o + 128], T.ws[:, 128 * o:128 * o + 128], T.wb[:, 512 * o:512 * o + 512]))
 
     m0 = SLOT * rank
-    word = lambda rk, w: T.msg[:, SLOT * rk + w:SLOT * rk + w + 1]
     mate = T.cores[rank ^ 1]
-    wait("g", kp[3])
-    in_raw = remote(T.spm[:, 0:4], T.sp[:, 0:4], mate, "hr")
-    wait("g", k_one)
-    G(g.affine_select(T.seg[:, 0:224], T.seg[:, 0:224], [[0, 7], [1, 32]], OP.is_gt, 0.0, 0, 0))
-    wait("g", k_pu)
-    in_places = remote(T.pum[:, 0:4], T.pu1[:, 0:4], mate, "hp")
-    wait("g", iota(T.rs[:, 0:128], [[0, 128]], 0, 0))
-    k_rs = G(g.affine_select(T.rs[:, 0:128], T.rs[:, 0:128], [[0, 8], [1, 16]], OP.is_gt, -2 * BIG, 0, 0))
-    S(s.activation(T.pcq[:, 0:1], T.pcf[:, 1:2], COPY, scale=1.0 / 128))
-    k = S(s.activation(T.pcq[:, 1:2], T.pcf[:, 0:1], COPY, scale=2.0))
-    for buf, a, n in ((T.winm, lom - 16, 160), (T.ow, 0, 32), (T.ow, 160, 96), (T.win2, 0, 160), (T.cp, 0, 64), (T.idr, 64, 192)):
-        S(s.activation(buf[:, a:a + n], T.thr[:, 128 * c01:128 * c01 + n], COPY, scale=0.0))
-    wait("s", k, k_i6)
-    S(s.activation(T.vals2[:, 0:32], T.i4[:, 0:32], IDENT, bias=T.pcq[:, 1:2]))
-    S(s.activation(T.jc[:, 0:16], T.i6[:, 0:16], IDENT, bias=T.pcq[:, 0:1], scale=1.0 / 128))
-    wait("s", in_raw)
+    in_raw = [remote(T.spm[:, c:c + 2], T.sp[:, c:c + 2], mate, sem, kp[i]) for c, sem, i in ((c01, "hr", 0), (2 - c01, "hq", 2))]
+    k_i5 = iota(T.i5[:, 0:16], [[1, 8], [0, 2]], 0, 0, False)
+    for i, (base, step) in enumerate(((16, 1), (143, -1), (0, 0 if OPT["three"] else 256))):
+        k_pt = iota(T.pt[:, i:i + 1], [[0, 1]], base, step)
+    iota(T.sq[:, 128:129], [[0, 1]], 0, -1)
+    k_sq0 = iota(T.sq[:, 129:130], [[0, 1]], -16, 0)
+    in_places = remote(T.pum[:, 0:4], T.pu1[:, 0:4], mate, "hp", k_pu)
+    wait("s", k_nb)
     for c in range(4):
-        k_vm = S(s.activation(T.valm[:, 16 * c:16 * c + 16], T.dg[:, 0:16], COPY, scale=T.spm[:, c:c + 1]))
+        k_vo = S(s.activation(T.valo[:, 16 * c:16 * c + 16], T.dg[:, 0:16], COPY, scale=sp[c]))
+    wait("s", *kc.values())
+    for c in B:
+        k_raw = S(s.activation(T.raw[:, 128 * c:128 * c + 128], row[c], COPY))
+    S(s.activation(T.idr[:, 64:256], T.thr[:, 0:192], COPY, scale=0.0))
+    wait("s", *in_raw)
+    for c in range(4):
+        S(s.activation(T.valm[:, 16 * c:16 * c + 16], T.nb[:, 0:16], IDENT, bias=T.spm[:, c:c + 1]))
 
-    k_q1, k_l1 = invert("1", (k_pu, k_v1), 4, T.vals1, lo1, 256.0, last_list)
+    lane = []
+
+    def sorted_scores(i):
+        if i == 0:
+            wait("v", k_vo)
+            lane.append(V(v.tensor_copy(T.wins[:, 0:528].indirect(T.pu1[:, 0:4]), T.valo[:, 0:64])))
+        elif i == 1:
+            wait("v", lane[0])
+            lane.append(V(v.transpose(T.tzs[:, 0:128], T.wins[:, lo1:lo1 + K])))
+        elif i == 2:
+            wait("v", lane[1], k_seg)
+            return V(v.tensor_tensor_scan(T.qa1[:, 288:416], T.seg[:, 0:128], T.tzs[:, 0:128], 0.0, OP.mult, OP.add))
+        elif i == 5:
+            wait("v", k_i5)
+            lane.append(V(v.tensor_copy(T.eoff[:, 0:16], T.i5[:, 0:16])))
+
+    k_q1, k_l1 = invert("1", (k_pu, k_v1), 4, T.vals1, lo1, 256.0, sorted_scores, 13)
+
+    def to_many(src, dsts, sem, *ready):
+        wait("g", *ready)
+        ids, m = [], topo.mask(core, mate)
+        for x in dsts:
+            rid, pid = topo.addr(T.cores[rank ^ x], core)
+            ids.append(DstId(rid=rid, pnc=pid))
+            m &= topo.mask(core, T.cores[rank ^ x])
+        n = bin(m).count("1")
+        g.remote_dma_fused([RemoteDMATransfer(dst_ids=ids, dma_engine_mask=m, remote_sem=T.sem[sem], srcs=[src],
+                                              dsts=list(dsts.values()))], local_sem=T.sem["sent"])
+        count["sent"] += n
+        return (sem, len(dsts) * n)
+    slot = T.msg[:, SLOT * odd:SLOT * odd + 4]
+    three = OPT["three"]
+    in_msg = to_many(T.qc1[:, 9:13], {2: slot, 3: slot, 1: T.msg[:, 8:12]} if three else {2: slot, 3: slot}, "hm", k_q1)
     wait("s", k_q1)
-    S(s.activation(T.msg[:, m0 + 5:m0 + 21], T.qc1[:, 0:9].indirect(T.goff[:, 0:1]), COPY))
-    a1, b1 = pick(T.c1[:, 0:K], T.s1[:, 0:K], T.xq[:, 0:512], T.xs[:, 0:512], T.lst1[:, 2:10], (k_l1,), (k_l1,))
-    in1c, in1s = send(T.c1[:, K:2 * K], T.c1[:, 0:K], T.s1[:, K:2 * K], T.s1[:, 0:K], a1, b1, mate, "h1c", "h1s")
+    k_at = S(s.activation(T.at[:, 0:16], T.qc1[:, 0:13].indirect(T.eoff[:, 18:19]), COPY))
 
-    wait("t", a1, b1)
-    kaf = X(t.matmul_mx(T.psf[:, 0:128], T.uq[:, 0:128], T.us[:, 0:128], T.c1[:, 0:128], T.s1[:, 0:128], True, True))
-    kap = X(t.matmul_mx(T.psp[:, 0:128], T.c1[:, 0:128], T.s1[:, 0:128], T.uq0[:, 2:130], T.us0[:, 2:130], True, True))
-    wait("s", kap)
-    k_m4 = S(s.activation(word(rank, 4), T.psp[:, 0:1], COPY))
-    wait("v", in_places, k_vm, k_one)
-    a = V(v.tensor_copy(T.winm[:, 0:528].indirect(T.pum[:, 0:4]), T.valm[:, 0:64]))
-    k_co = V(v.tensor_copy(T.eoff[:, 0:16], T.i5[:, 0:16]))
-    wait("v", kaf)
-    b = V(v.transpose(T.at[:, 0:128], T.psf[:, 0:128]))
-    wait("v", a)
-    k_t1 = V(v.transpose(T.tzm[:, 0:128], T.winm[:, lom:lom + 128]))
-    wait("v", b)
-    k_msg = V(v.tensor_copy(T.msg[:, m0:m0 + 4], T.at[:, 0:128:32]))
-    wait("g", k_msg, k_m4)
-    ids, m = [], topo.mask(core, mate)
-    for other in (rank ^ 2, rank ^ 3):
-        dst = T.cores[other]
-        rid, pid = topo.addr(dst, core)
-        ids.append(DstId(rid=rid, pnc=pid))
-        m &= topo.mask(core, dst)
-    n = bin(m).count("1")
-    view = T.msg[:, m0:m0 + 6]
-    g.remote_dma_fused([RemoteDMATransfer(dst_ids=ids, dma_engine_mask=m, remote_sem=T.sem["hm"], srcs=[view], dsts=[view] * 2)],
-                       local_sem=T.sem["sent"])
-    in_msg = ("hm", 2 * n)
-    count["sent"] += n
-    in_ids = remote(word(rank, 5), word(rank, 5), mate, "hi")
+    off = T.lst1[:, 2:10]
+    mine = T.osr[:, lom:lom + K]
+    a1 = pick_codes(T.c1[:, 0:K], T.xq[:, 0:512], off, k_l1)
+    wait("s", k_l1, k_raw)
+    k_os = S(s.activation(mine, T.raw[:, 0:512].indirect(off), COPY))
+    b1 = pick_scales(T.s1[:, 0:K], T.xs[:, 0:512], off)
+    in1c = remote(T.c1[:, K:2 * K], T.c1[:, 0:K], mate, "h1c", a1)
+    in1s = remote(T.s1[:, K:2 * K], T.s1[:, 0:K], mate, "h1s", b1)
+    if three:
+        in_ids = to_many(T.lst1[:, 0:1], {x: T.cu[:, x:x + 1] for x in (1, 2, 3)}, "hi")
+    else:
+        in_ids = to_many(T.at[:, 0:1], {x: T.at[:, 16 + x:17 + x] for x in (1, 2, 3)}, "hi", k_at)
 
-    fr = (T.psf[:, 512:640], T.psf[:, 0:128]) if odd else (T.psf[:, 0:128], T.psf[:, 512:640])
-    ps, nsel = [[T[b][:, j:j + 1] for j in range(2)] for b in ("ps", "nsel")]
-    sel = [T.cp[:, 0:1], T.sel[:, 0:1]]
-    a = V(v.transpose(T.tzm[:, 128:288], T.winm[:, lom - 16:lom + 144]))
-    b = V(v.tensor_tensor(T.am[:, 0:128], T.nb[:, 0:128], T.psf[:, 0:128], OP.add))
-    wait("v", a, k_rs)
-    a = V(v.tensor_tensor_scan(T.qam[:, 64:288], T.seg[:, 0:224], T.tzm[:, 64:288], 0.0, OP.mult, OP.add))
-    wait("s", k_t1)
-    for h in range(2):
-        k = S(s.activation(T.qam[:, 288 + 32 * h:320 + 32 * h], T.tzm[:, 32 * h:32 * h + 32], COPY,
-                           accum_out=T.qam[:, 32 * h + 31:32 * h + 32]))
-    wait("v", b)
-    V(v.tensor_tensor_scan(T.ow[:, 32:160], T.rs[:, 0:128], T.am[:, 0:128], 0.0, OP.add, OP.max))
-    wait("v", a, k)
-    a = over_blocks(T.qcm, T.qbm, lambda p, q: T.qam[p:q, 31:288:32], lambda i: None)
     k_w = [w_codes(0)]
-    wait("s", a)
-    k_ml = S(s.activation(T.ml[:, 0:16], T.qcm[:, 0:9].indirect(T.goff[:, 0:1]), COPY))
-    wait("v", a)
-    a = V(v.tensor_tensor(T.bc[:, 0:16], T.qcm[:, 0:9].indirect(T.goff[:, 0:1]), T.ow[:, 15:256:16], OP.is_ge if odd else OP.is_gt))
+    wait("v", in_places, k_os)
+    a = V(v.tensor_tensor(T.cb[:, 0:64], T.osr[:, 0:528].indirect(T.pum[:, 0:4]), T.valm[:, 0:64], OP.is_le if odd else OP.is_lt))
     k_w.append(w_codes(1))
     wait("v", a)
-    a = V(v.tensor_tensor(T.bs[:, 0:16], T.bc[:, 0:16], T.jc[:, 0:16], OP.add))
-    E, O = (T.ml[:, 0:1], word(rank, 4)) if odd else (word(rank, 4), T.ml[:, 0:1])
-    wait("v", k_ml, k_m4)
-    b = V(v.tensor_tensor(sel[P], O, E, OP.is_gt))
-    V(v.tensor_tensor(nsel[P], E, O, OP.is_ge))
+    a = V(v.tensor_tensor_scan(T.cr[0:64, 0:96], T.cb[0:64, 0:96], T.cb[64:128, 0:96], 0.0, OP.add, OP.add))
     wait("v", a)
-    k_o2 = V(v.tensor_scalar(T.off2[:, 0:16], T.bs[:, 0:16], 128.0, None, OP.mult))
-    V(v.tensor_tensor(ps[P], E, O, OP.max))
-    wait("v", b)
-    k_sp = V(v.tensor_scalar(T.kc[:, P:P + 1], sel[P], T.pt[:, 1:2], T.pt[:, 0:1], OP.mult, OP.add))
+    a = V(v.transpose(T.ct[0:64, 0:32], T.cr[0:64, 64:96]))
+    wait("v", a)
+    for h in range(2):
+        a = V(v.tensor_tensor_scan(T.cn[32 * h:32 * h + 32, 0:32], T.ct[0:32, 0:32], T.ct[32:64, 0:32], 0.0, OP.add, OP.add))
+    wait("v", a)
+    for h in range(2):
+        o, i = T.bc[64 * h:64 * h + 64, 0:8], T.jt[64 * h:64 * h + 64, 0:8]
+        if odd:
+            a = V(v.tensor_scalar(o, i, T.cn[0:64, 31:32], None, OP.is_lt))
+        else:
+            a = V(v.tensor_scalar(o, i, T.cn[0:64, 31:32], float(K), OP.add, OP.is_ge))
+    wait("s", in_msg, lane[2], b1)
+    kx = S(s.activation(T.yx[:, 256:272], T.msg[:, 0:16 if three else 8].indirect(T.eoff[:, 16:17]), COPY))
+    ky = {h: S(s.activation(T.yx[:, 128 * h:128 * h + 128], T.msg[:, 0:8].indirect(T.eoff[:, 8 * h:8 * h + 8]), COPY)) for h in (1, 0)}
+    ps, sel = [[T[b][:, j:j + 1] for j in range(2)] for b in ("ps", "sel")]
+    me, him, E, O = T.at[:, 1:2], T.yx[:, 258:259] if three else T.psp[:, 0:1], T.yx[:, 256:257], T.yx[:, 257:258]
 
-    wait("t", in1c, in1s)
-    kb = X(t.matmul_mx(T.psf[:, 512:640], T.uq[:, 0:128], T.us[:, 0:128], T.c1[:, 128:256], T.s1[:, 128:256], True, True))
-    kbs = X(t.matmul_mx(T.psp[:, 1024:1280], T.uq[:, 0:128], T.us[:, 0:128], T.c1[:, 0:256], T.s1[:, 0:256], True, True))
-    wait("s", in_msg, k_co)
-    ky = S(s.activation(T.yx[:, 0:256], T.msg[:, 2 * SLOT * Q:2 * SLOT * (Q + 1)].indirect(T.eoff[:, 0:16]), COPY))
-    a2, b2 = pick(T.c2[:, own], T.s2[:, own], T.c1[:, 0:256], T.s1[:, 0:256], T.off2[:, 2:10], (k_o2, in1c), (k_o2, in1s))
-    in2c, in2s = send(T.c2[:, own], T.c2[:, own], T.s2[:, own], T.s2[:, own], a2, b2, T.cores[rank ^ 2], "h2c", "h2s")
+    def with_mate(*ready):
+        wait("v", k_at, *ready)
+        return V(v.tensor_tensor(ps[P], me, him, OP.max))
+
+    def turn(h):
+        wait("v", ky[h])
+        return V(v.transpose(T.fs[:, 128 * h:128 * h + 128], T.yx[:, 128 * h:128 * h + 128]))
+    wait("v", kx)
+    k_pq = V(v.tensor_tensor(ps[Q], E, O, OP.max))
+    V(v.tensor_tensor(sel[Q], O, E, OP.is_gt))
+    if three:
+        k_sel = with_mate()
+    wait("v", a)
+    a = V(v.tensor_tensor(T.bs[:, 0:8], T.bc[:, 0:8], T.jc[:, 0:8], OP.add))
+    kf = turn(1)
+    wait("v", a)
+    k_o2 = V(v.tensor_scalar(T.off2[:, 0:8], T.bs[:, 0:8], 128.0, None, OP.mult))
+    kg = turn(0)
+
+    wait("t", in1c, in1s, a1, b1)
+    kb = X(t.matmul_mx(T.psf[:, 0:128], T.uq[:, 0:128], T.us[:, 0:128], T.c1[:, K:2 * K], T.s1[:, K:2 * K], True, True))
+    if not three:
+        kd = X(t.matmul_mx(T.psp[:, 0:128], T.c1[:, K:2 * K], T.s1[:, K:2 * K], T.uq0[:, 2:130], T.us0[:, 2:130], True, True))
+    a2 = pick_codes(T.c2[:, own], T.c1[:, 0:256], T.off2[:, 0:8], k_o2, in1c)
+    wait("s", k_pq)
+    ks = S(s.activation(T.sq[:, 144:272], mine, ACT.Sign, bias=ps[Q], scale=-1.0))
+    wait("s", kf)
+    kt2 = S(s.activation(T.sq[:, 0:128], T.fs[:, 128:256], ACT.Sign, bias=E, scale=-1.0))
+    b2 = pick_scales(T.s2[:, own], T.s1[:, 0:256], T.off2[:, 0:8], k_o2, in1s)
+    in2c = remote(T.c2[:, own], T.c2[:, own], T.cores[rank ^ 2], "h2c", a2)
+    in2s = remote(T.s2[:, own], T.s2[:, own], T.cores[rank ^ 2], "h2s", b2)
 
     def products(side, bank, *ready):
         wait("t", *k_w, *ready)
         return [X(t.matmul_mx(bank[:, 512 * (o + 2):512 * (o + 2) + 128], T.wq[:, 128 * o:128 * o + 128], T.ws[:, 128 * o:128 * o + 128],
                               T.c2[:, side], T.s2[:, side], True, True)) for o in range(2)]
     ko = products(own, T.psf, a2, b2)
-
-    E, O = word(2 * Q, 4), word(2 * Q + 1, 4)
-    wait("v", in_msg)
-    a = V(v.tensor_tensor(ps[Q], E, O, OP.max))
-    wait("v", kb, k_sp)
-    cmp(T.ba[:, 0:128], fr[1], ps[P], OP.is_gt, nsel[P])
-    wait("v", ky)
-    kf = V(v.transpose(T.fs[:, 0:256], T.yx[:, 0:256]))
-    k_sq = V(v.tensor_tensor(sel[Q], O, E, OP.is_gt))
-    k_nq = V(v.tensor_tensor(nsel[Q], E, O, OP.is_ge))
-    cmp(T.ba[:, 128:256], fr[0], ps[P], OP.is_ge, sel[P])
-    wait("s", a, kbs)
-    ks = S(s.activation(T.sq[:, 0:256], T.psp[:, 1024:1280], ACT.Sign, bias=ps[Q], scale=-1.0))
-    wait("s", kf)
-    k = S(s.activation(T.sq[:, 256:384], T.fs[:, 0:128], ACT.Sign, bias=ps[Q], scale=-1.0))
-    wait("s", ks, k_sq)
-    kc = S(s.activation(T.kc[:, Q:Q + 1], sel[Q], IDENT, bias=T.pt[:, 4:5], scale=T.pt[:, 3:4]))
-    S(s.activation(T.sq[:, 384:640], T.sq[:, 0:256], ACT.Relu, scale=1.0 if P < Q else -1.0, accum_out=T.lq[:, 0:1]))
-    wait("s", k)
-    kq2 = S(s.activation(T.sq[:, 640:768], T.sq[:, 256:384], ACT.Relu, scale=sel[Q], accum_out=T.lq[:, 1:2]))
-    wait("t", ks)
     kn = products(arr, T.psp, in2c, in2s)
-    wait("v", kf)
-    a = cmp(T.ba[:, 256:512], T.fs[:, 0:256], ps[P], OP.is_ge if Q < P else OP.is_gt)
-    wait("v", k_nq)
-    b = cmp(T.bb[:, 0:128], T.fs[:, 128:256], ps[Q], OP.is_gt, nsel[Q])
-    wait("v", a, kc)
-    a = add_up(T.bt[:, 0:256], T.ba, 0, 256, T.kc[:, P:P + 1])
-    wait("v", b)
-    b = add_up(T.bu[:, 0:64], T.bb, 0, 64, T.kc[:, Q:Q + 1])
-    wait("v", a)
-    V(v.tensor_scalar(T.pu2[:, P:P + 1], T.bt[:, 255:256], 144.0, None, OP.add))
-    wait("v", b, kq2)
-    kv = V(v.tensor_scalar(T.pu2[:, Q:Q + 1], T.bu[:, 63:64], T.lq[:, 1:2], T.lq[:, 0:1], OP.subtract, OP.subtract if P < Q else OP.add))
 
-    wait("s", in_ids)
+    his = T.psf[:, 0:128]
+    bu = lambda i, n=64: T.bu[:, 64 * i:64 * i + n]
+    last = lambda i: T.bu[:, 64 * i + 63:64 * i + 64]
+    wait("s", ks)
+    S(s.activation(T.sq[:, 272:400], T.sq[:, 144:272], ACT.Relu, scale=1.0 if P < Q else -1.0, accum_out=T.lq[:, 0:1]))
+    wait("s", kt2, k_sq0)
+    kq2 = S(s.activation(T.junk[:, 0:130], T.sq[:, 0:130], ACT.Relu, scale=-1.0, accum_out=T.lq[:, 1:2]))
+    wait("v", kg, k_pt)
+    a = cmp(T.ba[:, 0:128], T.fs[:, 0:128], O, OP.is_ge)
+    pick_p = lambda: V(v.tensor_tensor(sel[P], me, him, OP.is_gt if odd else OP.is_lt))
+    if three:
+        b = cmp(T.ba[:, 128:256], mine, him, OP.is_gt if odd else OP.is_ge)
+        wait("v", k_sel)
+        c = cmp(T.ba[:, 256:512], T.fs[:, 0:256], ps[P], OP.is_ge if Q < P else OP.is_gt)
+        wait("v", b)
+        a = add_up(bu(0), T.ba, 0, 64, T.pt[:, 1:2])
+        wait("v", kb)
+        d = cmp(T.ba[:, 512:640], his, me, OP.is_ge if odd else OP.is_gt)
+        e = cmp(T.ba[:, 640:768], his, ps[Q], OP.is_ge if P < Q else OP.is_gt)
+        wait("v", c)
+        add_up(bu(2, 128), T.ba, 256, 128, 0.0)
+        wait("v", d)
+        add_up(bu(4), T.ba, 512, 64, T.pt[:, odd:odd + 1])
+        d = add_up(bu(1), T.ba, 128, 64, T.pt[:, 1 - odd:2 - odd])
+        wait("v", e)
+        e = add_up(bu(5), T.ba, 640, 64, 128.0 if P < Q else 0.0)
+        wait("v", kq2, a)
+        f = V(v.tensor_scalar(T.bu[:, 384:385], last(0), T.lq[:, 1:2], T.lq[:, 0:1], OP.min, OP.subtract if P < Q else OP.add))
+        wait("v", d)
+        V(v.tensor_scalar(T.pu2[:, P:P + 1], last(4), last(1), last(3), OP.min, OP.add))
+        wait("v", f, e)
+        kv = V(v.tensor_scalar(T.pu2[:, Q:Q + 1], last(5), T.bu[:, 384:385], None, OP.add))
+        pick_p()
+        V(v.tensor_copy(T.cf[:, 0:1], T.lst1[:, 0:1]))
+        wait("v", in_ids)
+        k_cf = V(v.tensor_copy(T.cf[:, 1:4], T.cu[:, 1:4]))
+        col = lambda r: T.cf[:, (rank ^ r):(rank ^ r) + 1]
+    else:
+        wait("v", kb, k_at)
+        d = cmp(T.ba[:, 512:640], his, me, OP.is_ge if odd else OP.is_gt)
+        e = cmp(T.ba[:, 640:768], his, ps[Q], OP.is_ge if P < Q else OP.is_gt)
+        k_sel = with_mate(kd)
+        b = cmp(T.ba[:, 128:256], mine, him, OP.is_gt if odd else OP.is_ge)
+        wait("v", e)
+        a = add_up(bu(0), T.ba, 0, 64, T.pt[:, 1:2])
+        wait("v", k_sel)
+        c = cmp(T.ba[:, 256:512], T.fs[:, 0:256], ps[P], OP.is_ge if Q < P else OP.is_gt)
+        add_up(bu(4), T.ba, 512, 64, T.pt[:, odd:odd + 1])
+        e = add_up(bu(5), T.ba, 640, 64, 128.0 if P < Q else 0.0)
+        wait("v", kq2, a)
+        f = V(v.tensor_scalar(T.bu[:, 384:385], last(0), T.lq[:, 1:2], T.lq[:, 0:1], OP.min, OP.subtract if P < Q else OP.add))
+        wait("v", c)
+        d = add_up(bu(2, 128), T.ba, 256, 128, 0.0)
+        d = add_up(bu(1), T.ba, 128, 64, T.pt[:, 1 - odd:2 - odd])
+        wait("v", f, e)
+        V(v.tensor_scalar(T.pu2[:, Q:Q + 1], last(5), T.bu[:, 384:385], None, OP.add))
+        k_cf = pick_p()
+        wait("v", d)
+        kv = V(v.tensor_scalar(T.pu2[:, P:P + 1], last(4), last(1), last(3), OP.min, OP.add))
+        col = lambda r: T.at[:, 16 + (rank ^ r):17 + (rank ^ r)] if r != rank else T.at[:, 0:1]
+
+    yw = (T.yw0, T.yw1)
+    for o in range(2):
+        wait("s", ko[o])
+        S(s.activation(yw[o][:, P:256:2], T.psf[:, 512 * (o + 2):512 * (o + 2) + 128], COPY))
+    wait("s", k_cf if three else in_ids)
     for j in range(2):
-        k = S(s.activation(T.vd[:, j:j + 1], word(2 * j, 5), IDENT, bias=word(2 * j + 1, 5), scale=-1.0))
-    S(s.activation(T.cp[:, 32:33], sel[1], IDENT, bias=2.0))
+        k = S(s.activation(T.vd[:, j:j + 1], col(2 * j), IDENT, bias=col(2 * j + 1), scale=-1.0))
+    wait("s", k_cf)
+    for j in range(2):
+        S(s.activation(T.cp[:, 32 * j:32 * j + 1], sel[j], IDENT, bias=2.0 * j))
     wait("s", k)
     for j in range(2):
-        kcp = S(s.activation(T.cp[:, 32 * j + 1:32 * j + 2], T.vd[:, j:j + 1], IDENT, bias=word(2 * j, 5), scale=sel[j]))
-    yw = (T.yw0, T.yw1)
-    wait("s", ko[1])
-    S(s.activation(T.yw1[:, P:256:2], T.psf[:, 1536:1664], COPY))
+        kcp = S(s.activation(T.cp[:, 32 * j + 1:32 * j + 2], T.vd[:, j:j + 1], IDENT, bias=col(2 * j), scale=sel[j]))
     kz = []
 
     def numbers(i):
-        if i == 0:
-            wait("v", ko[0])
-            V(v.tensor_copy(T.yw0[:, P:256:2], T.psf[:, 1024:1152]))
-        elif i < 3:
+        if i == 2:
             wait("v", kcp)
-            kz.append(V(v.transpose(T.idr[:, i - 1:64:2], T.cp[:, 32 * i - 32:32 * i])))
-        else:
+            for j in range(2):
+                kz.append(V(v.transpose(T.idr[:, j:64:2], T.cp[:, 32 * j:32 * j + 32])))
+        elif i > 2:
             wait("v", kz[1])
             kz.append(V(v.tensor_copy(T.idr[0:2, 64 * i - 128:64 * i - 64], T.idr[32 * i - 64:32 * i - 62, 0:64])))
     k_q2, k_l2 = invert("2", (kv,), 2, T.vals2, 16, 128.0, numbers)
@@ -484,5 +537,5 @@ def rank_program(g, core, T, topo):
     d0 = done(y.dma_start(T.y[:, 0:256], T.yb[:, 0:256]), "dy", 16)
     wait("s", ki)
     d2 = done(s.dma_start(T["id"][0:2, 0:128], T.idb[0:2, 0:128]), "did", 16)
-    wait("g", ("sent", count["sent"]), in1c, in1s, in2c, in2s, in_msg, in_raw, in_places, in_ids, du, *dx.values(), dw,
+    wait("g", ("sent", count["sent"]), in1c, in1s, in2c, in2s, in_msg, *in_raw, in_places, in_ids, du, *dx.values(), dw,
          ("gc", count["gc"]), ("v", count["v"]), ("s", count["s"]), ("t", count["t"]), d0, d2)

@@ -10,9 +10,11 @@ STEP = 1.25 * 2.0 ** -24
 TINY = 2.0 ** -122
 SLOT = 4
 
-OPT = {"q0": True, "three": False, "scal": [(2, 0), (3, 0), (3, 1)],
-       "order": "d0 r0 q1 d1 s0 r1 b0 b1 q2 z0 d2 r2 q3 z1 d3 s2 r3 c10 c01 c02 c00 c12 c11 c21 g20 b2 g30 b3 g31 l2 l3 "
-                "c03 c13 c23 c32 c22 t0 c33 t1 t2 t3 p02 p2 p3"}
+OPT = {"q0": True, "loads": [[0], [1], [2], [3]], "banks": [[0], [1], [2, 3]], "split": True, "valm": False, "apart": 0, "folds": [[0, 1, 2, 3], []], "tail": 3, "numbers": {1: [0], 3: [1], 4: [2, 3]}, "pair": 0, "two": "v4", "mi": 1,
+       "second": "V2 x eO eE n5 pQ n6 tO pc g1 gA mD mI mH pz rA g2' rC sQ tE ps b a c d' B C A D se uQ uP v0 v1 r0 r1 k0 k1 y0 y1",
+       "scal": [(2, 0), (3, 0), (3, 1)],
+       "order": "d0 s0 v0 r0 q1 z0 r1 d1 b0 s1 z3 v1 q2 z2 r2 d2 q3 z1 b1 d3 s2 r3 c01 c00 c02 c10 c12 c11 c21 g20 b2 g30 b3 g31 l2 l3 v2 v3 "
+                "c03 c13 c23 c32 t0 c22 t1 c33 p02 t2 t3 x01 p2 p3 x00 x21 x20"}
 
 SCRATCH = {
     "ur": ("sbuf", [128, 520], "bfloat16"), "zoff": ("sbuf", [128, 8], "uint16"),
@@ -29,41 +31,41 @@ SCRATCH = {
     "psf": ("psum", [128, 2048], "float32"),
     "psp": ("psum", [128, 2048], "float32"),
     "ip": ("sbuf", [128, 2], "int32"), "pt": ("sbuf", [128, 8], "float32"),
-    "it": ("sbuf", [128, 128], "int32"), "ita": ("sbuf", [128, 16], "int32"), "tri": ("sbuf", [128, 128], "float32"),
-    "nb": ("sbuf", [128, 16], "float32"), "dg": ("sbuf", [128, 16], "float32"), "seg": ("sbuf", [128, 128], "float32"),
-    "i3": ("sbuf", [128, 64], "float32"), "vals1": ("sbuf", [128, 64], "bfloat16"),
+    "it": ("sbuf", [128, 128], "int32"), "ita": ("sbuf", [128, 64], "int32"), "tri": ("sbuf", [128, 128], "float32"),
+    "nb": ("sbuf", [128, 64], "float32"), "dg": ("sbuf", [128, 16], "float32"), "seg": ("sbuf", [128, 128], "float32"),
+    "i3": ("sbuf", [128, 64], "float32"), "vals1": ("sbuf", [128, 64], "float32"),
     "i4": ("sbuf", [128, 32], "float32"), "vals2": ("sbuf", [128, 32], "bfloat16"),
-    "i5": ("sbuf", [128, 16], "int32"), "eoff": ("sbuf", [128, 20], "uint16"),
-    "i6": ("sbuf", [128, 8], "float32"), "jt": ("sbuf", [128, 8], "float32"), "jc": ("sbuf", [128, 8], "float32"),
-    "gr": ("sbuf", [128, 96], "float32"), "gt": ("sbuf", [128, 96], "float32"), "goff": ("sbuf", [128, 2], "uint16"),
-    "pca": ("sbuf", [128, 2], "int32"), "pcf": ("sbuf", [128, 2], "float32"), "pcq": ("sbuf", [128, 2], "float32"),
+    "i5": ("sbuf", [128, 28], "int32"), "eoff": ("sbuf", [128, 28], "uint16"),
+    "iy": ("sbuf", [128, 256], "bfloat16"), "one": ("sbuf", [128, 256], "bfloat16"), "jump": ("sbuf", [128, 256], "bfloat16"),
+    "tab": ("sbuf", [128, 256], "bfloat16"), "kq": ("sbuf", [128, 3], "float32"), "yl": ("sbuf", [128, 2], "uint16"),
+    "gr": ("sbuf", [128, 96], "float32"), "gt": ("sbuf", [128, 96], "float32"), "goff": ("sbuf", [128, 6], "uint16"),
+    "keep": ("sbuf", [128, 1], "float32"), "bg": ("sbuf", [128, 3], "float32"),
+    "pca": ("sbuf", [128, 2], "int32"), "pcf": ("sbuf", [128, 2], "float32"), "pcq": ("sbuf", [128, 3], "float32"),
     "sp": ("sbuf", [128, 4], "float32"), "dl": ("sbuf", [128, 4], "float32"), "thr": ("sbuf", [128, 512], "float32"),
     "cm": ("sbuf", [128, 2048], "bfloat16"), "cs": ("sbuf", [128, 1024], "bfloat16"),
-    "sg": ("sbuf", [128, 512], "bfloat16"), "junk": ("sbuf", [128, 512], "bfloat16"), "ls": ("sbuf", [128, 4], "float32"),
+    "sg": ("sbuf", [128, 1152], "bfloat16"), "junk": ("sbuf", [128, 1152], "bfloat16"), "ls": ("sbuf", [128, 4], "float32"),
     "raw": ("sbuf", [128, 512], "float32"), "valo": ("sbuf", [128, 64], "float32"),
     "wins": ("sbuf", [128, 528], "float32"), "tzs": ("sbuf", [128, 128], "float32"),
-    "msg": ("sbuf", [128, 16], "float32"), "cu": ("sbuf", [128, 4], "uint16"), "cf": ("sbuf", [128, 4], "float32"), "at": ("sbuf", [128, 20], "float32"),
+    "msg": ("sbuf", [128, 16], "float32"), "cu": ("sbuf", [128, 4], "uint16"), "cf": ("sbuf", [128, 4], "float32"), "at": ("sbuf", [128, 40], "float32"),
     "spm": ("sbuf", [128, 4], "float32"), "pum": ("sbuf", [128, 8], "uint16"), "valm": ("sbuf", [128, 64], "float32"),
     "osr": ("sbuf", [128, 528], "float32"), "cb": ("sbuf", [128, 96], "bfloat16"), "cr": ("sbuf", [64, 96], "bfloat16"),
-    "ct": ("sbuf", [64, 32], "bfloat16"), "cn": ("sbuf", [64, 32], "float32"),
-    "bc": ("sbuf", [128, 8], "float32"), "bs": ("sbuf", [128, 8], "float32"), "off2": ("sbuf", [128, 8], "uint16"),
-    "yx": ("sbuf", [128, 272], "float32"), "fs": ("sbuf", [128, 256], "float32"),
+    "ct": ("sbuf", [64, 32], "bfloat16"), "cn": ("sbuf", [128, 32], "float32"), "off2": ("sbuf", [128, 16], "uint16"),
+    "yx": ("sbuf", [128, 400], "float32"), "fs": ("sbuf", [128, 384], "float32"),
     "ps": ("sbuf", [128, 2], "float32"), "sel": ("sbuf", [128, 2], "float32"), "vd": ("sbuf", [128, 2], "float32"),
-    "ba": ("sbuf", [128, 768], "bfloat16"), "bu": ("sbuf", [128, 400], "float32"),
-    "sq": ("sbuf", [128, 528], "bfloat16"), "lq": ("sbuf", [128, 2], "float32"),
+    "ba": ("sbuf", [128, 768], "bfloat16"), "bu": ("sbuf", [128, 400], "float32"), "bt": ("sbuf", [128, 192], "bfloat16"),
+    "sq": ("sbuf", [128, 528], "bfloat16"), "lq": ("sbuf", [128, 3], "float32"),
     "cp": ("sbuf", [128, 64], "float32"), "idr": ("sbuf", [128, 256], "float32"), "idb": ("sbuf", [128, 128], "float32"),
 }
 for _n in ("1", "2"):
     SCRATCH["pu" + _n] = ("sbuf", [128, 4], "uint16")
-    SCRATCH["win" + _n] = ("sbuf", [128, 528], "bfloat16")
-    SCRATCH["tz" + _n] = ("sbuf", [128, 288], "bfloat16")
-    SCRATCH["qa" + _n] = ("sbuf", [128, 416], "float32")
-    SCRATCH["qb" + _n] = ("sbuf", [64, 16], "float32")
-    SCRATCH["qc" + _n] = ("sbuf", [128, 16], "float32")
+    SCRATCH["win" + _n] = ("sbuf", [128, 528], "float32" if _n == "1" else "bfloat16")
+    SCRATCH["tz" + _n] = ("sbuf", [128, 288], "float32" if _n == "1" else "bfloat16")
+    SCRATCH["qa" + _n] = ("sbuf", [64, 432], "float32")
+    SCRATCH["qc" + _n] = ("sbuf", [128, 24], "float32")
     SCRATCH["lst" + _n] = ("sbuf", [128, 16], "uint16")
 
 SEMAPHORES = ["v", "s", "t", "gc", "du", "dx0", "dx1", "dx2", "dx3", "dw", "dy", "did",
-              "h1c", "h1s", "h2c", "h2s", "hm", "hr", "hq", "hp", "hi", "sent"]
+              "h1c", "h1s", "h2c", "h2s", "hm", "hr", "hq", "hp", "hi", "hj", "sent"]
 
 
 def rank_program(g, core, T, topo):
@@ -97,7 +99,11 @@ def rank_program(g, core, T, topo):
 
     B = [0, 1, 2, 3] if odd else [3, 2, 1, 0]
     du = done(s.dma_start(T.ur[:, 8:16], T.u[:, 0:8]), "du", 16)
-    dx = {d: done(y.dma_start(T.xb[:, 512 * d:512 * d + 512], T.x[:, 512 * d:512 * d + 512]), "dx%d" % d, 16) for d in B}
+    dx = {}
+    for grp in OPT["loads"]:
+        a, b = 512 * min(B[i] for i in grp), 512 * max(B[i] for i in grp) + 512
+        k = done(y.dma_start(T.xb[:, a:b], T.x[:, a:b]), "dx%d" % grp[0], 16)
+        dx.update({B[i]: k for i in grp})
     wait("y", dx[B[3]])
     dw = done(y.dma_start(T.wb[:, 0:1024], T.w[:, 0:1024]), "dw", 16)
 
@@ -107,46 +113,48 @@ def rank_program(g, core, T, topo):
         return G(g.iota(buf, pattern, base, cm))
     k_it = iota(T.it[:, 0:128], [[1, 128]], 128, -1, False)
     k_ip = iota(T.ip[:, 0:2], [[0, 2]], 0, 1, False)
-    k_i3 = iota(T.i3[:, 0:64], [[128, 4], [1, 16]], -256, 0)
-    k_i4 = iota(T.i4[:, 0:32], [[1, 2], [2, 16]], -128, 0)
-    k_i6 = iota(T.i6[:, 0:8], [[16, 8]], 0, 0)
-    iota(T.seg[:, 0:128], [[0, 128]], 1, 0)
+    sign1, best = (1.0, OP.max) if odd else (-1.0, OP.min)
+    kb = iota(T.bg[:, 2:3], [[0, 1]], 0, 0)
     k = iota(T.gr[:, 0:32], [[0, 32]], 0, 1)
-    iota(T.gr[:, 32:64], [[0, 8], [64 * SLOT, 2], [32 * SLOT, 2]] if False else [[0, 8], [128, 4]] if OPT["three"] else [[0, 16], [128, 2]], 0, 1)
-    iota(T.gr[:, 64:96], [[0, 16], [32 * 9, 2]], 0, 1)
+    iota(T.gr[:, 32:64], [[0, 16], [32 * SLOT, 2]], 64 * SLOT * Q, 1)
+    wait("g", kb)
+    kb = G(g.affine_select(T.bg[:, 1:2], T.bg[:, 2:3], [[0, 1]], OP.not_equal, -BIG * sign1, -88, 1))
     wait("g", k)
     iota(T.gr[:, 2:10], [[32, 4], [160, 2]], 0, 0)
-    k_gr = iota(T.gr[:, 18:26], [[32, 4], [-128, 2]], 128, 0)
-    k_seg = iota(T.seg[:, 0:128:32], [[0, 4]], 0, 0)
+    iota(T.gr[:, 18:26], [[32, 4], [-128, 2]], 128, 0)
+    wait("g", kb)
+    k_bg = G(g.affine_select(T.bg[:, 0:1], T.bg[:, 1:2], [[0, 1]], OP.not_equal, -BIG * sign1, -120, 1))
+    k_gr = iota(T.gr[:, 64:96], [[0, 32]], 128, 1)
+    k_i3 = iota(T.i3[:, 0:64], [[128, 4], [1, 16]], 0, 0)
+    k_i4 = iota(T.i4[:, 0:32], [[1, 2], [2, 16]], 0, 0)
     lo1, lom = (384, 16) if odd else (16, 384)
 
     V(v.memset(T.ur[:, 0:8], 0.0))
     k_ur = V(v.memset(T.ur[:, 16:520], 0.0))
     k_zo = V(v.memset(T.zoff[:, 0:8], 2))
-    V(v.memset(T.win1[:, lo1 - 16:lo1 + 144], 0.0))
+    V(v.memset(T.one[:, 0:256], -sign1))
     wait("s", k_ur)
     for a, b in ((0, lom), (lom + K, 528)):
         S(s.activation(T.osr[:, a:b], T.ur[:, 16:16 + b - a], IDENT, bias=BIG))
-    S(s.activation(T.wins[:, lo1:lo1 + K], T.ur[:, 16:16 + K], COPY))
+    S(s.activation(T.wins[:, lo1:lo1 + K], T.ur[:, 16:16 + K], IDENT, bias=-BIG * sign1))
+    S(s.activation(T.idr[:, 64:256], T.ur[:, 16:208], COPY))
     wait("v", k_it)
     if odd:
         k_tri = V(v.tensor_scalar(T.tri[:, 0:128], T.it[:, 0:128], 128.0, None, OP.is_gt))
     else:
         k_tri = V(v.tensor_scalar(T.tri[:, 0:128], T.it[:, 0:128], 128.0, -1.0, OP.is_lt, OP.mult))
-    V(v.tensor_scalar(T.ita[:, 0:16], T.it[:, 0:16], 15, None, OP.bitwise_and))
+    V(v.tensor_scalar(T.ita[:, 0:64], T.it[:, 0:64], 15, None, OP.bitwise_and))
     wait("v", k_ip)
     V(v.tensor_scalar(T.pca[:, 0:1], T.ip[:, 0:1], 112, None, OP.bitwise_and))
     k = V(v.tensor_scalar(T.pca[:, 1:2], T.ip[:, 0:1], 15, None, OP.bitwise_and))
-    V(v.memset(T.win2[:, 0:160], 0.0))
     V(v.memset(T.cb[:, 64:96], 0.0))
     V(v.memset(T.cp[:, 0:64], 0.0))
     wait("v", k)
+    V(v.tensor_scalar(T.keep[:, 0:1], T.pca[:, 1:2], 8.0, sign1, OP.not_equal, OP.mult))
     k_pc = V(v.tensor_copy(T.pcf[:, 0:2], T.pca[:, 0:2]))
-    V(v.tensor_scalar(T.nb[:, 0:16], T.ita[:, 0:16], 0.0, -BIG, OP.not_equal, OP.mult))
-    k_nb = V(v.tensor_scalar(T.dg[:, 0:16], T.ita[:, 0:16], 0.0, None, OP.is_equal))
-    wait("s", k_pc, k_i3)
-    k = S(s.activation(T.pcq[:, 1:2], T.pcf[:, 0:1], COPY, scale=2.0))
-    k_v1 = S(s.activation(T.vals1[:, 0:64], T.i3[:, 0:64], IDENT, bias=T.pcf[:, 0:1]))
+    k_nb = V(v.tensor_scalar(T.nb[:, 0:64], T.ita[:, 0:64], 0.0, -BIG, OP.not_equal, OP.mult))
+    wait("s", k_pc)
+    S(s.activation(T.pcq[:, 1:2], T.pcf[:, 0:1], COPY, scale=2.0))
 
     wait("v", du, k_ur)
     k_u0 = V(v.quantize_mx(T.uq0[:, 0:130], T.us0[:, 0:130], T.ur[:, 0:520]))
@@ -164,11 +172,8 @@ def rank_program(g, core, T, topo):
         quant(0)
     wait("s", k_u0, k_zo)
     k_us = S(s.activation(T.us[:, 0:128], T.us0[:, 0:130].indirect(T.zoff[:, 0:8]), COPY))
-    wait("s", k, k_i6)
-    k = S(s.activation(T.jt[:, 0:8], T.i6[:, 0:8], IDENT, bias=T.pcf[:, 1:2]))
-    S(s.activation(T.vals2[:, 0:32], T.i4[:, 0:32], IDENT, bias=T.pcq[:, 1:2]))
-    wait("s", k)
-    S(s.activation(T.jc[:, 0:8], T.jt[:, 0:8], COPY, scale=1.0 / 128))
+    wait("s", k_bg)
+    k_b1 = S(s.activation(T.pcq[:, 2:3], T.pcf[:, 0:1], IDENT, bias=T.bg[:, 0:1], scale=T.keep[:, 0:1]))
 
     kr, kp, kt, kl, kc, ks = {}, {}, {}, {}, {}, {}
     strict, loose = (OP.is_lt, OP.is_le) if odd else (OP.is_gt, OP.is_ge)
@@ -182,16 +187,22 @@ def rank_program(g, core, T, topo):
         kr[i] = X(t.matmul_mx(row[B[i]], T.uq[:, 0:128], T.us[:, 0:128], T.xq[:, e], T.xs[:, e], True, True))
 
     def down(i):
-        c, bank = B[i], 512 * (i // 2)
-        e, m = slice(128 * c, 128 * c + 128), slice(2 - 2 * (c % 2), 130 - 2 * (c % 2))
+        grp = [h for h in OPT["banks"] if i in h][0]
+        c, bank = B[i], 512 * OPT["banks"].index(grp)
+        at = 2 * (c - min(B[h] for h in grp))
+        e, m = slice(128 * c, 128 * c + 128), slice(2 - at, 130 - at)
         wait("t", k_u0, kq[c])
-        return X(t.matmul_mx(T.psp[:, bank:bank + 128], T.xq[:, e], T.xs[:, e], T.uq0[:, m], T.us0[:, m], i % 2 == 0, i % 2 == 1))
+        kd[i] = X(t.matmul_mx(T.psp[:, bank:bank + 128], T.xq[:, e], T.xs[:, e], T.uq0[:, m], T.us0[:, m], i == grp[0], i == grp[-1]))
 
-    def scores(i, k):
-        c, src = min(B[i:i + 2]), T.psp[:, 256 * i:256 * i + 4:2]
-        wait("s", k)
-        kp[i] = kp[i + 1] = S(s.activation(T.sp[:, c:c + 2], src, COPY))
-        return S(s.activation(T.dl[:, c:c + 2], src, ACT.Abs, bias=TINY, scale=STEP))
+    def scores(i):
+        grp = [h for h in OPT["banks"] if i in h][0]
+        c, n, bank = min(B[h] for h in grp), len(grp), 512 * OPT["banks"].index(grp)
+        src = T.psp[:, bank:bank + 2 * n:2]
+        wait("s", *[kd[h] for h in grp])
+        a = S(s.activation(T.sp[:, c:c + n], src, COPY))
+        b = S(s.activation(T.dl[:, c:c + n], src, ACT.Abs, bias=TINY, scale=STEP))
+        for h in grp:
+            kp[h], kd["s", h] = a, b
 
     def bound(i, k):
         c = B[i]
@@ -207,6 +218,7 @@ def rank_program(g, core, T, topo):
 
     def cell(i, j):
         c, d, o = B[i], B[j], 512 * i + 128 * mine_v[i].index(j)
+        wait("v", *[k for (h, e), k in ks.items() if e == j])
         if i == j:
             wait("v", kr[j], kt[i])
             kc[i, j] = V(v.tensor_tensor(cm[:, o:o + 128], row[d], T.thr[:, 128 * c:128 * c + 128], strict))
@@ -218,13 +230,13 @@ def rank_program(g, core, T, topo):
         return V(v.tensor_tensor_scan(out, buf[:, o:o + n], buf[:, o + n:o + 2 * n], first, OP.add, OP.add))
 
     def signs(i, j):
-        o = 256 * (i - 2) + 128 * mine_s[i].index(j)
-        wait("s", kp[i], *[kc[h, j] for h in range(4) if j in mine_v[h]])
-        ks[i] = S(s.activation(T.sg[:, o:o + 128], row[B[j]], ACT.Sign, bias=sp[B[i]], scale=-1.0))
+        o = 384 * (i - 1) + 128 * mine_s[i].index(j)
+        wait("s", kp[i], kr[j], *[k for (h, e), k in kc.items() if e == j])
+        ks[i, j] = S(s.activation(T.sg[:, o:o + 128], row[B[j]], ACT.Sign, bias=sp[B[i]], scale=-1.0))
 
     def sum_signs(i):
-        o, n = 256 * (i - 2), 128 * len(mine_s[i])
-        wait("s", ks[i])
+        o, n = 384 * (i - 1), 128 * len(mine_s[i])
+        wait("s", *[ks[i, j] for j in mine_s[i]])
         kl[i] = S(s.activation(T.junk[:, o:o + n], T.sg[:, o:o + n], ACT.Relu, scale=1.0 if odd else -1.0, accum_out=T.ls[:, i:i + 1]))
 
     def total(i):
@@ -241,45 +253,66 @@ def rank_program(g, core, T, topo):
             kn_["pu"] = V(v.tensor_scalar(T.pu1[:, c:c + 1], src, T.ls[:, i:i + 1], lift, OP.add, OP.add))
         else:
             kn_["pu"] = V(v.tensor_scalar(T.pu1[:, c:c + n], src, lift, None, OP.add))
+        for h in range(i, i + n):
+            kn_["p", h] = kn_["pu"]
 
     def lists(i):
         if i == 0:
             wait("v", k_gr)
             kn_["gt"] = V(v.transpose(T.gt[:, 0:96], T.gr[:, 0:96]))
-        else:
+        elif i == 1:
             wait("v", kn_["gt"])
-            V(v.tensor_scalar(T.goff[:, 0:2], T.gt[:, 0:2], 1.0 / 32, None, OP.mult))
-            V(v.tensor_scalar(T.eoff[:, 16:20:2], T.gt[:, 32:96:32], 1.0 / 32, None, OP.mult))
+            V(v.tensor_scalar(T.goff[:, 0:6:2], T.gt[:, 0:96:32], 1.0 / 32, None, OP.mult))
+        elif i == 2:
+            wait("v", k_bg)
+            kn_["w"] = V(v.tensor_scalar(T.win1[:, lo1 - 16:lo1 + 144], T.ur[:, 16:176], T.bg[:, 0:1], None, OP.add))
+        else:
+            wait("s", k_i3, k_b1)
+            kn_["v1"] = S(s.activation(T.vals1[:, 0:64], T.i3[:, 0:64], IDENT, bias=T.pcq[:, 2:3], scale=T.keep[:, 0:1]))
+
+    def alone(i):
+        c = B[i]
+        wait("s", k_nb, kp[i])
+        kn_["v", i] = S(s.activation(T.valo[:, 16 * c:16 * c + 16], T.nb[:, 0:16], IDENT, bias=sp[c], scale=sign1))
+
+    def scatter(i, what):
+        c = min(B[i:i + 2])
+        wait("v", kn_["p", i], kn_["p", i + 1], *((kn_["v", i], kn_["v", i + 1]) if what else (kn_["v1"], kn_["w"])))
+        if "x%d" % what in kn_:
+            wait("v", kn_["x%d" % what])
+        win, vals = (T.wins, T.valo) if what else (T.win1, T.vals1)
+        kn_["x%d" % what] = V(v.tensor_copy(win[:, 0:528].indirect(T.pu1[:, c:c + 2]), vals[:, 16 * c:16 * c + 32]))
 
     kn_, kd = {}, {}
     c01 = min(B[0:2])
-    call = {"q": quant, "d": lambda i: kd.update({i: down(i)}), "r": rows, "s": lambda i: kd.update({i: scores(i, kd[i + 1])}),
-            "b": lambda i: bound(i, kd[i & 2]), "c": cell, "g": signs, "l": sum_signs, "t": total, "p": places, "z": lists}
+    call = {"v": alone, "x": scatter,"q": quant, "d": down, "r": rows, "s": scores,
+            "b": lambda i: bound(i, kd["s", i]), "c": cell, "g": signs, "l": sum_signs, "t": total, "p": places, "z": lists}
     for step in OPT["order"].split():
         call[step[0]](*[int(ch) for ch in step[1:]])
     k_pu = kn_["pu"]
 
     def invert(n, ready, cols, vals, lo, lift, fill, wide=9):
         W = lambda b: T[b + n]
-        wait("v", *ready)
-        a = V(v.tensor_copy(W("win")[:, 0:528].indirect(W("pu")[:, 0:cols]), vals[:, 0:16 * cols]))
+        if cols:
+            wait("v", *ready)
+            a = V(v.tensor_copy(W("win")[:, 0:528].indirect(W("pu")[:, 0:cols]), vals[:, 0:16 * cols]))
+        else:
+            a = ready
         fill(0)
         wait("v", a)
         V(v.transpose(W("tz")[:, 0:128], W("win")[:, lo:lo + 128]))
         a = V(v.transpose(W("tz")[:, 128:288], W("win")[:, lo - 16:lo + 144]))
         fill(1)
         wait("v", a)
-        a = V(v.tensor_tensor(W("qa")[:, 31:288:32], W("tz")[:, 0:288:32], W("tz")[:, 16:288:32], OP.add))
-        a = fill(2) or a
-        wait("v", a)
-        a = V(v.tensor_tensor(W("qb")[0:64, 0:wide], W("qa")[0:64, 31:32 * wide:32], W("qa")[64:128, 31:32 * wide:32], OP.add))
+        a = V(v.tensor_tensor_scan(W("qa")[0:64, 143:431:8], W("tz")[0:64, 0:288:8], W("tz")[64:128, 0:288:8], 0.0, best, OP.add))
+        half = lambda p: W("qa")[p:p + 32, 447 - 32 * wide:431:32]
         fill(3)
         wait("v", a)
         for h in range(4):
-            a = V(v.tensor_tensor(W("qc")[32 * h:32 * h + 32, 0:wide], W("qb")[0:32, 0:wide], W("qb")[32:64, 0:wide], OP.add))
+            a = V(v.tensor_tensor(W("qc")[32 * h:32 * h + 32, 17 - wide:17], half(0), half(32), best))
         fill(4)
         wait("v", a)
-        b = V(v.tensor_scalar(W("lst")[:, 0:16], W("qc")[:, 0:9].indirect(T.goff[:, 0:1]), lift, None, OP.add))
+        b = V(v.tensor_scalar(W("lst")[:, 0:16], W("qc")[:, 8:17].indirect(T.goff[:, 0:1]), sign1, None, OP.mult))
         fill(5)
         return a, b
 
@@ -295,7 +328,7 @@ def rank_program(g, core, T, topo):
         wait("g", *ready)
         rid, pid = topo.addr(dst, core)
         n = len(topo.engines(core, dst))
-        codes = sem in ("h1c", "h2c")
+        codes = sem in ("h1c", "h2c", "h1d", "h2d")
         g.remote_dma(o.bitcast(dt.uint8) if codes else o, i.bitcast(dt.uint8) if codes else i, T.sem[sem], T.sem["sent"], pid, rid,
                      topo.mask(core, dst))
         count["sent"] = count.get("sent", 0) + n
@@ -306,42 +339,48 @@ def rank_program(g, core, T, topo):
         return V(v.quantize_mx(T.wq[:, 128 * o:128 * o + 128], T.ws[:, 128 * o:128 * o + 128], T.wb[:, 512 * o:512 * o + 512]))
 
     m0 = SLOT * rank
+    more = 2 * K if P < Q else 0
     mate = T.cores[rank ^ 1]
-    in_raw = [remote(T.spm[:, c:c + 2], T.sp[:, c:c + 2], mate, sem, kp[i]) for c, sem, i in ((c01, "hr", 0), (2 - c01, "hq", 2))]
-    k_i5 = iota(T.i5[:, 0:16], [[1, 8], [0, 2]], 0, 0, False)
-    for i, (base, step) in enumerate(((16, 1), (143, -1), (0, 0 if OPT["three"] else 256))):
-        k_pt = iota(T.pt[:, i:i + 1], [[0, 1]], base, step)
-    iota(T.sq[:, 128:129], [[0, 1]], 0, -1)
-    k_sq0 = iota(T.sq[:, 129:130], [[0, 1]], -16, 0)
+    k_i5 = iota(T.i5[:, 0:16], [[1, 8], [0, 2]], 2 * SLOT * Q, 0, False)
+    in_raw = [remote(T.spm[:, B[0]:B[0] + 1], T.sp[:, B[0]:B[0] + 1], mate, "hr", kp[0]),
+              remote(T.spm[:, odd:odd + 3], T.sp[:, odd:odd + 3], mate, "hq", kp[3])]
+    k_iy = iota(T.iy[:, 0:256], [[1, 256]], 0, 0)
     in_places = remote(T.pum[:, 0:4], T.pu1[:, 0:4], mate, "hp", k_pu)
-    wait("s", k_nb)
-    for c in range(4):
-        k_vo = S(s.activation(T.valo[:, 16 * c:16 * c + 16], T.dg[:, 0:16], COPY, scale=sp[c]))
     wait("s", *kc.values())
     for c in B:
         k_raw = S(s.activation(T.raw[:, 128 * c:128 * c + 128], row[c], COPY))
-    S(s.activation(T.idr[:, 64:256], T.thr[:, 0:192], COPY, scale=0.0))
-    wait("s", *in_raw)
-    for c in range(4):
-        S(s.activation(T.valm[:, 16 * c:16 * c + 16], T.nb[:, 0:16], IDENT, bias=T.spm[:, c:c + 1]))
+    wait("s", k_i4)
+    for i, (base, step) in enumerate(((113.0, 1.0), (113.0, 1.0), (112.0, -16.0)) if odd else ((128.0, -1.0), (-129.0, 1.0), (0.0, 16.0))):
+        k_kq = S(s.activation(T.kq[:, i:i + 1], T.pcf[:, 1:2], IDENT, bias=base, scale=step))
+    S(s.activation(T.pt[:, 3:4], T.pcf[:, 1:2], IDENT, bias=T.pcf[:, 0:1]))
+    S(s.activation(T.pcq[:, 0:1], T.pcq[:, 1:2], IDENT, bias=T.bg[:, 0:1], scale=T.keep[:, 0:1]))
+    S(s.activation(T.win2[:, 0:160], T.thr[:, 0:160], IDENT, bias=T.bg[:, 0:1], scale=0.0))
+    if not OPT["valm"]:
+        wait("s", *in_raw)
+        for c in range(4):
+            S(s.activation(T.valm[:, 16 * c:16 * c + 16], T.nb[:, 0:16], IDENT, bias=T.spm[:, c:c + 1]))
 
     lane = []
 
     def sorted_scores(i):
-        if i == 0:
-            wait("v", k_vo)
-            lane.append(V(v.tensor_copy(T.wins[:, 0:528].indirect(T.pu1[:, 0:4]), T.valo[:, 0:64])))
-        elif i == 1:
-            wait("v", lane[0])
+        apart = OPT["apart"]
+        if i == apart:
+            wait("v", kn_["x1"])
             lane.append(V(v.transpose(T.tzs[:, 0:128], T.wins[:, lo1:lo1 + K])))
-        elif i == 2:
-            wait("v", lane[1], k_seg)
-            return V(v.tensor_tensor_scan(T.qa1[:, 288:416], T.seg[:, 0:128], T.tzs[:, 0:128], 0.0, OP.mult, OP.add))
-        elif i == 5:
-            wait("v", k_i5)
-            lane.append(V(v.tensor_copy(T.eoff[:, 0:16], T.i5[:, 0:16])))
+        elif i == 1 + 2 * apart:
+            wait("v", lane[0])
+            lane.append(V(v.tensor_tensor_scan(T.qa1[0:64, 0:128], T.tzs[0:64, 0:128], T.tzs[64:128, 0:128], -BIG * sign1, best, best)))
+        elif i == 5 and not apart:
+            wait("v", k_iy, k_kq)
+            V(v.tensor_scalar(T.jump[:, 0:256], T.iy[:, 0:256], T.kq[:, 0:1], float(K), OP.is_equal, OP.mult))
+        elif apart and i > 3:
+            wait("v", lane[1])
+            for h in OPT["folds"][i - 4]:
+                lane.append(V(v.tensor_tensor(T.qc1[32 * h:32 * h + 32, 4:8], T.qa1[0:32, 31:128:32], T.qa1[32:64, 31:128:32], best)))
 
-    k_q1, k_l1 = invert("1", (k_pu, k_v1), 4, T.vals1, lo1, 256.0, sorted_scores, 13)
+    k_q1, k_l1 = invert("1", kn_["x0"], 0, T.vals1, lo1, 256.0, sorted_scores, 9 if OPT["apart"] else 13)
+    if OPT["apart"]:
+        k_q1 = lane[-1]
 
     def to_many(src, dsts, sem, *ready):
         wait("g", *ready)
@@ -355,11 +394,21 @@ def rank_program(g, core, T, topo):
                                               dsts=list(dsts.values()))], local_sem=T.sem["sent"])
         count["sent"] += n
         return (sem, len(dsts) * n)
-    slot = T.msg[:, SLOT * odd:SLOT * odd + 4]
-    three = OPT["three"]
-    in_msg = to_many(T.qc1[:, 9:13], {2: slot, 3: slot, 1: T.msg[:, 8:12]} if three else {2: slot, 3: slot}, "hm", k_q1)
-    wait("s", k_q1)
-    k_at = S(s.activation(T.at[:, 0:16], T.qc1[:, 0:13].indirect(T.eoff[:, 18:19]), COPY))
+    slot = T.msg[:, m0:m0 + SLOT]
+    two = OPT["two"]
+    if not OPT.get("late_msg"):
+        in_msg = to_many(T.qc1[:, 4:8], {x: slot for x in (2, 3)}, "hm", k_q1)
+
+    def at_t():
+        wait("s", k_q1)
+        k = S(s.activation(T.at[:, 0:16], T.qc1[:, 8:17].indirect(T.goff[:, 0:1]), COPY, scale=sign1))
+        if two == "early":
+            wait("s", k)
+        return S(s.activation(T.at[:, 1:17] if two == "early" else T.at[:, 24:40], T.qc1[:, 0:8].indirect(T.goff[:, 4:5]), COPY))
+    if two == "early":
+        k_at = at_t()
+    if two == "early":
+        in_ids = remote(T.at[:, 20:22], T.at[:, 0:2], mate, "hi", k_at)
 
     off = T.lst1[:, 2:10]
     mine = T.osr[:, lom:lom + K]
@@ -367,175 +416,251 @@ def rank_program(g, core, T, topo):
     wait("s", k_l1, k_raw)
     k_os = S(s.activation(mine, T.raw[:, 0:512].indirect(off), COPY))
     b1 = pick_scales(T.s1[:, 0:K], T.xs[:, 0:512], off)
-    in1c = remote(T.c1[:, K:2 * K], T.c1[:, 0:K], mate, "h1c", a1)
-    in1s = remote(T.s1[:, K:2 * K], T.s1[:, 0:K], mate, "h1s", b1)
-    if three:
-        in_ids = to_many(T.lst1[:, 0:1], {x: T.cu[:, x:x + 1] for x in (1, 2, 3)}, "hi")
-    else:
-        in_ids = to_many(T.at[:, 0:1], {x: T.at[:, 16 + x:17 + x] for x in (1, 2, 3)}, "hi", k_at)
+    if two != "early":
+        k_at = at_t()
+    wait("s", k_os)
+    S(s.activation(T.sq[:, 129:130], T.pcf[:, 0:1], IDENT, bias=-16.0 - more, scale=0.0))
+    S(s.activation(T.sq[:, 128:129], T.pt[:, 3:4], COPY, scale=-1.0))
+    for i, (base, step) in enumerate(((16.0, 1.0), (143.0, -1.0), (143.0 + more, -1.0))):
+        k_pt = k_sq0 = S(s.activation(T.pt[:, i:i + 1], T.pt[:, 3:4], IDENT, bias=base, scale=step))
 
+    extra = []
+    if OPT.get("halves"):
+        in1a = remote(T.c1[:, K:K + 64], T.c1[:, 0:64], mate, "h1d", a1)
+        in1c = remote(T.c1[:, K + 64:2 * K], T.c1[:, 64:K], mate, "h1c", a1)
+        extra.append(in1a)
+    else:
+        in1c = remote(T.c1[:, K:2 * K], T.c1[:, 0:K], mate, "h1c", a1)
+    if OPT.get("late_msg"):
+        in_msg = to_many(T.qc1[:, 4:8], {x: slot for x in (2, 3)}, "hm", k_q1)
+    if two == "mid":
+        in_ids = remote(T.at[:, 16:18], T.at[:, 0:2], mate, "hi", k_at)
+    in1s = remote(T.s1[:, K:2 * K], T.s1[:, 0:K], mate, "h1s", b1)
+    if two == "late":
+        in_ids = remote(T.at[:, 16:18], T.at[:, 0:2], mate, "hi", k_at)
+    if two == "v4" and OPT.get("pair"):
+        in_ids = remote(T.at[:, 20:21], T.at[:, 0:1], mate, "hi", k_at)
+    elif two == "v4":
+        in_ids = to_many(T.at[:, 0:1], {x: T.at[:, 16 + x:17 + x] for x in (1, 2, 3)}, "hi", k_at)
+    if not two:
+        in_ids = to_many(T.lst1[:, 0:1], {x: T.cu[:, x:x + 1] for x in (1, 2, 3)}, "hi")
+
+    if OPT["valm"]:
+        wait("v", lane[2], *in_raw)
+        a = V(v.tensor_tensor(T.valm[:, 0:64], T.spm[:, 0:4].indirect(T.eoff[:, 16:20]), T.nb[:, 0:64], OP.add))
     k_w = [w_codes(0)]
-    wait("v", in_places, k_os)
+    wait("v", k_i5)
+    k_eo = V(v.tensor_copy(T.eoff[:, 0:16], T.i5[:, 0:16]))
+    wait("v", in_places, k_os, *([a] if OPT["valm"] else []))
     a = V(v.tensor_tensor(T.cb[:, 0:64], T.osr[:, 0:528].indirect(T.pum[:, 0:4]), T.valm[:, 0:64], OP.is_le if odd else OP.is_lt))
     k_w.append(w_codes(1))
     wait("v", a)
     a = V(v.tensor_tensor_scan(T.cr[0:64, 0:96], T.cb[0:64, 0:96], T.cb[64:128, 0:96], 0.0, OP.add, OP.add))
     wait("v", a)
     a = V(v.transpose(T.ct[0:64, 0:32], T.cr[0:64, 64:96]))
+    V(v.tensor_tensor_scan(T.tab[:, 0:256], T.one[:, 0:256], T.jump[:, 0:256], T.kq[:, 1:2], OP.add, OP.add))
     wait("v", a)
-    for h in range(2):
+    for h in range(4):
         a = V(v.tensor_tensor_scan(T.cn[32 * h:32 * h + 32, 0:32], T.ct[0:32, 0:32], T.ct[32:64, 0:32], 0.0, OP.add, OP.add))
-    wait("v", a)
-    for h in range(2):
-        o, i = T.bc[64 * h:64 * h + 64, 0:8], T.jt[64 * h:64 * h + 64, 0:8]
-        if odd:
-            a = V(v.tensor_scalar(o, i, T.cn[0:64, 31:32], None, OP.is_lt))
-        else:
-            a = V(v.tensor_scalar(o, i, T.cn[0:64, 31:32], float(K), OP.add, OP.is_ge))
-    wait("s", in_msg, lane[2], b1)
-    kx = S(s.activation(T.yx[:, 256:272], T.msg[:, 0:16 if three else 8].indirect(T.eoff[:, 16:17]), COPY))
-    ky = {h: S(s.activation(T.yx[:, 128 * h:128 * h + 128], T.msg[:, 0:8].indirect(T.eoff[:, 8 * h:8 * h + 8]), COPY)) for h in (1, 0)}
-    ps, sel = [[T[b][:, j:j + 1] for j in range(2)] for b in ("ps", "sel")]
-    me, him, E, O = T.at[:, 1:2], T.yx[:, 258:259] if three else T.psp[:, 0:1], T.yx[:, 256:257], T.yx[:, 257:258]
-
-    def with_mate(*ready):
-        wait("v", k_at, *ready)
-        return V(v.tensor_tensor(ps[P], me, him, OP.max))
-
-    def turn(h):
-        wait("v", ky[h])
-        return V(v.transpose(T.fs[:, 128 * h:128 * h + 128], T.yx[:, 128 * h:128 * h + 128]))
-    wait("v", kx)
-    k_pq = V(v.tensor_tensor(ps[Q], E, O, OP.max))
-    V(v.tensor_tensor(sel[Q], O, E, OP.is_gt))
-    if three:
-        k_sel = with_mate()
-    wait("v", a)
-    a = V(v.tensor_tensor(T.bs[:, 0:8], T.bc[:, 0:8], T.jc[:, 0:8], OP.add))
-    kf = turn(1)
-    wait("v", a)
-    k_o2 = V(v.tensor_scalar(T.off2[:, 0:8], T.bs[:, 0:8], 128.0, None, OP.mult))
-    kg = turn(0)
-
-    wait("t", in1c, in1s, a1, b1)
-    kb = X(t.matmul_mx(T.psf[:, 0:128], T.uq[:, 0:128], T.us[:, 0:128], T.c1[:, K:2 * K], T.s1[:, K:2 * K], True, True))
-    if not three:
-        kd = X(t.matmul_mx(T.psp[:, 0:128], T.c1[:, K:2 * K], T.s1[:, K:2 * K], T.uq0[:, 2:130], T.us0[:, 2:130], True, True))
-    a2 = pick_codes(T.c2[:, own], T.c1[:, 0:256], T.off2[:, 0:8], k_o2, in1c)
-    wait("s", k_pq)
-    ks = S(s.activation(T.sq[:, 144:272], mine, ACT.Sign, bias=ps[Q], scale=-1.0))
-    wait("s", kf)
-    kt2 = S(s.activation(T.sq[:, 0:128], T.fs[:, 128:256], ACT.Sign, bias=E, scale=-1.0))
-    b2 = pick_scales(T.s2[:, own], T.s1[:, 0:256], T.off2[:, 0:8], k_o2, in1s)
-    in2c = remote(T.c2[:, own], T.c2[:, own], T.cores[rank ^ 2], "h2c", a2)
-    in2s = remote(T.s2[:, own], T.s2[:, own], T.cores[rank ^ 2], "h2s", b2)
-
+    n_wins = T.cn[:, 31:32]
     def products(side, bank, *ready):
         wait("t", *k_w, *ready)
         return [X(t.matmul_mx(bank[:, 512 * (o + 2):512 * (o + 2) + 128], T.wq[:, 128 * o:128 * o + 128], T.ws[:, 128 * o:128 * o + 128],
                               T.c2[:, side], T.s2[:, side], True, True)) for o in range(2)]
-    ko = products(own, T.psf, a2, b2)
-    kn = products(arr, T.psp, in2c, in2s)
 
-    his = T.psf[:, 0:128]
-    bu = lambda i, n=64: T.bu[:, 64 * i:64 * i + n]
+    fs = lambda h, n=1: T.fs[:, 128 * h:128 * (h + n)]
+    yx = lambda h: T.yx[:, 128 * h:128 * h + 128]
+    at = lambda r: T.yx[:, 384 + r:385 + r]
+    ba = lambda i, n=1: T.ba[:, 128 * i:128 * (i + n)]
     last = lambda i: T.bu[:, 64 * i + 63:64 * i + 64]
-    wait("s", ks)
-    S(s.activation(T.sq[:, 272:400], T.sq[:, 144:272], ACT.Relu, scale=1.0 if P < Q else -1.0, accum_out=T.lq[:, 0:1]))
-    wait("s", kt2, k_sq0)
-    kq2 = S(s.activation(T.junk[:, 0:130], T.sq[:, 0:130], ACT.Relu, scale=-1.0, accum_out=T.lq[:, 1:2]))
-    wait("v", kg, k_pt)
-    a = cmp(T.ba[:, 0:128], T.fs[:, 0:128], O, OP.is_ge)
-    pick_p = lambda: V(v.tensor_tensor(sel[P], me, him, OP.is_gt if odd else OP.is_lt))
-    if three:
-        b = cmp(T.ba[:, 128:256], mine, him, OP.is_gt if odd else OP.is_ge)
-        wait("v", k_sel)
-        c = cmp(T.ba[:, 256:512], T.fs[:, 0:256], ps[P], OP.is_ge if Q < P else OP.is_gt)
-        wait("v", b)
-        a = add_up(bu(0), T.ba, 0, 64, T.pt[:, 1:2])
-        wait("v", kb)
-        d = cmp(T.ba[:, 512:640], his, me, OP.is_ge if odd else OP.is_gt)
-        e = cmp(T.ba[:, 640:768], his, ps[Q], OP.is_ge if P < Q else OP.is_gt)
-        wait("v", c)
-        add_up(bu(2, 128), T.ba, 256, 128, 0.0)
-        wait("v", d)
-        add_up(bu(4), T.ba, 512, 64, T.pt[:, odd:odd + 1])
-        d = add_up(bu(1), T.ba, 128, 64, T.pt[:, 1 - odd:2 - odd])
-        wait("v", e)
-        e = add_up(bu(5), T.ba, 640, 64, 128.0 if P < Q else 0.0)
-        wait("v", kq2, a)
-        f = V(v.tensor_scalar(T.bu[:, 384:385], last(0), T.lq[:, 1:2], T.lq[:, 0:1], OP.min, OP.subtract if P < Q else OP.add))
-        wait("v", d)
-        V(v.tensor_scalar(T.pu2[:, P:P + 1], last(4), last(1), last(3), OP.min, OP.add))
-        wait("v", f, e)
-        kv = V(v.tensor_scalar(T.pu2[:, Q:Q + 1], last(5), T.bu[:, 384:385], None, OP.add))
-        pick_p()
-        V(v.tensor_copy(T.cf[:, 0:1], T.lst1[:, 0:1]))
-        wait("v", in_ids)
-        k_cf = V(v.tensor_copy(T.cf[:, 1:4], T.cu[:, 1:4]))
-        col = lambda r: T.cf[:, (rank ^ r):(rank ^ r) + 1]
-    else:
-        wait("v", kb, k_at)
-        d = cmp(T.ba[:, 512:640], his, me, OP.is_ge if odd else OP.is_gt)
-        e = cmp(T.ba[:, 640:768], his, ps[Q], OP.is_ge if P < Q else OP.is_gt)
-        k_sel = with_mate(kd)
-        b = cmp(T.ba[:, 128:256], mine, him, OP.is_gt if odd else OP.is_ge)
-        wait("v", e)
-        a = add_up(bu(0), T.ba, 0, 64, T.pt[:, 1:2])
-        wait("v", k_sel)
-        c = cmp(T.ba[:, 256:512], T.fs[:, 0:256], ps[P], OP.is_ge if Q < P else OP.is_gt)
-        add_up(bu(4), T.ba, 512, 64, T.pt[:, odd:odd + 1])
-        e = add_up(bu(5), T.ba, 640, 64, 128.0 if P < Q else 0.0)
-        wait("v", kq2, a)
-        f = V(v.tensor_scalar(T.bu[:, 384:385], last(0), T.lq[:, 1:2], T.lq[:, 0:1], OP.min, OP.subtract if P < Q else OP.add))
-        wait("v", c)
-        d = add_up(bu(2, 128), T.ba, 256, 128, 0.0)
-        d = add_up(bu(1), T.ba, 128, 64, T.pt[:, 1 - odd:2 - odd])
-        wait("v", f, e)
-        V(v.tensor_scalar(T.pu2[:, Q:Q + 1], last(5), T.bu[:, 384:385], None, OP.add))
-        k_cf = pick_p()
-        wait("v", d)
-        kv = V(v.tensor_scalar(T.pu2[:, P:P + 1], last(4), last(1), last(3), OP.min, OP.add))
-        col = lambda r: T.at[:, 16 + (rank ^ r):17 + (rank ^ r)] if r != rank else T.at[:, 0:1]
-
+    col = lambda r: T.cf[:, (rank ^ r):(rank ^ r) + 1] if r != rank else T.at[:, 0:1]
+    ps, sel = [[T[b][:, j:j + 1] for j in range(2)] for b in ("ps", "sel")]
+    me, him, E, O = at(rank), at(rank ^ 1), at(2 * Q), at(2 * Q + 1)
+    if two:
+        me, him, E, O = T.at[:, 1:2] if two == "early" else T.at[:, 24:25], T.at[:, 21:22], at(0), at(1)
     yw = (T.yw0, T.yw1)
-    for o in range(2):
-        wait("s", ko[o])
-        S(s.activation(yw[o][:, P:256:2], T.psf[:, 512 * (o + 2):512 * (o + 2) + 128], COPY))
-    wait("s", k_cf if three else in_ids)
+    spread = lambda h: s.activation(yx(h), T.msg[:, 0:16].indirect(T.eoff[:, 8 * h:8 * h + 8]), COPY)
+    sign = lambda o, src, c: s.activation(T.sq[:, o:o + 128], src, ACT.Sign, bias=c, scale=-1.0)
+    summed = lambda i, o, n, first: v.tensor_tensor_scan(T.bu[:, 64 * i:64 * i + n], T.ba[:, o:o + n], T.ba[:, o + n:o + 2 * n], first,
+                                                         OP.add, OP.add)
+    tok = {"n": a, "msg": in_msg, "eoff": k_eo, "a1": a1, "b1": b1, "in1c": in1c, "in1s": in1s, "ids": in_ids, "pt": k_pt, "sq0": k_sq0}
+    steps = {
+        "x": ("s", "msg eoff b1", lambda: s.activation(T.yx[:, 384:400], T.msg[:, 0:16].indirect(T.goff[:, 2:3]), COPY)),
+        "eE": ("s", "msg eoff", lambda: spread(0)), "eO": ("s", "msg eoff", lambda: spread(1)), "eM": ("s", "msg eoff", lambda: spread(2)),
+        "wE": ("v", "msg eoff", lambda: v.tensor_copy(yx(0), T.msg[:, 0:16].indirect(T.eoff[:, 0:8]))),
+        "wO": ("v", "msg eoff", lambda: v.tensor_copy(yx(1), T.msg[:, 0:16].indirect(T.eoff[:, 8:16]))),
+        "wM": ("v", "msg eoff", lambda: v.tensor_copy(yx(2), T.msg[:, 0:16].indirect(T.eoff[:, 16:24]))),
+        "V2": ("s", "", lambda: s.activation(T.vals2[:, 0:32], T.i4[:, 0:32], IDENT, bias=T.pcq[:, 0:1], scale=T.keep[:, 0:1])),
+        "tE": ("v", "eE", lambda: v.transpose(fs(0), yx(0))), "tO": ("v", "eO", lambda: v.transpose(fs(1), yx(1))),
+        "tM": ("v", "eM", lambda: v.transpose(fs(2), yx(2))),
+        "ps": ("v", "x", lambda: v.tensor_tensor(T.ps[:, 0:2], T.yx[:, 384:388:2], T.yx[:, 385:388:2], OP.max)),
+        "se": ("v", "x", lambda: v.tensor_tensor(T.sel[:, 0:2], T.yx[:, 385:388:2], T.yx[:, 384:388:2], OP.is_gt)),
+        "n5": ("v", "n", lambda: v.tensor_scalar(T.yl[:, 0:1], T.kq[:, 2:3], n_wins, 255.0, OP.add, OP.min)),
+        "n6": ("v", "n5", lambda: v.tensor_scalar(T.off2[:, 0:16], T.tab[:, 0:256].indirect(T.yl[:, 0:1]), n_wins, 0.0 if odd else float(K),
+                                                  OP.add if odd else OP.subtract, OP.add)),
+        "a": ("v", "tE x", lambda: v.tensor_scalar(ba(0), fs(0), O, None, OP.is_ge)),
+        "b": ("v", "x", lambda: v.tensor_scalar(ba(1), mine, him, None, OP.is_gt if odd else OP.is_ge)),
+        "c": ("v", "tE tO ps", lambda: v.tensor_scalar(ba(2, 2), fs(0, 2), ps[P], None, OP.is_ge if Q < P else OP.is_gt)),
+        "d": ("v", "tM x", lambda: v.tensor_scalar(ba(4), fs(2), me, None, OP.is_ge if odd else OP.is_gt)),
+        "mH": ("t", "in1c in1s a1 b1", lambda: t.matmul_mx(T.psf[:, 0:128], T.uq[:, 0:128], T.us[:, 0:128], T.c1[:, K:2 * K], T.s1[:, K:2 * K], True, True)),
+        "mI": ("t", "in1c in1s a1 b1", lambda: t.matmul_mx(T.psp[:, 0:128], T.uq[:, 0:128], T.us[:, 0:128], T.c1[:, K:2 * K], T.s1[:, K:2 * K], True, True)),
+        "d'": ("v", "mH x", lambda: v.tensor_scalar(ba(4), T.psf[:, 0:128], me, None, OP.is_ge if odd else OP.is_gt)),
+        "g2'": ("s", "mI ps", lambda: sign(272, T.psp[:, 0:128], ps[Q])),
+        "A": ("v", "a pt", lambda: summed(0, 0, 64, T.pt[:, 2:3])),
+        "B": ("v", "b pt", lambda: v.tensor_tensor_scan(T.bt[:, 0:64], T.ba[:, 128:192], T.ba[:, 192:256], T.pt[:, 1 - odd:2 - odd], OP.add, OP.add)),
+        "C": ("v", "c", lambda: v.tensor_tensor_scan(T.bt[:, 64:192], T.ba[:, 256:384], T.ba[:, 384:512], 0.0, OP.add, OP.add)),
+        "D": ("v", "d pt", lambda: summed(4, 512, 64, T.pt[:, odd:odd + 1])),
+        "g1": ("s", "ps", lambda: sign(144, mine, ps[Q])), "g2": ("s", "ps tM", lambda: sign(272, fs(2), ps[Q])),
+        "gA": ("s", "x tO", lambda: sign(0, fs(1), E)),
+        "rA": ("s", "gA sq0", lambda: s.activation(T.junk[:, 0:130], T.sq[:, 0:130], ACT.Relu, scale=-1.0, accum_out=T.lq[:, 1:2])),
+        "rC": ("s", "g1 g2", lambda: s.activation(T.junk[:, 144:400], T.sq[:, 144:400], ACT.Relu, scale=1.0 if P < Q else -1.0,
+                                                  accum_out=T.lq[:, 0:1])),
+        "uP": ("v", "B C D", lambda: v.tensor_scalar(T.pu2[:, P:P + 1], last(4), T.bt[:, 63:64], T.bt[:, 191:192], OP.min, OP.add)),
+        "uQ": ("v", "A rA rC", lambda: v.tensor_scalar(T.pu2[:, Q:Q + 1], last(0), T.lq[:, 1:2], T.lq[:, 0:1], OP.min,
+                                                       OP.subtract if P < Q else OP.add)),
+        "cf": ("v", "ids", lambda: v.tensor_copy(T.cf[:, 1:4], T.cu[:, 1:4])),
+    }
     for j in range(2):
-        k = S(s.activation(T.vd[:, j:j + 1], col(2 * j), IDENT, bias=col(2 * j + 1), scale=-1.0))
-    wait("s", k_cf)
-    for j in range(2):
-        S(s.activation(T.cp[:, 32 * j:32 * j + 1], sel[j], IDENT, bias=2.0 * j))
-    wait("s", k)
-    for j in range(2):
-        kcp = S(s.activation(T.cp[:, 32 * j + 1:32 * j + 2], T.vd[:, j:j + 1], IDENT, bias=col(2 * j), scale=sel[j]))
+        steps["y%d" % j] = ("s", "m%d" % j, lambda o=j: s.activation(yw[o][:, P:256:2], T.psf[:, 512 * (o + 2):512 * (o + 2) + 128], COPY))
+        steps["v%d" % j] = ("s", "cf", lambda j=j: s.activation(T.vd[:, j:j + 1], col(2 * j), IDENT, bias=col(2 * j + 1), scale=-1.0))
+        steps["r%d" % j] = ("s", "se", lambda j=j: s.activation(T.cp[:, 32 * j:32 * j + 1], sel[j], IDENT, bias=2.0 * j))
+        steps["k%d" % j] = ("s", "se v%d" % j, lambda j=j: s.activation(T.cp[:, 32 * j + 1:32 * j + 2], T.vd[:, j:j + 1], IDENT,
+                                                                      bias=col(2 * j), scale=sel[j]))
+    if two:
+        mark = T.cp[:, 32 * P:32 * P + 2]
+        steps.update({
+            "pQ": ("v", "x", lambda: v.tensor_tensor(ps[Q], E, O, OP.max)),
+            "ps": ("v", "ids b1", lambda: v.tensor_tensor(ps[P], me, him, OP.max)),
+            "se": ("v", "ids b1", lambda: v.tensor_tensor(sel[0], him, me, OP.is_ge if odd else OP.is_gt)),
+            "v0": ("s", "ids", lambda: s.activation(T.vd[:, 0:1], T.at[:, 0:1], IDENT, bias=T.at[:, 20:21], scale=-1.0)),
+            "r0": ("s", "se", lambda: s.activation(T.cp[:, 32 * P:32 * P + 1], sel[0], IDENT, bias=float(rank), scale=-1.0 if odd else 1.0)),
+            "k0": ("s", "se v0", lambda: s.activation(T.cp[:, 32 * P + 1:32 * P + 2], T.vd[:, 0:1], IDENT, bias=T.at[:, 0:1], scale=sel[0])),
+            "b": ("v", "ids b1", steps["b"][2]), "g1": ("s", "pQ", steps["g1"][2]), "g2'": ("s", "mI pQ", steps["g2'"][2]),
+        })
+    if two == "v4":
+        him = T.psp[:, 0:1]
+        col = lambda r: T.at[:, 16 + (rank ^ r):17 + (rank ^ r)] if r != rank else T.at[:, 0:1]
+        steps.update({
+            "mD": ("t", "in1c in1s a1 b1", lambda: t.matmul_mx(T.psp[:, 0:128], T.c1[:, K:2 * K], T.s1[:, K:2 * K], T.uq0[:, 2:130], T.us0[:, 2:130], True, True)),
+            "ps": ("v", "mD", steps["ps"][2]), "b": ("v", "mD", steps["b"][2]),
+            "sQ": ("v", "x", lambda: v.tensor_tensor(sel[Q], O, E, OP.is_gt)),
+            "se": ("v", "mD", lambda: v.tensor_tensor(sel[P], me, him, OP.is_gt if odd else OP.is_lt)),
+            "E1": ("v", "mH pQ", lambda: v.tensor_scalar(ba(5), T.psf[:, 0:128], ps[Q], None, OP.is_ge if P < Q else OP.is_gt)),
+            "E2": ("v", "E1", lambda: summed(5, 640, 64, -128.0 if P < Q else 0.0)),
+            "rC": ("s", "g1", lambda: s.activation(T.junk[:, 144:272], T.sq[:, 144:272], ACT.Relu, scale=1.0 if P < Q else -1.0, accum_out=T.lq[:, 0:1])),
+            "f": ("v", "A rA rC", lambda: v.tensor_scalar(T.bu[:, 384:385], last(0), T.lq[:, 1:2], T.lq[:, 0:1], OP.min, OP.subtract if P < Q else OP.add)),
+            "uQ": ("v", "f E2", lambda: v.tensor_scalar(T.pu2[:, Q:Q + 1], last(5), T.bu[:, 384:385], None, OP.add)),
+        })
+        if OPT.get("mi"):
+            steps["mI"] = ("t", "in1c in1s a1 b1", lambda: t.matmul_mx(T.psp[:, 512:640], T.uq[:, 0:128], T.us[:, 0:128], T.c1[:, K:2 * K], T.s1[:, K:2 * K], True, True))
+            steps["g2'"] = ("s", "mI pQ", lambda: sign(272, T.psp[:, 512:640], ps[Q]))
+            steps["rC"] = ("s", "g1 g2", lambda: s.activation(T.junk[:, 144:400], T.sq[:, 144:400], ACT.Relu, scale=1.0 if P < Q else -1.0, accum_out=T.lq[:, 0:1]))
+            steps["uQ"] = ("v", "A rA rC", lambda: v.tensor_scalar(T.pu2[:, Q:Q + 1], last(0), T.lq[:, 1:2], T.lq[:, 0:1], OP.min, OP.subtract if P < Q else OP.add))
+        if OPT.get("rsplit"):
+            way, less = (1.0, OP.subtract) if P < Q else (-1.0, OP.add)
+            steps["rB"] = ("s", "g1", lambda: s.activation(T.junk[:, 144:272], T.sq[:, 144:272], ACT.Relu, scale=way, accum_out=T.lq[:, 0:1]))
+            steps["rC"] = ("s", "g2", lambda: s.activation(T.junk[:, 272:400], T.sq[:, 272:400], ACT.Relu, scale=way, accum_out=T.lq[:, 2:3]))
+            steps["f"] = ("v", "A rA rB", lambda: v.tensor_scalar(T.bu[:, 384:385], last(0), T.lq[:, 1:2], T.lq[:, 0:1], OP.min, less))
+            steps["uQ"] = ("v", "f rC", lambda: v.tensor_scalar(T.pu2[:, Q:Q + 1], T.bu[:, 384:385], T.lq[:, 2:3], None, less))
+        for j in range(2):
+            steps["v%d" % j] = ("s", "ids", lambda j=j: s.activation(T.vd[:, j:j + 1], col(2 * j), IDENT, bias=col(2 * j + 1), scale=-1.0))
+            steps["r%d" % j] = ("s", "se", lambda j=j: s.activation(T.cp[:, 32 * j:32 * j + 1], sel[j], IDENT, bias=2.0 * j))
+            steps["k%d" % j] = ("s", "se v%d" % j, lambda j=j: s.activation(T.cp[:, 32 * j + 1:32 * j + 2], T.vd[:, j:j + 1], IDENT, bias=col(2 * j), scale=sel[j]))
+        in_cp = in_ids
+        if OPT.get("pair"):
+            steps.update({
+                "se": ("v", "mD", lambda: v.tensor_tensor(sel[0], me, him, OP.is_le if odd else OP.is_lt)),
+                "v0": ("s", "ids", lambda: s.activation(T.vd[:, 0:1], T.at[:, 0:1], IDENT, bias=T.at[:, 20:21], scale=-1.0)),
+                "r0": ("s", "se", lambda: s.activation(T.cp[:, 32 * P:32 * P + 1], sel[0], IDENT, bias=float(rank), scale=-1.0 if odd else 1.0)),
+                "k0": ("s", "se v0", lambda: s.activation(T.cp[:, 32 * P + 1:32 * P + 2], T.vd[:, 0:1], IDENT, bias=T.at[:, 0:1], scale=sel[0])),
+            })
+    for name in OPT["second"].split():
+        if name == "sc":
+            in_cp = remote(mark, mark, T.cores[rank ^ 2], "hj", tok["r0"], tok["k0"])
+        elif name == "pc" and OPT.get("halves"):
+            for h, (ar, sem) in enumerate(((in1a, "h2d"), (in1c, "h2c"))):
+                e = slice(K * P + 64 * h, K * P + 64 * h + 64)
+                tok[name] = pick_codes(T.c2[:, e], T.c1[:, 0:256], T.off2[:, 4 * h:4 * h + 4], tok["n6"], ar)
+                in2c = remote(T.c2[:, e], T.c2[:, e], T.cores[rank ^ 2], sem, tok[name])
+                extra.append(in2c)
+        elif name == "pc":
+            tok[name] = pick_codes(T.c2[:, own], T.c1[:, 0:256], T.off2[:, 0:8], tok["n6"], in1c)
+            in2c = remote(T.c2[:, own], T.c2[:, own], T.cores[rank ^ 2], "h2c", tok[name])
+        elif name == "pz":
+            tok[name] = pick_scales(T.s2[:, own], T.s1[:, 0:256], T.off2[:, 0:8], tok["n6"], in1s)
+            in2s = remote(T.s2[:, own], T.s2[:, own], T.cores[rank ^ 2], "h2s", tok[name])
+            tok["m0"], tok["m1"] = products(own, T.psf, tok["pc"], tok["pz"])
+            kn = products(arr, T.psp, in2c, in2s)
+        else:
+            q, ready, make = steps[name]
+            wait(q, *[tok[r] for r in ready.split()])
+            tok[name.replace("w", "e").replace("'", "")] = done(make(), q)
+    kv, kcp = max(tok["uP"], tok["uQ"]), max(tok[r] for r in ("k0", "k1", "r0", "r1") if r in tok)
     kz = []
 
     def numbers(i):
-        if i == 2:
-            wait("v", kcp)
-            for j in range(2):
-                kz.append(V(v.transpose(T.idr[:, j:64:2], T.cp[:, 32 * j:32 * j + 32])))
-        elif i > 2:
-            wait("v", kz[1])
-            kz.append(V(v.tensor_copy(T.idr[0:2, 64 * i - 128:64 * i - 64], T.idr[32 * i - 64:32 * i - 62, 0:64])))
-    k_q2, k_l2 = invert("2", (kv,), 2, T.vals2, 16, 128.0, numbers)
-    for o in range(2):
-        wait("s", kn[o])
-        kyw = S(s.activation(yw[o][:, Q:256:2], T.psp[:, 512 * (o + 2):512 * (o + 2) + 128], COPY))
-
+        for h in OPT["numbers"].get(i, ()):
+            if h == 9:
+                wait("v", kn[0])
+                tok["a0"] = V(v.tensor_copy(T.yw0[:, Q:256:2], T.psp[:, 1024:1152]))
+            elif h == 0:
+                wait("v", kcp, *([in_cp] if two else []))
+                for j in range(2):
+                    kz.append(V(v.transpose(T.idr[:, j:64:2], T.cp[:, 32 * j:32 * j + 32])))
+            else:
+                wait("v", kz[1])
+                kz.append(V(v.tensor_copy(T.idr[0:2, 64 * h:64 * h + 64], T.idr[32 * h:32 * h + 2, 0:64])))
+    k_q2, k_l2 = invert("2", (kv,), 2, T.vals2, 16, 0.0, numbers)
     off = T.lst2[:, 2:10]
-    wait("v", k_l2, kyw)
-    ky0 = V(v.tensor_copy(T.yb[:, 0:128], T.yw0[:, 0:256].indirect(off)))
-    wait("v", *kz)
-    ki = V(v.tensor_scalar(T.idb[:, 0:128], T.idr[:, 0:256].indirect(off), T.pt[:, 2:3], None, OP.add))
-    wait("s", k_l2, kyw)
-    ky1 = S(s.activation(T.yb[:, 128:256], T.yw1[:, 0:256].indirect(off), COPY))
-    wait("y", ky0, ky1)
-    d0 = done(y.dma_start(T.y[:, 0:256], T.yb[:, 0:256]), "dy", 16)
+    if OPT["tail"] == 3:
+        kyw, ky = [], []
+        for o in range(2):
+            wait("v", kn[o])
+            kyw.append(V(v.tensor_copy(yw[o][:, Q:256:2], T.psp[:, 512 * (o + 2):512 * (o + 2) + 128])))
+        for o in range(2):
+            wait("s", k_l2, kyw[o], tok["y%d" % o])
+            a = S(s.activation(T.yb[:, K * o:K * o + 64], yw[o][:, 0:256].indirect(T.lst2[:, 2:6]), COPY))
+            wait("v", k_l2, kyw[o], tok["y%d" % o])
+            ky.append((a, V(v.tensor_copy(T.yb[:, K * o + 64:K * o + K], yw[o][:, 0:256].indirect(T.lst2[:, 6:10])))))
+        wait("v", *kz)
+        ki = V(v.tensor_copy(T.idb[:, 0:128], T.idr[:, 0:256].indirect(off)))
+        ky0, ky1 = ky
+    elif OPT["tail"] == 0:
+        kyw = []
+        for o in range(2):
+            wait("s", kn[o])
+            kyw.append(S(s.activation(yw[o][:, Q:256:2], T.psp[:, 512 * (o + 2):512 * (o + 2) + 128], COPY)))
+        if OPT.get("pair"):
+            wait("s", kz[1])
+            kz.append(S(s.activation(T.idr[0:2, 192:256], T.idr[96:98, 0:64], COPY)))
+        wait("v", k_l2, kyw[0])
+        ky0 = V(v.tensor_copy(T.yb[:, 0:128], T.yw0[:, 0:256].indirect(off)))
+        wait("v", *kz)
+        ki = V(v.tensor_copy(T.idb[:, 0:128], T.idr[:, 0:256].indirect(off)))
+        wait("s", k_l2, kyw[1])
+        ky1 = S(s.activation(T.yb[:, 128:256], T.yw1[:, 0:256].indirect(off), COPY))
+    else:
+        if OPT["tail"] == 1:
+            wait("s", kn[0])
+            a = S(s.activation(T.yw0[:, Q:256:2], T.psp[:, 1024:1152], COPY))
+        else:
+            a = tok["a0"]
+        wait("v", kn[1])
+        b = V(v.tensor_copy(T.yw1[:, Q:256:2], T.psp[:, 1536:1664]))
+        wait("s", k_l2, a)
+        ky0 = S(s.activation(T.yb[:, 0:128], T.yw0[:, 0:256].indirect(off), COPY))
+        wait("v", k_l2, b, tok["y1"])
+        ky1 = V(v.tensor_copy(T.yb[:, 128:256], T.yw1[:, 0:256].indirect(off)))
+        wait("s", *kz)
+        ki = S(s.activation(T.idb[:, 0:128], T.idr[:, 0:256].indirect(off), COPY))
+    if OPT["split"]:
+        for o, k in enumerate((ky0, ky1)):
+            wait("y", *(k if OPT["tail"] == 3 else (k,)))
+            d0 = done(y.dma_start(T.y[:, K * o:K * o + K], T.yb[:, K * o:K * o + K]), "dy", 16)
+    else:
+        wait("y", ky0, ky1)
+        d0 = done(y.dma_start(T.y[:, 0:256], T.yb[:, 0:256]), "dy", 16)
     wait("s", ki)
     d2 = done(s.dma_start(T["id"][0:2, 0:128], T.idb[0:2, 0:128]), "did", 16)
-    wait("g", ("sent", count["sent"]), in1c, in1s, in2c, in2s, in_msg, *in_raw, in_places, in_ids, du, *dx.values(), dw,
+    wait("g", ("sent", count["sent"]), in1c, in1s, in2c, in2s, *extra, in_msg, *in_raw, in_places, in_ids, *([in_cp] if two else []), du, *dx.values(), dw,
          ("gc", count["gc"]), ("v", count["v"]), ("s", count["s"]), ("t", count["t"]), d0, d2)

from concourse.bass import DstId, RemoteDMATransfer
from concourse.mybir import dt, AluOpType, ActivationFunctionType

OP = AluOpType
ACT = ActivationFunctionType
COPY, IDENT = ACT.Copy, ACT.Identity
K = 128
BIG = 1e29
STEP = 1.25 * 2.0 ** -24
TINY = 2.0 ** -122
SLOT = 4

OPT = {"q0": True, "loads": [[0], [1], [2], [3]], "banks": [[0], [1], [2, 3]], "split": True, "valm": False, "apart": 0, "folds": [[0, 1, 2, 3], []], "tail": 3, "numbers": {1: [0], 3: [1], 4: [2, 3]}, "pair": 0, "two": "v4", "mi": 1,
       "second": "V2 x eO eE n5 pQ n6 tO pc g1 gA mD mI mH pz rA g2' rC sQ tE ps b a c d' B C A D se uQ uP v0 v1 r0 r1 k0 k1 y0 y1",
       "scal": [(2, 0), (3, 0), (3, 1)],
       "order": "d0 s0 v0 r0 q1 z0 r1 d1 b0 s1 z3 v1 q2 z2 r2 d2 q3 z1 b1 d3 s2 r3 c01 c00 c02 c10 c12 c11 c21 g20 b2 g30 b3 g31 l2 l3 v2 v3 "
                "c03 c13 c23 c32 t0 c22 t1 c33 p02 t2 t3 x01 p2 p3 x00 x21 x20"}

SCRATCH = {
    "ur": ("sbuf", [128, 520], "bfloat16"), "zoff": ("sbuf", [128, 8], "uint16"),
    "uq0": ("sbuf", [128, 130], "float8_e4m3fn_x4"), "us0": ("sbuf", [128, 130], "uint8"),
    "uq": ("sbuf", [128, 128], "float8_e4m3fn_x4"), "us": ("sbuf", [128, 128], "uint8"),
    "xb": ("sbuf", [128, 2048], "bfloat16"),
    "xq": ("sbuf", [128, 512], "float8_e4m3fn_x4"), "xs": ("sbuf", [128, 512], "uint8"),
    "wb": ("sbuf", [128, 1024], "bfloat16"),
    "wq": ("sbuf", [128, 256], "float8_e4m3fn_x4"), "ws": ("sbuf", [128, 256], "uint8"),
    "c1": ("sbuf", [128, 256], "float8_e4m3fn_x4"), "s1": ("sbuf", [128, 256], "uint8"),
    "c2": ("sbuf", [128, 256], "float8_e4m3fn_x4"), "s2": ("sbuf", [128, 256], "uint8"),
    "yw0": ("sbuf", [128, 256], "float32"), "yw1": ("sbuf", [128, 256], "float32"),
    "yb": ("sbuf", [128, 256], "float32"),
    "psf": ("psum", [128, 2048], "float32"),
    "psp": ("psum", [128, 2048], "float32"),
    "ip": ("sbuf", [128, 2], "int32"), "pt": ("sbuf", [128, 8], "float32"),
    "it": ("sbuf", [128, 128], "int32"), "ita": ("sbuf", [128, 64], "int32"), "tri": ("sbuf", [128, 128], "float32"),
    "nb": ("sbuf", [128, 64], "float32"), "dg": ("sbuf", [128, 16], "float32"), "seg": ("sbuf", [128, 128], "float32"),
    "i3": ("sbuf", [128, 64], "float32"), "vals1": ("sbuf", [128, 64], "float32"),
    "i4": ("sbuf", [128, 32], "float32"), "vals2": ("sbuf", [128, 32], "bfloat16"),
    "i5": ("sbuf", [128, 28], "int32"), "eoff": ("sbuf", [128, 28], "uint16"),
    "iy": ("sbuf", [128, 256], "bfloat16"), "one": ("sbuf", [128, 256], "bfloat16"), "jump": ("sbuf", [128, 256], "bfloat16"),
    "tab": ("sbuf", [128, 256], "bfloat16"), "kq": ("sbuf", [128, 3], "float32"), "yl": ("sbuf", [128, 2], "uint16"),
    "gr": ("sbuf", [128, 96], "float32"), "gt": ("sbuf", [128, 96], "float32"), "goff": ("sbuf", [128, 6], "uint16"),
    "keep": ("sbuf", [128, 1], "float32"), "bg": ("sbuf", [128, 3], "float32"),
    "pca": ("sbuf", [128, 2], "int32"), "pcf": ("sbuf", [128, 2], "float32"), "pcq": ("sbuf", [128, 3], "float32"),
    "sp": ("sbuf", [128, 4], "float32"), "dl": ("sbuf", [128, 4], "float32"), "thr": ("sbuf", [128, 512], "float32"),
    "cm": ("sbuf", [128, 2048], "bfloat16"), "cs": ("sbuf", [128, 1024], "bfloat16"),
    "sg": ("sbuf", [128, 1152], "bfloat16"), "junk": ("sbuf", [128, 1152], "bfloat16"), "ls": ("sbuf", [128, 4], "float32"),
    "raw": ("sbuf", [128, 512], "float32"), "valo": ("sbuf", [128, 64], "float32"),
    "wins": ("sbuf", [128, 528], "float32"), "tzs": ("sbuf", [128, 128], "float32"),
    "msg": ("sbuf", [128, 16], "float32"), "cu": ("sbuf", [128, 4], "uint16"), "cf": ("sbuf", [128, 4], "float32"), "at": ("sbuf", [128, 40], "float32"),
    "spm": ("sbuf", [128, 4], "float32"), "pum": ("sbuf", [128, 8], "uint16"), "valm": ("sbuf", [128, 64], "float32"),
    "osr": ("sbuf", [128, 528], "float32"), "cb": ("sbuf", [128, 96], "bfloat16"), "cr": ("sbuf", [64, 96], "bfloat16"),
    "ct": ("sbuf", [64, 32], "bfloat16"), "cn": ("sbuf", [128, 32], "float32"), "off2": ("sbuf", [128, 16], "uint16"),
    "yx": ("sbuf", [128, 400], "float32"), "fs": ("sbuf", [128, 384], "float32"),
    "ps": ("sbuf", [128, 2], "float32"), "sel": ("sbuf", [128, 2], "float32"), "vd": ("sbuf", [128, 2], "float32"),
    "ba": ("sbuf", [128, 768], "bfloat16"), "bu": ("sbuf", [128, 400], "float32"), "bt": ("sbuf", [128, 192], "bfloat16"),
    "sq": ("sbuf", [128, 528], "bfloat16"), "lq": ("sbuf", [128, 3], "float32"),
    "cp": ("sbuf", [128, 64], "float32"), "idr": ("sbuf", [128, 256], "float32"), "idb": ("sbuf", [128, 128], "float32"),
}
for _n in ("1", "2"):
    SCRATCH["pu" + _n] = ("sbuf", [128, 4], "uint16")
    SCRATCH["win" + _n] = ("sbuf", [128, 528], "float32" if _n == "1" else "bfloat16")
    SCRATCH["tz" + _n] = ("sbuf", [128, 288], "float32" if _n == "1" else "bfloat16")
    SCRATCH["qa" + _n] = ("sbuf", [64, 432], "float32")
    SCRATCH["qc" + _n] = ("sbuf", [128, 24], "float32")
    SCRATCH["lst" + _n] = ("sbuf", [128, 16], "uint16")

SEMAPHORES = ["v", "s", "t", "gc", "du", "dx0", "dx1", "dx2", "dx3", "dw", "dy", "did",
              "h1c", "h1s", "h2c", "h2s", "hm", "hr", "hq", "hp", "hi", "hj", "sent"]


def rank_program(g, core, T, topo):
    rank = T.rank_of(core)
    if rank is None:
        return
    v, s, t, y = g.vector, g.scalar, g.tensor, g.sync
    queue = {"g": g, "v": v, "s": s, "t": t, "y": y}
    count, waited = {}, {}
    odd, P, Q = rank % 2, rank // 2, (rank // 2) ^ 1
    own, arr = slice(K * P, K * P + K), slice(K * Q, K * Q + K)

    def done(ins, sem, n=1):
        ins.then_inc(T.sem[sem], n)
        count[sem] = count.get(sem, 0) + n
        return (sem, count[sem])

    def wait(q, *tokens):
        best = {}
        for sem, n in tokens:
            best[sem] = max(best.get(sem, 0), n)
        for sem, n in best.items():
            if waited.get((q, sem), 0) < n:
                waited[(q, sem)] = n
                queue[q].wait_ge(T.sem[sem], n)

    def V(ins): return done(ins, "v")
    def S(ins): return done(ins, "s")
    def X(ins): return done(ins, "t")
    def G(ins): return done(ins, "gc")

    B = [0, 1, 2, 3] if odd else [3, 2, 1, 0]
    du = done(s.dma_start(T.ur[:, 8:16], T.u[:, 0:8]), "du", 16)
    dx = {}
    for grp in OPT["loads"]:
        a, b = 512 * min(B[i] for i in grp), 512 * max(B[i] for i in grp) + 512
        k = done(y.dma_start(T.xb[:, a:b], T.x[:, a:b]), "dx%d" % grp[0], 16)
        dx.update({B[i]: k for i in grp})
    wait("y", dx[B[3]])
    dw = done(y.dma_start(T.wb[:, 0:1024], T.w[:, 0:1024]), "dw", 16)

    def iota(buf, pattern, base, cm, flt=True):
        if flt:
            return G(g.iota(buf, pattern, base, cm, allow_small_or_imprecise_dtypes=True))
        return G(g.iota(buf, pattern, base, cm))
    k_it = iota(T.it[:, 0:128], [[1, 128]], 128, -1, False)
    k_ip = iota(T.ip[:, 0:2], [[0, 2]], 0, 1, False)
    sign1, best = (1.0, OP.max) if odd else (-1.0, OP.min)
    kb = iota(T.bg[:, 2:3], [[0, 1]], 0, 0)
    k = iota(T.gr[:, 0:32], [[0, 32]], 0, 1)
    iota(T.gr[:, 32:64], [[0, 16], [32 * SLOT, 2]], 64 * SLOT * Q, 1)
    wait("g", kb)
    kb = G(g.affine_select(T.bg[:, 1:2], T.bg[:, 2:3], [[0, 1]], OP.not_equal, -BIG * sign1, -88, 1))
    wait("g", k)
    iota(T.gr[:, 2:10], [[32, 4], [160, 2]], 0, 0)
    iota(T.gr[:, 18:26], [[32, 4], [-128, 2]], 128, 0)
    wait("g", kb)
    k_bg = G(g.affine_select(T.bg[:, 0:1], T.bg[:, 1:2], [[0, 1]], OP.not_equal, -BIG * sign1, -120, 1))
    k_gr = iota(T.gr[:, 64:96], [[0, 32]], 128, 1)
    k_i3 = iota(T.i3[:, 0:64], [[128, 4], [1, 16]], 0, 0)
    k_i4 = iota(T.i4[:, 0:32], [[1, 2], [2, 16]], 0, 0)
    lo1, lom = (384, 16) if odd else (16, 384)

    V(v.memset(T.ur[:, 0:8], 0.0))
    k_ur = V(v.memset(T.ur[:, 16:520], 0.0))
    k_zo = V(v.memset(T.zoff[:, 0:8], 2))
    V(v.memset(T.one[:, 0:256], -sign1))
    wait("s", k_ur)
    for a, b in ((0, lom), (lom + K, 528)):
        S(s.activation(T.osr[:, a:b], T.ur[:, 16:16 + b - a], IDENT, bias=BIG))
    S(s.activation(T.wins[:, lo1:lo1 + K], T.ur[:, 16:16 + K], IDENT, bias=-BIG * sign1))
    S(s.activation(T.idr[:, 64:256], T.ur[:, 16:208], COPY))
    wait("v", k_it)
    if odd:
        k_tri = V(v.tensor_scalar(T.tri[:, 0:128], T.it[:, 0:128], 128.0, None, OP.is_gt))
    else:
        k_tri = V(v.tensor_scalar(T.tri[:, 0:128], T.it[:, 0:128], 128.0, -1.0, OP.is_lt, OP.mult))
    V(v.tensor_scalar(T.ita[:, 0:64], T.it[:, 0:64], 15, None, OP.bitwise_and))
    wait("v", k_ip)
    V(v.tensor_scalar(T.pca[:, 0:1], T.ip[:, 0:1], 112, None, OP.bitwise_and))
    k = V(v.tensor_scalar(T.pca[:, 1:2], T.ip[:, 0:1], 15, None, OP.bitwise_and))
    V(v.memset(T.cb[:, 64:96], 0.0))
    V(v.memset(T.cp[:, 0:64], 0.0))
    wait("v", k)
    V(v.tensor_scalar(T.keep[:, 0:1], T.pca[:, 1:2], 8.0, sign1, OP.not_equal, OP.mult))
    k_pc = V(v.tensor_copy(T.pcf[:, 0:2], T.pca[:, 0:2]))
    k_nb = V(v.tensor_scalar(T.nb[:, 0:64], T.ita[:, 0:64], 0.0, -BIG, OP.not_equal, OP.mult))
    wait("s", k_pc)
    S(s.activation(T.pcq[:, 1:2], T.pcf[:, 0:1], COPY, scale=2.0))

    wait("v", du, k_ur)
    k_u0 = V(v.quantize_mx(T.uq0[:, 0:130], T.us0[:, 0:130], T.ur[:, 0:520]))
    kq = {}

    def quant(i):
        d = B[i]
        wait("v", dx[d])
        kq[d] = V(v.quantize_mx(T.xq[:, 128 * d:128 * d + 128], T.xs[:, 128 * d:128 * d + 128], T.xb[:, 512 * d:512 * d + 512]))
    if OPT["q0"]:
        quant(0)
    wait("v", k_u0, k_zo)
    k_uc = V(v.tensor_copy(T.uq[:, 0:128].bitcast(dt.uint32), T.uq0[:, 0:130].bitcast(dt.uint32).indirect(T.zoff[:, 0:8])))
    if not OPT["q0"]:
        quant(0)
    wait("s", k_u0, k_zo)
    k_us = S(s.activation(T.us[:, 0:128], T.us0[:, 0:130].indirect(T.zoff[:, 0:8]), COPY))
    wait("s", k_bg)
    k_b1 = S(s.activation(T.pcq[:, 2:3], T.pcf[:, 0:1], IDENT, bias=T.bg[:, 0:1], scale=T.keep[:, 0:1]))

    kr, kp, kt, kl, kc, ks = {}, {}, {}, {}, {}, {}
    strict, loose = (OP.is_lt, OP.is_le) if odd else (OP.is_gt, OP.is_ge)
    row = [T.psf[:, 512 * d:512 * d + 128] for d in range(4)]
    sp = [T.sp[:, c:c + 1] for c in range(4)]
    cm = T.cm

    def rows(i):
        e = slice(128 * B[i], 128 * B[i] + 128)
        wait("t", k_uc, k_us, kq[B[i]])
        kr[i] = X(t.matmul_mx(row[B[i]], T.uq[:, 0:128], T.us[:, 0:128], T.xq[:, e], T.xs[:, e], True, True))

    def down(i):
        grp = [h for h in OPT["banks"] if i in h][0]
        c, bank = B[i], 512 * OPT["banks"].index(grp)
        at = 2 * (c - min(B[h] for h in grp))
        e, m = slice(128 * c, 128 * c + 128), slice(2 - at, 130 - at)
        wait("t", k_u0, kq[c])
        kd[i] = X(t.matmul_mx(T.psp[:, bank:bank + 128], T.xq[:, e], T.xs[:, e], T.uq0[:, m], T.us0[:, m], i == grp[0], i == grp[-1]))

    def scores(i):
        grp = [h for h in OPT["banks"] if i in h][0]
        c, n, bank = min(B[h] for h in grp), len(grp), 512 * OPT["banks"].index(grp)
        src = T.psp[:, bank:bank + 2 * n:2]
        wait("s", *[kd[h] for h in grp])
        a = S(s.activation(T.sp[:, c:c + n], src, COPY))
        b = S(s.activation(T.dl[:, c:c + n], src, ACT.Abs, bias=TINY, scale=STEP))
        for h in grp:
            kp[h], kd["s", h] = a, b

    def bound(i, k):
        c = B[i]
        wait("s", k, k_tri)
        kt[i] = S(s.activation(T.thr[:, 128 * c:128 * c + 128], T.tri[:, 0:128], IDENT, bias=sp[c], scale=T.dl[:, c:c + 1]))

    def cmp(out, src, col, op):
        return V(v.tensor_scalar(out, src, col, None, op))

    SCAL = OPT["scal"]
    mine_v = {i: [j for j in range(4) if (i, j) not in SCAL] for i in range(4)}
    mine_s = {i: [j for j in range(4) if (i, j) in SCAL] for i in range(4)}

    def cell(i, j):
        c, d, o = B[i], B[j], 512 * i + 128 * mine_v[i].index(j)
        wait("v", *[k for (h, e), k in ks.items() if e == j])
        if i == j:
            wait("v", kr[j], kt[i])
            kc[i, j] = V(v.tensor_tensor(cm[:, o:o + 128], row[d], T.thr[:, 128 * c:128 * c + 128], strict))
        else:
            wait("v", kr[j], kp[i])
            kc[i, j] = cmp(cm[:, o:o + 128], row[d], sp[c], loose if i < j else strict)

    def add_up(out, buf, o, n, first):
        return V(v.tensor_tensor_scan(out, buf[:, o:o + n], buf[:, o + n:o + 2 * n], first, OP.add, OP.add))

    def signs(i, j):
        o = 384 * (i - 1) + 128 * mine_s[i].index(j)
        wait("s", kp[i], kr[j], *[k for (h, e), k in kc.items() if e == j])
        ks[i, j] = S(s.activation(T.sg[:, o:o + 128], row[B[j]], ACT.Sign, bias=sp[B[i]], scale=-1.0))

    def sum_signs(i):
        o, n = 384 * (i - 1), 128 * len(mine_s[i])
        wait("s", *[ks[i, j] for j in mine_s[i]])
        kl[i] = S(s.activation(T.junk[:, o:o + n], T.sg[:, o:o + n], ACT.Relu, scale=1.0 if odd else -1.0, accum_out=T.ls[:, i:i + 1]))

    def total(i):
        n, e = 64 * len(mine_v[i]), 256 * B[i] + 256
        wait("v", *[kc[i, j] for j in mine_v[i]])
        kn_[i] = add_up(T.cs[:, e - n:e], cm, 512 * i, n, -256.0)

    def places(i, n=1):
        c, lift = min(B[i:i + n]), 256.0 if odd else 272.0
        wait("v", *[kn_[h] for h in range(i, i + n)])
        src = T.cs[:, 256 * c + 255:256 * (c + n):256]
        if mine_s[i]:
            wait("v", kl[i])
            kn_["pu"] = V(v.tensor_scalar(T.pu1[:, c:c + 1], src, T.ls[:, i:i + 1], lift, OP.add, OP.add))
        else:
            kn_["pu"] = V(v.tensor_scalar(T.pu1[:, c:c + n], src, lift, None, OP.add))
        for h in range(i, i + n):
            kn_["p", h] = kn_["pu"]

    def lists(i):
        if i == 0:
            wait("v", k_gr)
            kn_["gt"] = V(v.transpose(T.gt[:, 0:96], T.gr[:, 0:96]))
        elif i == 1:
            wait("v", kn_["gt"])
            V(v.tensor_scalar(T.goff[:, 0:6:2], T.gt[:, 0:96:32], 1.0 / 32, None, OP.mult))
        elif i == 2:
            wait("v", k_bg)
            kn_["w"] = V(v.tensor_scalar(T.win1[:, lo1 - 16:lo1 + 144], T.ur[:, 16:176], T.bg[:, 0:1], None, OP.add))
        else:
            wait("s", k_i3, k_b1)
            kn_["v1"] = S(s.activation(T.vals1[:, 0:64], T.i3[:, 0:64], IDENT, bias=T.pcq[:, 2:3], scale=T.keep[:, 0:1]))

    def alone(i):
        c = B[i]
        wait("s", k_nb, kp[i])
        kn_["v", i] = S(s.activation(T.valo[:, 16 * c:16 * c + 16], T.nb[:, 0:16], IDENT, bias=sp[c], scale=sign1))

    def scatter(i, what):
        c = min(B[i:i + 2])
        wait("v", kn_["p", i], kn_["p", i + 1], *((kn_["v", i], kn_["v", i + 1]) if what else (kn_["v1"], kn_["w"])))
        if "x%d" % what in kn_:
            wait("v", kn_["x%d" % what])
        win, vals = (T.wins, T.valo) if what else (T.win1, T.vals1)
        kn_["x%d" % what] = V(v.tensor_copy(win[:, 0:528].indirect(T.pu1[:, c:c + 2]), vals[:, 16 * c:16 * c + 32]))

    kn_, kd = {}, {}
    c01 = min(B[0:2])
    call = {"v": alone, "x": scatter,"q": quant, "d": down, "r": rows, "s": scores,
            "b": lambda i: bound(i, kd["s", i]), "c": cell, "g": signs, "l": sum_signs, "t": total, "p": places, "z": lists}
    for step in OPT["order"].split():
        call[step[0]](*[int(ch) for ch in step[1:]])
    k_pu = kn_["pu"]

    def invert(n, ready, cols, vals, lo, lift, fill, wide=9):
        W = lambda b: T[b + n]
        if cols:
            wait("v", *ready)
            a = V(v.tensor_copy(W("win")[:, 0:528].indirect(W("pu")[:, 0:cols]), vals[:, 0:16 * cols]))
        else:
            a = ready
        fill(0)
        wait("v", a)
        V(v.transpose(W("tz")[:, 0:128], W("win")[:, lo:lo + 128]))
        a = V(v.transpose(W("tz")[:, 128:288], W("win")[:, lo - 16:lo + 144]))
        fill(1)
        wait("v", a)
        a = V(v.tensor_tensor_scan(W("qa")[0:64, 143:431:8], W("tz")[0:64, 0:288:8], W("tz")[64:128, 0:288:8], 0.0, best, OP.add))
        half = lambda p: W("qa")[p:p + 32, 447 - 32 * wide:431:32]
        fill(3)
        wait("v", a)
        for h in range(4):
            a = V(v.tensor_tensor(W("qc")[32 * h:32 * h + 32, 17 - wide:17], half(0), half(32), best))
        fill(4)
        wait("v", a)
        b = V(v.tensor_scalar(W("lst")[:, 0:16], W("qc")[:, 8:17].indirect(T.goff[:, 0:1]), sign1, None, OP.mult))
        fill(5)
        return a, b

    def pick_codes(dc, sc, off, *ready):
        wait("v", *ready)
        return V(v.tensor_copy(dc.bitcast(dt.uint32), sc.bitcast(dt.uint32).indirect(off)))

    def pick_scales(ds, ss, off, *ready):
        wait("s", *ready)
        return S(s.activation(ds, ss.indirect(off), COPY))

    def remote(o, i, dst, sem, *ready):
        wait("g", *ready)
        rid, pid = topo.addr(dst, core)
        n = len(topo.engines(core, dst))
        codes = sem in ("h1c", "h2c", "h1d", "h2d")
        g.remote_dma(o.bitcast(dt.uint8) if codes else o, i.bitcast(dt.uint8) if codes else i, T.sem[sem], T.sem["sent"], pid, rid,
                     topo.mask(core, dst))
        count["sent"] = count.get("sent", 0) + n
        return (sem, n)

    def w_codes(o):
        wait("v", dw)
        return V(v.quantize_mx(T.wq[:, 128 * o:128 * o + 128], T.ws[:, 128 * o:128 * o + 128], T.wb[:, 512 * o:512 * o + 512]))

    m0 = SLOT * rank
    more = 2 * K if P < Q else 0
    mate = T.cores[rank ^ 1]
    k_i5 = iota(T.i5[:, 0:16], [[1, 8], [0, 2]], 2 * SLOT * Q, 0, False)
    in_raw = [remote(T.spm[:, B[0]:B[0] + 1], T.sp[:, B[0]:B[0] + 1], mate, "hr", kp[0]),
              remote(T.spm[:, odd:odd + 3], T.sp[:, odd:odd + 3], mate, "hq", kp[3])]
    k_iy = iota(T.iy[:, 0:256], [[1, 256]], 0, 0)
    in_places = remote(T.pum[:, 0:4], T.pu1[:, 0:4], mate, "hp", k_pu)
    wait("s", *kc.values())
    for c in B:
        k_raw = S(s.activation(T.raw[:, 128 * c:128 * c + 128], row[c], COPY))
    wait("s", k_i4)
    for i, (base, step) in enumerate(((113.0, 1.0), (113.0, 1.0), (112.0, -16.0)) if odd else ((128.0, -1.0), (-129.0, 1.0), (0.0, 16.0))):
        k_kq = S(s.activation(T.kq[:, i:i + 1], T.pcf[:, 1:2], IDENT, bias=base, scale=step))
    S(s.activation(T.pt[:, 3:4], T.pcf[:, 1:2], IDENT, bias=T.pcf[:, 0:1]))
    S(s.activation(T.pcq[:, 0:1], T.pcq[:, 1:2], IDENT, bias=T.bg[:, 0:1], scale=T.keep[:, 0:1]))
    S(s.activation(T.win2[:, 0:160], T.thr[:, 0:160], IDENT, bias=T.bg[:, 0:1], scale=0.0))
    if not OPT["valm"]:
        wait("s", *in_raw)
        for c in range(4):
            S(s.activation(T.valm[:, 16 * c:16 * c + 16], T.nb[:, 0:16], IDENT, bias=T.spm[:, c:c + 1]))

    lane = []

    def sorted_scores(i):
        apart = OPT["apart"]
        if i == apart:
            wait("v", kn_["x1"])
            lane.append(V(v.transpose(T.tzs[:, 0:128], T.wins[:, lo1:lo1 + K])))
        elif i == 1 + 2 * apart:
            wait("v", lane[0])
            lane.append(V(v.tensor_tensor_scan(T.qa1[0:64, 0:128], T.tzs[0:64, 0:128], T.tzs[64:128, 0:128], -BIG * sign1, best, best)))
        elif i == 5 and not apart:
            wait("v", k_iy, k_kq)
            V(v.tensor_scalar(T.jump[:, 0:256], T.iy[:, 0:256], T.kq[:, 0:1], float(K), OP.is_equal, OP.mult))
        elif apart and i > 3:
            wait("v", lane[1])
            for h in OPT["folds"][i - 4]:
                lane.append(V(v.tensor_tensor(T.qc1[32 * h:32 * h + 32, 4:8], T.qa1[0:32, 31:128:32], T.qa1[32:64, 31:128:32], best)))

    k_q1, k_l1 = invert("1", kn_["x0"], 0, T.vals1, lo1, 256.0, sorted_scores, 9 if OPT["apart"] else 13)
    if OPT["apart"]:
        k_q1 = lane[-1]

    def to_many(src, dsts, sem, *ready):
        wait("g", *ready)
        ids, m = [], topo.mask(core, mate)
        for x in dsts:
            rid, pid = topo.addr(T.cores[rank ^ x], core)
            ids.append(DstId(rid=rid, pnc=pid))
            m &= topo.mask(core, T.cores[rank ^ x])
        n = bin(m).count("1")
        g.remote_dma_fused([RemoteDMATransfer(dst_ids=ids, dma_engine_mask=m, remote_sem=T.sem[sem], srcs=[src],
                                              dsts=list(dsts.values()))], local_sem=T.sem["sent"])
        count["sent"] += n
        return (sem, len(dsts) * n)
    slot = T.msg[:, m0:m0 + SLOT]
    two = OPT["two"]
    if not OPT.get("late_msg"):
        in_msg = to_many(T.qc1[:, 4:8], {x: slot for x in (2, 3)}, "hm", k_q1)

    def at_t():
        wait("s", k_q1)
        k = S(s.activation(T.at[:, 0:16], T.qc1[:, 8:17].indirect(T.goff[:, 0:1]), COPY, scale=sign1))
        if two == "early":
            wait("s", k)
        return S(s.activation(T.at[:, 1:17] if two == "early" else T.at[:, 24:40], T.qc1[:, 0:8].indirect(T.goff[:, 4:5]), COPY))
    if two == "early":
        k_at = at_t()
    if two == "early":
        in_ids = remote(T.at[:, 20:22], T.at[:, 0:2], mate, "hi", k_at)

    off = T.lst1[:, 2:10]
    mine = T.osr[:, lom:lom + K]
    a1 = pick_codes(T.c1[:, 0:K], T.xq[:, 0:512], off, k_l1)
    wait("s", k_l1, k_raw)
    k_os = S(s.activation(mine, T.raw[:, 0:512].indirect(off), COPY))
    b1 = pick_scales(T.s1[:, 0:K], T.xs[:, 0:512], off)
    if two != "early":
        k_at = at_t()
    wait("s", k_os)
    S(s.activation(T.sq[:, 129:130], T.pcf[:, 0:1], IDENT, bias=-16.0 - more, scale=0.0))
    S(s.activation(T.sq[:, 128:129], T.pt[:, 3:4], COPY, scale=-1.0))
    for i, (base, step) in enumerate(((16.0, 1.0), (143.0, -1.0), (143.0 + more, -1.0))):
        k_pt = k_sq0 = S(s.activation(T.pt[:, i:i + 1], T.pt[:, 3:4], IDENT, bias=base, scale=step))

    extra = []
    if OPT.get("halves"):
        in1a = remote(T.c1[:, K:K + 64], T.c1[:, 0:64], mate, "h1d", a1)
        in1c = remote(T.c1[:, K + 64:2 * K], T.c1[:, 64:K], mate, "h1c", a1)
        extra.append(in1a)
    else:
        in1c = remote(T.c1[:, K:2 * K], T.c1[:, 0:K], mate, "h1c", a1)
    if OPT.get("late_msg"):
        in_msg = to_many(T.qc1[:, 4:8], {x: slot for x in (2, 3)}, "hm", k_q1)
    if two == "mid":
        in_ids = remote(T.at[:, 16:18], T.at[:, 0:2], mate, "hi", k_at)
    in1s = remote(T.s1[:, K:2 * K], T.s1[:, 0:K], mate, "h1s", b1)
    if two == "late":
        in_ids = remote(T.at[:, 16:18], T.at[:, 0:2], mate, "hi", k_at)
    if two == "v4" and OPT.get("pair"):
        in_ids = remote(T.at[:, 20:21], T.at[:, 0:1], mate, "hi", k_at)
    elif two == "v4":
        in_ids = to_many(T.at[:, 0:1], {x: T.at[:, 16 + x:17 + x] for x in (1, 2, 3)}, "hi", k_at)
    if not two:
        in_ids = to_many(T.lst1[:, 0:1], {x: T.cu[:, x:x + 1] for x in (1, 2, 3)}, "hi")

    if OPT["valm"]:
        wait("v", lane[2], *in_raw)
        a = V(v.tensor_tensor(T.valm[:, 0:64], T.spm[:, 0:4].indirect(T.eoff[:, 16:20]), T.nb[:, 0:64], OP.add))
    k_w = [w_codes(0)]
    wait("v", k_i5)
    k_eo = V(v.tensor_copy(T.eoff[:, 0:16], T.i5[:, 0:16]))
    wait("v", in_places, k_os, *([a] if OPT["valm"] else []))
    a = V(v.tensor_tensor(T.cb[:, 0:64], T.osr[:, 0:528].indirect(T.pum[:, 0:4]), T.valm[:, 0:64], OP.is_le if odd else OP.is_lt))
    k_w.append(w_codes(1))
    wait("v", a)
    a = V(v.tensor_tensor_scan(T.cr[0:64, 0:96], T.cb[0:64, 0:96], T.cb[64:128, 0:96], 0.0, OP.add, OP.add))
    wait("v", a)
    a = V(v.transpose(T.ct[0:64, 0:32], T.cr[0:64, 64:96]))
    V(v.tensor_tensor_scan(T.tab[:, 0:256], T.one[:, 0:256], T.jump[:, 0:256], T.kq[:, 1:2], OP.add, OP.add))
    wait("v", a)
    for h in range(4):
        a = V(v.tensor_tensor_scan(T.cn[32 * h:32 * h + 32, 0:32], T.ct[0:32, 0:32], T.ct[32:64, 0:32], 0.0, OP.add, OP.add))
    n_wins = T.cn[:, 31:32]
    def products(side, bank, *ready):
        wait("t", *k_w, *ready)
        return [X(t.matmul_mx(bank[:, 512 * (o + 2):512 * (o + 2) + 128], T.wq[:, 128 * o:128 * o + 128], T.ws[:, 128 * o:128 * o + 128],
                              T.c2[:, side], T.s2[:, side], True, True)) for o in range(2)]

    fs = lambda h, n=1: T.fs[:, 128 * h:128 * (h + n)]
    yx = lambda h: T.yx[:, 128 * h:128 * h + 128]
    at = lambda r: T.yx[:, 384 + r:385 + r]
    ba = lambda i, n=1: T.ba[:, 128 * i:128 * (i + n)]
    last = lambda i: T.bu[:, 64 * i + 63:64 * i + 64]
    col = lambda r: T.cf[:, (rank ^ r):(rank ^ r) + 1] if r != rank else T.at[:, 0:1]
    ps, sel = [[T[b][:, j:j + 1] for j in range(2)] for b in ("ps", "sel")]
    me, him, E, O = at(rank), at(rank ^ 1), at(2 * Q), at(2 * Q + 1)
    if two:
        me, him, E, O = T.at[:, 1:2] if two == "early" else T.at[:, 24:25], T.at[:, 21:22], at(0), at(1)
    yw = (T.yw0, T.yw1)
    spread = lambda h: s.activation(yx(h), T.msg[:, 0:16].indirect(T.eoff[:, 8 * h:8 * h + 8]), COPY)
    sign = lambda o, src, c: s.activation(T.sq[:, o:o + 128], src, ACT.Sign, bias=c, scale=-1.0)
    summed = lambda i, o, n, first: v.tensor_tensor_scan(T.bu[:, 64 * i:64 * i + n], T.ba[:, o:o + n], T.ba[:, o + n:o + 2 * n], first,
                                                         OP.add, OP.add)
    tok = {"n": a, "msg": in_msg, "eoff": k_eo, "a1": a1, "b1": b1, "in1c": in1c, "in1s": in1s, "ids": in_ids, "pt": k_pt, "sq0": k_sq0}
    steps = {
        "x": ("s", "msg eoff b1", lambda: s.activation(T.yx[:, 384:400], T.msg[:, 0:16].indirect(T.goff[:, 2:3]), COPY)),
        "eE": ("s", "msg eoff", lambda: spread(0)), "eO": ("s", "msg eoff", lambda: spread(1)), "eM": ("s", "msg eoff", lambda: spread(2)),
        "wE": ("v", "msg eoff", lambda: v.tensor_copy(yx(0), T.msg[:, 0:16].indirect(T.eoff[:, 0:8]))),
        "wO": ("v", "msg eoff", lambda: v.tensor_copy(yx(1), T.msg[:, 0:16].indirect(T.eoff[:, 8:16]))),
        "wM": ("v", "msg eoff", lambda: v.tensor_copy(yx(2), T.msg[:, 0:16].indirect(T.eoff[:, 16:24]))),
        "V2": ("s", "", lambda: s.activation(T.vals2[:, 0:32], T.i4[:, 0:32], IDENT, bias=T.pcq[:, 0:1], scale=T.keep[:, 0:1])),
        "tE": ("v", "eE", lambda: v.transpose(fs(0), yx(0))), "tO": ("v", "eO", lambda: v.transpose(fs(1), yx(1))),
        "tM": ("v", "eM", lambda: v.transpose(fs(2), yx(2))),
        "ps": ("v", "x", lambda: v.tensor_tensor(T.ps[:, 0:2], T.yx[:, 384:388:2], T.yx[:, 385:388:2], OP.max)),
        "se": ("v", "x", lambda: v.tensor_tensor(T.sel[:, 0:2], T.yx[:, 385:388:2], T.yx[:, 384:388:2], OP.is_gt)),
        "n5": ("v", "n", lambda: v.tensor_scalar(T.yl[:, 0:1], T.kq[:, 2:3], n_wins, 255.0, OP.add, OP.min)),
        "n6": ("v", "n5", lambda: v.tensor_scalar(T.off2[:, 0:16], T.tab[:, 0:256].indirect(T.yl[:, 0:1]), n_wins, 0.0 if odd else float(K),
                                                  OP.add if odd else OP.subtract, OP.add)),
        "a": ("v", "tE x", lambda: v.tensor_scalar(ba(0), fs(0), O, None, OP.is_ge)),
        "b": ("v", "x", lambda: v.tensor_scalar(ba(1), mine, him, None, OP.is_gt if odd else OP.is_ge)),
        "c": ("v", "tE tO ps", lambda: v.tensor_scalar(ba(2, 2), fs(0, 2), ps[P], None, OP.is_ge if Q < P else OP.is_gt)),
        "d": ("v", "tM x", lambda: v.tensor_scalar(ba(4), fs(2), me, None, OP.is_ge if odd else OP.is_gt)),
        "mH": ("t", "in1c in1s a1 b1", lambda: t.matmul_mx(T.psf[:, 0:128], T.uq[:, 0:128], T.us[:, 0:128], T.c1[:, K:2 * K], T.s1[:, K:2 * K], True, True)),
        "mI": ("t", "in1c in1s a1 b1", lambda: t.matmul_mx(T.psp[:, 0:128], T.uq[:, 0:128], T.us[:, 0:128], T.c1[:, K:2 * K], T.s1[:, K:2 * K], True, True)),
        "d'": ("v", "mH x", lambda: v.tensor_scalar(ba(4), T.psf[:, 0:128], me, None, OP.is_ge if odd else OP.is_gt)),
        "g2'": ("s", "mI ps", lambda: sign(272, T.psp[:, 0:128], ps[Q])),
        "A": ("v", "a pt", lambda: summed(0, 0, 64, T.pt[:, 2:3])),
        "B": ("v", "b pt", lambda: v.tensor_tensor_scan(T.bt[:, 0:64], T.ba[:, 128:192], T.ba[:, 192:256], T.pt[:, 1 - odd:2 - odd], OP.add, OP.add)),
        "C": ("v", "c", lambda: v.tensor_tensor_scan(T.bt[:, 64:192], T.ba[:, 256:384], T.ba[:, 384:512], 0.0, OP.add, OP.add)),
        "D": ("v", "d pt", lambda: summed(4, 512, 64, T.pt[:, odd:odd + 1])),
        "g1": ("s", "ps", lambda: sign(144, mine, ps[Q])), "g2": ("s", "ps tM", lambda: sign(272, fs(2), ps[Q])),
        "gA": ("s", "x tO", lambda: sign(0, fs(1), E)),
        "rA": ("s", "gA sq0", lambda: s.activation(T.junk[:, 0:130], T.sq[:, 0:130], ACT.Relu, scale=-1.0, accum_out=T.lq[:, 1:2])),
        "rC": ("s", "g1 g2", lambda: s.activation(T.junk[:, 144:400], T.sq[:, 144:400], ACT.Relu, scale=1.0 if P < Q else -1.0,
                                                  accum_out=T.lq[:, 0:1])),
        "uP": ("v", "B C D", lambda: v.tensor_scalar(T.pu2[:, P:P + 1], last(4), T.bt[:, 63:64], T.bt[:, 191:192], OP.min, OP.add)),
        "uQ": ("v", "A rA rC", lambda: v.tensor_scalar(T.pu2[:, Q:Q + 1], last(0), T.lq[:, 1:2], T.lq[:, 0:1], OP.min,
                                                       OP.subtract if P < Q else OP.add)),
        "cf": ("v", "ids", lambda: v.tensor_copy(T.cf[:, 1:4], T.cu[:, 1:4])),
    }
    for j in range(2):
        steps["y%d" % j] = ("s", "m%d" % j, lambda o=j: s.activation(yw[o][:, P:256:2], T.psf[:, 512 * (o + 2):512 * (o + 2) + 128], COPY))
        steps["v%d" % j] = ("s", "cf", lambda j=j: s.activation(T.vd[:, j:j + 1], col(2 * j), IDENT, bias=col(2 * j + 1), scale=-1.0))
        steps["r%d" % j] = ("s", "se", lambda j=j: s.activation(T.cp[:, 32 * j:32 * j + 1], sel[j], IDENT, bias=2.0 * j))
        steps["k%d" % j] = ("s", "se v%d" % j, lambda j=j: s.activation(T.cp[:, 32 * j + 1:32 * j + 2], T.vd[:, j:j + 1], IDENT,
                                                                      bias=col(2 * j), scale=sel[j]))
    if two:
        mark = T.cp[:, 32 * P:32 * P + 2]
        steps.update({
            "pQ": ("v", "x", lambda: v.tensor_tensor(ps[Q], E, O, OP.max)),
            "ps": ("v", "ids b1", lambda: v.tensor_tensor(ps[P], me, him, OP.max)),
            "se": ("v", "ids b1", lambda: v.tensor_tensor(sel[0], him, me, OP.is_ge if odd else OP.is_gt)),
            "v0": ("s", "ids", lambda: s.activation(T.vd[:, 0:1], T.at[:, 0:1], IDENT, bias=T.at[:, 20:21], scale=-1.0)),
            "r0": ("s", "se", lambda: s.activation(T.cp[:, 32 * P:32 * P + 1], sel[0], IDENT, bias=float(rank), scale=-1.0 if odd else 1.0)),
            "k0": ("s", "se v0", lambda: s.activation(T.cp[:, 32 * P + 1:32 * P + 2], T.vd[:, 0:1], IDENT, bias=T.at[:, 0:1], scale=sel[0])),
            "b": ("v", "ids b1", steps["b"][2]), "g1": ("s", "pQ", steps["g1"][2]), "g2'": ("s", "mI pQ", steps["g2'"][2]),
        })
    if two == "v4":
        him = T.psp[:, 0:1]
        col = lambda r: T.at[:, 16 + (rank ^ r):17 + (rank ^ r)] if r != rank else T.at[:, 0:1]
        steps.update({
            "mD": ("t", "in1c in1s a1 b1", lambda: t.matmul_mx(T.psp[:, 0:128], T.c1[:, K:2 * K], T.s1[:, K:2 * K], T.uq0[:, 2:130], T.us0[:, 2:130], True, True)),
            "ps": ("v", "mD", steps["ps"][2]), "b": ("v", "mD", steps["b"][2]),
            "sQ": ("v", "x", lambda: v.tensor_tensor(sel[Q], O, E, OP.is_gt)),
            "se": ("v", "mD", lambda: v.tensor_tensor(sel[P], me, him, OP.is_gt if odd else OP.is_lt)),
            "E1": ("v", "mH pQ", lambda: v.tensor_scalar(ba(5), T.psf[:, 0:128], ps[Q], None, OP.is_ge if P < Q else OP.is_gt)),
            "E2": ("v", "E1", lambda: summed(5, 640, 64, -128.0 if P < Q else 0.0)),
            "rC": ("s", "g1", lambda: s.activation(T.junk[:, 144:272], T.sq[:, 144:272], ACT.Relu, scale=1.0 if P < Q else -1.0, accum_out=T.lq[:, 0:1])),
            "f": ("v", "A rA rC", lambda: v.tensor_scalar(T.bu[:, 384:385], last(0), T.lq[:, 1:2], T.lq[:, 0:1], OP.min, OP.subtract if P < Q else OP.add)),
            "uQ": ("v", "f E2", lambda: v.tensor_scalar(T.pu2[:, Q:Q + 1], last(5), T.bu[:, 384:385], None, OP.add)),
        })
        if OPT.get("mi"):
            steps["mI"] = ("t", "in1c in1s a1 b1", lambda: t.matmul_mx(T.psp[:, 512:640], T.uq[:, 0:128], T.us[:, 0:128], T.c1[:, K:2 * K], T.s1[:, K:2 * K], True, True))
            steps["g2'"] = ("s", "mI pQ", lambda: sign(272, T.psp[:, 512:640], ps[Q]))
            steps["rC"] = ("s", "g1 g2", lambda: s.activation(T.junk[:, 144:400], T.sq[:, 144:400], ACT.Relu, scale=1.0 if P < Q else -1.0, accum_out=T.lq[:, 0:1]))
            steps["uQ"] = ("v", "A rA rC", lambda: v.tensor_scalar(T.pu2[:, Q:Q + 1], last(0), T.lq[:, 1:2], T.lq[:, 0:1], OP.min, OP.subtract if P < Q else OP.add))
        if OPT.get("rsplit"):
            way, less = (1.0, OP.subtract) if P < Q else (-1.0, OP.add)
            steps["rB"] = ("s", "g1", lambda: s.activation(T.junk[:, 144:272], T.sq[:, 144:272], ACT.Relu, scale=way, accum_out=T.lq[:, 0:1]))
            steps["rC"] = ("s", "g2", lambda: s.activation(T.junk[:, 272:400], T.sq[:, 272:400], ACT.Relu, scale=way, accum_out=T.lq[:, 2:3]))
            steps["f"] = ("v", "A rA rB", lambda: v.tensor_scalar(T.bu[:, 384:385], last(0), T.lq[:, 1:2], T.lq[:, 0:1], OP.min, less))
            steps["uQ"] = ("v", "f rC", lambda: v.tensor_scalar(T.pu2[:, Q:Q + 1], T.bu[:, 384:385], T.lq[:, 2:3], None, less))
        for j in range(2):
            steps["v%d" % j] = ("s", "ids", lambda j=j: s.activation(T.vd[:, j:j + 1], col(2 * j), IDENT, bias=col(2 * j + 1), scale=-1.0))
            steps["r%d" % j] = ("s", "se", lambda j=j: s.activation(T.cp[:, 32 * j:32 * j + 1], sel[j], IDENT, bias=2.0 * j))
            steps["k%d" % j] = ("s", "se v%d" % j, lambda j=j: s.activation(T.cp[:, 32 * j + 1:32 * j + 2], T.vd[:, j:j + 1], IDENT, bias=col(2 * j), scale=sel[j]))
        in_cp = in_ids
        if OPT.get("pair"):
            steps.update({
                "se": ("v", "mD", lambda: v.tensor_tensor(sel[0], me, him, OP.is_le if odd else OP.is_lt)),
                "v0": ("s", "ids", lambda: s.activation(T.vd[:, 0:1], T.at[:, 0:1], IDENT, bias=T.at[:, 20:21], scale=-1.0)),
                "r0": ("s", "se", lambda: s.activation(T.cp[:, 32 * P:32 * P + 1], sel[0], IDENT, bias=float(rank), scale=-1.0 if odd else 1.0)),
                "k0": ("s", "se v0", lambda: s.activation(T.cp[:, 32 * P + 1:32 * P + 2], T.vd[:, 0:1], IDENT, bias=T.at[:, 0:1], scale=sel[0])),
            })
    for name in OPT["second"].split():
        if name == "sc":
            in_cp = remote(mark, mark, T.cores[rank ^ 2], "hj", tok["r0"], tok["k0"])
        elif name == "pc" and OPT.get("halves"):
            for h, (ar, sem) in enumerate(((in1a, "h2d"), (in1c, "h2c"))):
                e = slice(K * P + 64 * h, K * P + 64 * h + 64)
                tok[name] = pick_codes(T.c2[:, e], T.c1[:, 0:256], T.off2[:, 4 * h:4 * h + 4], tok["n6"], ar)
                in2c = remote(T.c2[:, e], T.c2[:, e], T.cores[rank ^ 2], sem, tok[name])
                extra.append(in2c)
        elif name == "pc":
            tok[name] = pick_codes(T.c2[:, own], T.c1[:, 0:256], T.off2[:, 0:8], tok["n6"], in1c)
            in2c = remote(T.c2[:, own], T.c2[:, own], T.cores[rank ^ 2], "h2c", tok[name])
        elif name == "pz":
            tok[name] = pick_scales(T.s2[:, own], T.s1[:, 0:256], T.off2[:, 0:8], tok["n6"], in1s)
            in2s = remote(T.s2[:, own], T.s2[:, own], T.cores[rank ^ 2], "h2s", tok[name])
            tok["m0"], tok["m1"] = products(own, T.psf, tok["pc"], tok["pz"])
            kn = products(arr, T.psp, in2c, in2s)
        else:
            q, ready, make = steps[name]
            wait(q, *[tok[r] for r in ready.split()])
            tok[name.replace("w", "e").replace("'", "")] = done(make(), q)
    kv, kcp = max(tok["uP"], tok["uQ"]), max(tok[r] for r in ("k0", "k1", "r0", "r1") if r in tok)
    kz = []

    def numbers(i):
        for h in OPT["numbers"].get(i, ()):
            if h == 9:
                wait("v", kn[0])
                tok["a0"] = V(v.tensor_copy(T.yw0[:, Q:256:2], T.psp[:, 1024:1152]))
            elif h == 0:
                wait("v", kcp, *([in_cp] if two else []))
                for j in range(2):
                    kz.append(V(v.transpose(T.idr[:, j:64:2], T.cp[:, 32 * j:32 * j + 32])))
            else:
                wait("v", kz[1])
                kz.append(V(v.tensor_copy(T.idr[0:2, 64 * h:64 * h + 64], T.idr[32 * h:32 * h + 2, 0:64])))
    k_q2, k_l2 = invert("2", (kv,), 2, T.vals2, 16, 0.0, numbers)
    off = T.lst2[:, 2:10]
    if OPT["tail"] == 3:
        kyw, ky = [], []
        for o in range(2):
            wait("v", kn[o])
            kyw.append(V(v.tensor_copy(yw[o][:, Q:256:2], T.psp[:, 512 * (o + 2):512 * (o + 2) + 128])))
        for o in range(2):
            wait("s", k_l2, kyw[o], tok["y%d" % o])
            a = S(s.activation(T.yb[:, K * o:K * o + 64], yw[o][:, 0:256].indirect(T.lst2[:, 2:6]), COPY))
            wait("v", k_l2, kyw[o], tok["y%d" % o])
            ky.append((a, V(v.tensor_copy(T.yb[:, K * o + 64:K * o + K], yw[o][:, 0:256].indirect(T.lst2[:, 6:10])))))
        wait("v", *kz)
        ki = V(v.tensor_copy(T.idb[:, 0:128], T.idr[:, 0:256].indirect(off)))
        ky0, ky1 = ky
    elif OPT["tail"] == 0:
        kyw = []
        for o in range(2):
            wait("s", kn[o])
            kyw.append(S(s.activation(yw[o][:, Q:256:2], T.psp[:, 512 * (o + 2):512 * (o + 2) + 128], COPY)))
        if OPT.get("pair"):
            wait("s", kz[1])
            kz.append(S(s.activation(T.idr[0:2, 192:256], T.idr[96:98, 0:64], COPY)))
        wait("v", k_l2, kyw[0])
        ky0 = V(v.tensor_copy(T.yb[:, 0:128], T.yw0[:, 0:256].indirect(off)))
        wait("v", *kz)
        ki = V(v.tensor_copy(T.idb[:, 0:128], T.idr[:, 0:256].indirect(off)))
        wait("s", k_l2, kyw[1])
        ky1 = S(s.activation(T.yb[:, 128:256], T.yw1[:, 0:256].indirect(off), COPY))
    else:
        if OPT["tail"] == 1:
            wait("s", kn[0])
            a = S(s.activation(T.yw0[:, Q:256:2], T.psp[:, 1024:1152], COPY))
        else:
            a = tok["a0"]
        wait("v", kn[1])
        b = V(v.tensor_copy(T.yw1[:, Q:256:2], T.psp[:, 1536:1664]))
        wait("s", k_l2, a)
        ky0 = S(s.activation(T.yb[:, 0:128], T.yw0[:, 0:256].indirect(off), COPY))
        wait("v", k_l2, b, tok["y1"])
        ky1 = V(v.tensor_copy(T.yb[:, 128:256], T.yw1[:, 0:256].indirect(off)))
        wait("s", *kz)
        ki = S(s.activation(T.idb[:, 0:128], T.idr[:, 0:256].indirect(off), COPY))
    if OPT["split"]:
        for o, k in enumerate((ky0, ky1)):
            wait("y", *(k if OPT["tail"] == 3 else (k,)))
            d0 = done(y.dma_start(T.y[:, K * o:K * o + K], T.yb[:, K * o:K * o + K]), "dy", 16)
    else:
        wait("y", ky0, ky1)
        d0 = done(y.dma_start(T.y[:, 0:256], T.yb[:, 0:256]), "dy", 16)
    wait("s", ki)
    d2 = done(s.dma_start(T["id"][0:2, 0:128], T.idb[0:2, 0:128]), "did", 16)
    wait("g", ("sent", count["sent"]), in1c, in1s, in2c, in2s, *extra, in_msg, *in_raw, in_places, in_ids, *([in_cp] if two else []), du, *dx.values(), dw,
         ("gc", count["gc"]), ("v", count["v"]), ("s", count["s"]), ("t", count["t"]), d0, d2)
